import numpy as np, ml_dtypes
CORES = [6,15,38,47]
N = 4
import mx_ref
BF = ml_dtypes.bfloat16
def gentries(a):
    return np.ascontiguousarray(a.reshape(8, 16, -1).transpose(0, 2, 1)).reshape(8, -1)
def gtable(e):
    e = np.asarray(e); return np.ascontiguousarray(e.reshape(8, -1, 16).transpose(0, 2, 1)).reshape(128, -1).astype(np.int32)
def gcols(t, e):
    v = np.concatenate([t.reshape(8, 16, -1, 4), np.zeros((8, 16, 1, 4), BF)], axis=2)
    return np.ascontiguousarray(np.stack([v[g][:, e[g]] for g in range(8)])).reshape(128, -1)
def tile(rs):
    return np.stack(rs, axis=2).reshape(128, -1).astype(BF)
def pick(q, e):
    c = np.concatenate([q[0].reshape(128, -1, 4), np.zeros((128, 1, 4), np.uint8)], axis=1); s = np.concatenate([q[1], np.ones((16, 1), np.uint8)], axis=1)
    return (np.ascontiguousarray(c[:, e].reshape(128, -1)), np.ascontiguousarray(s[:, e]))
def join(*qs):
    return (np.concatenate([q[0] for q in qs], axis=1), np.concatenate([q[1] for q in qs], axis=1))
def put(q, e, v):
    c, s = q[0].reshape(128, -1, 4).copy(), q[1].copy(); c[:, e] = v[0].reshape(128, -1, 4); s[:, e] = v[1]
    return (c.reshape(128, -1), s)
def pk(c, s):
    return (np.ascontiguousarray(c), mx_ref.live(s))
def emit(q):
    return q[0], q[1]
def packed(v, rng):
    q = [mx_ref.quantize(np.ascontiguousarray(v[r])) for r in range(N)]
    return np.stack([a for a, b in q]), np.stack([mx_ref.plane(b, rng) for a, b in q])
def values_of_codes():
    e, c = np.zeros((128, 128, 4), np.float32), np.zeros((128, 2, 4), np.uint8)
    e[np.arange(128), np.arange(128), 0] = 1
    c[:127, :, 0] = np.arange(256).reshape(2, 128).T[:127]
    return mx_ref.matmul(mx_ref.quantize(e.reshape(128, 512).astype(BF)), (c.reshape(128, 8), np.full((16, 2), 127, np.uint8))).T.reshape(-1).astype(np.float64)
CODE_VALUE, SCALE_VALUE = values_of_codes(), 2.0 ** (np.arange(256) - 127.0)
def decode(q):
    return (CODE_VALUE[q[0]].reshape(16, 8, -1, 4) * SCALE_VALUE[q[1]][:, None, :, None] + 0.0).reshape(128, -1).astype(np.float32)
def f(rng, *shape):
    return mx_ref.flush((rng.standard_normal(shape, dtype=np.float32) * np.exp2(rng.integers(-2, 3, shape[:-1] + (1,)))).astype(BF))
def wide(rng, *shape, cols=0):
    v = rng.standard_normal(shape, dtype=np.float32) * np.exp2(rng.integers(-12, 13, shape)).astype(np.float32)
    if cols: v *= np.repeat(np.exp2(rng.integers(-cols, cols + 1, shape[:-2] + (1, shape[-1] // 4))) * (rng.random(shape[:-2] + (1, shape[-1] // 4)) > 0.0625), 4, axis=-1).astype(np.float32)
    return mx_ref.flush(v.astype(BF))
C, R = 320, 3
STEP = [2, 1, 3]
def big(v):
    v = v.astype(np.float32)
    v[np.abs(v) < np.float32(2.0 ** -16)] = 0
    return v.astype(BF)
def numbers_of(rng):
    return {"x": big(f(rng, N, 128, 4 * C)), "u": np.array(f(rng, N, 128, 512)), "v": np.array(f(rng, N, 128, 512))}
def layers(rng):
    return big(f(rng, N, 128, 2048)).reshape(N, 8, 16, 4, 8, 16, 4)
def weights(rng, w):
    c, p = packed(np.ascontiguousarray(w).reshape(N, 128, 2048), rng)
    return {"wc": c, "ws": p}
def stored(e):
    return {"vg": np.stack([gtable(e[r]) for r in range(N)])}
def pointers(rng):
    return stored(rng.integers(0, 2 * C, (N, 8, C)))
def setup_inputs(rng):
    return {**numbers_of(rng), **weights(rng, layers(rng)), **pointers(rng)}
def setup_inputs_ties(rng):
    d = numbers_of(rng)
    e = rng.permutation(N)
    lo, hi = sorted((int(e[0]), int(e[0]) ^ STEP[0]))
    u = d["u"].reshape(N, 128, 128, 4)
    for r in range(N):
        k = np.zeros(8, int) if r in (lo, hi) else rng.permutation(8) % 3
        a = u[r][:, 1:4].copy()
        a[:, 2] = 0
        u[r][:, ::16] = a[:, k]
    d["x"][e[1]] = 0
    p = rng.integers(0, 2 * C, (N, 8, C))
    p[lo, 7] = np.arange(C)
    p[hi, 7] = rng.permutation(C)
    return {"x": d["x"], "u": u.reshape(N, 128, 512), "v": d["v"], **weights(rng, layers(rng)), **stored(p)}
def setup_inputs_near(rng):
    d = numbers_of(rng)
    x = d["x"].astype(np.float32).reshape(N, 8, 16, C, 4)
    s = rng.integers(0, 4, (2, N, 8, C))
    x[:, :, 0] = 0
    x[:, :, 0, :, 0] = 1
    x[:, :, 8:10] = 0
    for i, k in ((0, 2.0 ** -22), (1, 2.0 ** -29)):
        x[:, :, 8 + i, :, 0] = (s[i] & 1) * k
        x[:, :, 8 + i, :, 1] = (s[i] >> 1) * (2 * k)
    x[:, :, 10:] = rng.integers(4, 8, (N, 8, 6, C, 4)) * 2.0 ** -25
    n = rng.integers(0, 4, (N, 8, C))
    x[:, :, 10, :, 0] = (8 + 2 * n) * 2.0 ** -33
    x[:, :, 11, :, 0] = (14 - 2 * n) * 2.0 ** -33
    u = d["u"].reshape(N, 128, 128, 4)
    u[:, :, ::16] = 0
    o = rng.permutation(N) % 4
    for r in range(N):
        k = (1.0, -1.0, 2.0 ** -30, 2.0 ** -30)[o[r]]
        for h in range(0, 128, 16):
            if o[r] < 3:
                u[r, h, h, 0] = k
                u[r, h + 8, h, :2] = abs(k)
            else:
                u[r, h + 9, h, :2] = k
                u[r, h + 10, h, 0] = 9 * 2.0 ** -33
                u[r, h + 11, h, 0] = 8 * 2.0 ** -33
        if o[r] == 3:
            h = 16 * int(rng.integers(8))
            u[r, h, h, 0] = 1.0
    w = layers(rng)
    for i in (0, 8, 9, 10, 11, 12, 13, 14, 15):
        w[:, :, i] = 0
        w[:, :, :, :, :, i] = 0
    return {"x": x.reshape(N, 128, 4 * C).astype(BF), "u": u.reshape(N, 128, 512), "v": d["v"], **weights(rng, w), **pointers(rng)}
def setup_inputs_huge(rng):
    d = numbers_of(rng)
    x = -2.0 ** 30 * (0.55 + 0.2 * rng.random((N, 8, 1, C, 1)) + 0.05 * rng.random((N, 8, 16, C, 4)))
    u = d["u"].reshape(N, 128, 128, 4)
    o = rng.permutation(N) % 4
    s = np.stack([np.full(8, 1.0 - 2.0 * o[r]) if o[r] < 2 else rng.permutation(8) % 2 * 2.0 - 1.0 for r in range(N)])
    own = np.where(np.arange(128)[:, None] // 16 == np.arange(8), 1.0, 0.75)
    a = 2.0 ** 30 * (1 - 0.1 * rng.random((N, 128, 8, 4))) * own[None, :, :, None] * s[:, None, :, None]
    u[:, :, ::16] = a.astype(np.float32).astype(BF)
    w = np.zeros((N, 128, 4, 128, 4), np.float32)
    i = np.arange(128)
    for b in range(4): w[:, i, b, i, b] = -1
    return {"x": x.astype(np.float32).reshape(N, 128, 4 * C).astype(BF), "u": u.reshape(N, 128, 512), "v": d["v"], **weights(rng, w.astype(BF)), **pointers(rng)}
def setup_inputs_asks(rng):
    d = numbers_of(rng)
    e = np.zeros((N, 8, C), int)
    first = [r for r in range(N) if r < (r ^ STEP[0])]
    for i, r in enumerate(rng.permutation(first)):
        m, o = np.arange(2 * C), rng.permutation(2 * C)
        if i == 0:
            k = C + rng.permutation(C)
            m[:C] = k
            m[k] = np.arange(C)
        if i == 1:
            m[o[C // 2:C]] = o[0]
            k = np.sort(o[C:])
            m[k[:-1]] = k[1:]
        if i == 2: m[:] = o[0]
        e[r] = m[:C]
        e[r ^ STEP[0]] = m[C:]
    return {**d, **weights(rng, layers(rng)), **stored(e)}
def setup_inputs_spread(rng):
    d = setup_inputs(rng)
    d["x"] = big(wide(rng, N, 128, 4 * C, cols=6))
    return d
def check_inputs(d):
    b = []
    for k in ("x", "u", "v"):
        a = np.abs(d[k].astype(np.float32))
        if not (np.isfinite(a).all() and ((a == 0) | (a >= 2.0 ** -30) & (a <= 2.0 ** 30)).all()): b.append("a value of " + k)
    if ((d["wc"] & 0x7F) == 0x7F).any(): b.append("a code of wc that is no number")
    none, least, most = [emit(mx_ref.quantize(np.full((128, 16), k, np.float32).astype(BF)))[1][0, 0] for k in (0.0, 2.0 ** -30, 2.0 ** 30)]
    for r in range(N):
        s = mx_ref.live(d["ws"][r])
        if ((s != none) & ((s < least) | (s > most))).any(): b.append("a scale of ws")
    if ((d["vg"] < 0) | (d["vg"] >= 2 * C)).any(): b.append("a pointer of vg")
    return b
def swapped(p, s):
    n = np.arange(2 * C)
    o = np.argsort(-(s + np.float32(0.0)), axis=0, kind="stable")
    a = p[o[7], n]
    asks = a != n
    low = np.where(asks, n, 2 * C)
    np.minimum.at(low, a[asks], n[asks])
    c = n[asks & (low == n) & (low[a] == n)]
    k, new = a[c], p.copy()
    for m in range(4):
        g = o[m, c]
        new[g, c], new[g, k] = p[g, k], p[g, c]
    g = o[7, c]
    new[g, c], new[g, k] = p[g, k], c
    return new
def reference(x, u, v, wc, ws, vg):
    qu = [mx_ref.quantize(u[r]) for r in range(N)]
    lay = [pk(wc[r], ws[r]) for r in range(N)]
    now = [x[r] for r in range(N)]
    at = [gentries(vg[r]) for r in range(N)]
    for t in range(R):
        had = [decode(mx_ref.quantize(now[r])).astype(BF) for r in range(N)]
        score = []
        for r in range(N):
            one, two = min(r, r ^ STEP[t]), max(r, r ^ STEP[t])
            z = np.concatenate([had[one], had[two]], axis=1)
            p = np.concatenate([at[one], at[two]], axis=1)
            a, b = gcols(z, at[r]), gcols(z, np.take_along_axis(p, at[r], axis=1))
            q = mx_ref.quantize(((a.astype(np.float32) + b.astype(np.float32)) * np.float32(0.5)).astype(BF))
            score.append(mx_ref.matmul(qu[r], q)[::16])
            now[r] = tile([np.maximum(mx_ref.matmul(pick(lay[r], np.arange(128 * i, 128 * i + 128)), q), np.float32(0.0)) * np.float32(0.03125) + had[r][:, i::4].astype(np.float32) for i in range(4)])
        for r in range(N):
            e = r ^ STEP[t]
            if r < e:
                p = swapped(np.concatenate([at[r], at[e]], axis=1), np.concatenate([score[r], score[e]], axis=1))
                at[r], at[e] = p[:, :C], p[:, C:]
    y, ov = np.zeros((N, 128, C), np.float32), np.zeros((N, 8, C), np.float32)
    oc, osc = np.zeros((N, 128, 4 * C), np.uint8), np.zeros((N, 16, C), np.uint8)
    for r in range(N):
        q = mx_ref.quantize(now[r])
        y[r] = mx_ref.matmul(mx_ref.quantize(v[r]), q)
        ov[r] = at[r]
        oc[r], osc[r] = emit(q)
    return {"y": y, "ov": ov, "oc": oc, "osc": osc}

@@ -1,0 +1,477 @@
+from concourse.mybir import dt, AluOpType as A, ActivationFunctionType as F
+
+C = 320
+STEP = [2, 1, 3]
+CODE = "float8_e4m3fn_x4"
+BLK = 336
+BIG = 16384.0
+
+SCRATCH = {}
+
+
+def _buf(name, n, dtype, where="sbuf"):
+    SCRATCH[name] = (where, [128] + (n if isinstance(n, list) else [n]), dtype)
+
+
+for _k in range(8):
+    _buf("ps%d" % _k, 512, "float32", "psum")
+for _n, _w in (("xin", 1280), ("uin", 512), ("vin", 512), ("Xt", 1280), ("Yt", 1280), ("Ct", 1280), ("Et", 2048), ("Wt", 1024),
+               ("Fh", 2560), ("Hh", 2560), ("tmp", 2560), ("D0", 5 * BLK), ("SO", 5 * BLK), ("one", BLK), ("diag", C), ("RD", C),
+               ("RS", C), ("keep16", C), ("c16", C), ("AZ", C), ("AB", C), ("AR", C), ("keep32", C)):
+    _buf(_n, _w, "bfloat16")
+for _n, _w in (("QX0", C), ("QX1", C), ("QX2", C), ("QX3", C), ("QP0", C), ("QP1", C), ("QP2", C), ("QY", C), ("QC", C), ("QE", 512),
+               ("QK", 256), ("QW", 512), ("QU", 128), ("QA", 128), ("QB", 128), ("QV", 128)):
+    _buf(_n, _w, CODE)
+    _buf("S" + _n, _w, "uint8")
+for _n, _w in (("TB", 1280), ("SB", C), ("V80", 80), ("SM", 80), ("keep8", 80), ("MQ", 32), ("SA", 48), ("A20", 20),
+               ("Tout", 672), ("GG", C), ("ZZ", C), ("PZ", 160), ("PS", 20), ("RT", C), ("PT", 80),
+               ("CF", 12), ("gv", 8), ("w1", 8), ("w2", 8), ("w3", 8), ("idm", 128), ("y20", 20), ("XW", 40), ("XQ", 40),
+               ("xc", 16), ("QQ", 40), ("DD", 40), ("MB", 40), ("ys", C), ("OT", 32), ("l1", 8), ("l2", 8), ("l3", 8),
+               ("P0", 40), ("P1", 40), ("P2", 40), ("P3", 40), ("MO", 96), ("MP0", 20), ("MP1", 20), ("MP2", 20)):
+    _buf(_n, _w, "float32")
+SMALL = ["pe", "k1", "k2", "s1", "s2", "c1", "c2", "n1", "low", "ee", "zz", "xk", "Dy", "sq", "a1", "a2"]
+_buf("SMA", 20 * len(SMALL), "float32")
+_buf("Tin", [42, 16], "float32")
+for _n, _w in (("vgi", 20), ("PI", 1), ("II", 24), ("CI", 8), ("NI", 40), ("Gi", 48), ("PtT", 48)):
+    _buf(_n, _w, "int32")
+for _n, _w in (("CU", 50), ("OFF", 20), ("PO0", 20), ("PO1", 20), ("PO2", 20), ("PP0", 20), ("PP1", 20), ("PP2", 20),
+               ("VO0", 90), ("VO1", 90), ("VO2", 90), ("VP0", 90), ("VP1", 90), ("VP2", 90)):
+    _buf(_n, _w, "uint16")
+SCRATCH["D2"] = ("dram", [16, 160], "float32")
+
+SEMAPHORES = ["cv", "cs", "ct", "cg", "sent", "lx0", "lx1", "lg", "lu", "lw", "lv", "out", "out2"]
+for _t in range(3):
+    SEMAPHORES += ["ax%d" % _t, "ap%d" % _t, "av%d" % _t, "am%d" % _t, "ra%d" % _t, "rb%d" % _t]
+
+
+def rank_program(g, core, T, topo):
+    r = T.rank_of(core)
+    if r is None:
+        return
+    V, S, PE = g.vector, g.scalar, g.tensor
+    queue = {"v": V, "s": S, "t": PE, "y": g.sync, "g": g}
+    own = {"v": "cv", "s": "cs", "t": "ct", "g": "cg"}
+    count, know, wrote, read, clock, seen = {}, {q: {} for q in queue}, {}, {}, {}, {}
+
+    def order(q, R, W):
+        need = {}
+        deps = []
+        for k in R:
+            deps += wrote.get(k, [])
+            if k.startswith("ps"):
+                deps += [d for d in read.get(k, []) if d[0] != own.get(q)]
+        for k in W:
+            deps += wrote.get(k, []) + read.get(k, [])
+        for s, n in deps:
+            if n is None:
+                n = count[s]
+            if q == "t" and s == "ct":
+                continue
+            if know[q].get(s, 0) < n:
+                need[s] = max(need.get(s, 0), n)
+        for s in list(need):
+            if any(o != s and clock.get((o, need[o]), {}).get(s, 0) >= need[s] for o in need):
+                need.pop(s)
+        for s, n in need.items():
+            queue[q].wait_ge(T.sem[s], n)
+            seen[s] = max(seen.get(s, 0), n)
+            know[q][s] = n
+            for o, m in clock.get((s, n), {}).items():
+                know[q][o] = max(know[q].get(o, 0), m)
+
+    def note(tok, R, W):
+        for k in R:
+            read.setdefault(k, []).append(tok)
+        for k in W:
+            wrote[k] = [tok]
+            read[k] = []
+
+    def op(q, R, W, call, *a, **kw):
+        R, W = R.split(), W.split()
+        order(q, R, W)
+        s = own[q]
+        call(*a, **kw).then_inc(T.sem[s], 1)
+        count[s] = count.get(s, 0) + 1
+        clock[(s, count[s])] = dict(know[q])
+        note((s, count[s]), R, W)
+
+    def dma(q, s, R, W, out, in_):
+        R, W = R.split(), W.split()
+        order(q, R, W)
+        queue[q].dma_start(out, in_).then_inc(T.sem[s], 16)
+        count[s] = count.get(s, 0) + 16
+        note((s, None), R, W)
+
+    def send(t, s, R, W, out, in_):
+        dst = T.cores[r ^ STEP[t]]
+        order("g", R.split(), [])
+        rid, pid = topo.addr(dst)[:2]
+        g.remote_dma(out, in_, T.sem[s], T.sem.sent, pid, rid, topo.mask(core, dst))
+        k = len(topo.engines(core, dst))
+        count["sent"] = count.get("sent", 0) + k
+        count[s] = count.get(s, 0) + k
+        note((s, None), [], W.split())
+
+    def ts(R, W, out, in0, s1, o0, s2=None, o1=None):
+        if o1 is None:
+            op("v", R, W, V.tensor_scalar, out, in0, s1, None, o0)
+        else:
+            op("v", R, W, V.tensor_scalar, out, in0, s1, s2, o0, o1)
+
+    def tt(R, W, out, a, b, o):
+        op("v", R, W, V.tensor_tensor, out, a, b, o)
+
+    def cp(R, W, out, a):
+        op("v", R, W, V.tensor_copy, out, a)
+
+    def scan(R, W, out, a, b, first, o0, o1):
+        op("v", R, W, V.tensor_tensor_scan, out, a, b, first, o0, o1)
+
+    def turn(R, W, out, a):
+        op("v", R, W, V.transpose, out, a)
+
+    def fill(W, ap, c):
+        op("v", "", W, V.memset, ap, c)
+
+    def act(R, W, out, a, f, **kw):
+        op("s", R, W, S.activation, out, a, f, **kw)
+
+    def quant(R, name, tile, lo=0, hi=None, key=None):
+        hi = hi or T[name].shape[1]
+        op("v", R, key or name, V.quantize_mx, T[name][:, lo:hi], T["S" + name][:, lo:hi], tile[:, 4 * lo:4 * hi])
+
+    def mm(bank, w, b, x):
+        op("t", w + " " + x, "ps%d" % bank, PE.matmul_mx, T["ps%d" % bank][:, 0:C], T[w][:, 128 * b:128 * b + 128],
+           T["S" + w][:, 128 * b:128 * b + 128], T[x][:], T["S" + x][:], True, True)
+
+    def iota(W, out, pat, cm, first=0):
+        op("g", "", W, g.iota, out, pat, first, cm, allow_small_or_imprecise_dtypes=True)
+
+    def ps(k):
+        return T["ps%d" % k][:, 0:C]
+
+    def sm(name):
+        k = 20 * SMALL.index(name)
+        return T.SMA[:, k:k + (10 if name in ("sq", "a1", "a2") else 20)]
+
+    def base(t):
+        return 0 if r < (r ^ STEP[t]) else C
+
+    JJ, GR, PAR, A0, A1, I8, K8, J32, G2K, GM5 = [T.CF[:, k:k + 1] for k in range(10)]
+    I1, I2, I3, NJ = T.II[:, 0:8], T.II[:, 8:16], T.II[:, 16:24], T.NI[:, 0:8]
+    shr, band = A.logical_shift_right, A.bitwise_and
+    H = C // 2
+
+    dma("y", "lx0", "", "xin0", T.xin[:, 0:4 * H], T.x[:, 0:4 * H])
+    dma("s", "lg", "", "vgi", T.vgi[:], T.vg[:])
+    dma("y", "lx1", "", "xin1", T.xin[:, 4 * H:4 * C], T.x[:, 4 * H:4 * C])
+
+    iota("PI", T.PI[:], [[0, 1]], 1)
+    iota("idm", T.idm[:], [[-1, 128]], 1)
+    iota("NI", T.NI[:], [[16, 40]], 0)
+    iota("gv", T.gv[:], [[1, 8]], 0)
+    fill("Et", T.Et[:], 0.0)
+    for k, (sh, m) in enumerate(((0, 15), (4, 7), (4, 1), (5, 1), (6, 1), (3, 7), (0, 7), (0, 31))):
+        ts("PI", "CI%d" % k, T.CI[:, k:k + 1], T.PI[:], sh, shr, m, band)
+    cp("vgi", "PO0", T.PO0[:], T.vgi[:])
+    send(0, "ap0", "PO0", "PP0", T.PP0[:], T.PO0[:])
+    for b in range(4):
+        ts("idm Et", "Et%d" % b, T.Et[:, 512 * b + b:512 * b + 512:4], T.idm[:], 0.0, A.is_equal)
+    cp("CI0 CI1 CI2 CI3 CI4 CI5 CI6 CI7", "CF", T.CF[:, 0:8], T.CI[:])
+
+    def send_half(t, tile, R, h):
+        q, p = "QX%d" % t, "QP%d" % t
+        quant(R, q, tile, H * h, H * h + H, q if h else q + "h")
+        send(t, "ax%d" % t, q if h else q + "h", p, T[p][:, H * h:H * h + H].bitcast(dt.uint8), T[q][:, H * h:H * h + H].bitcast(dt.uint8))
+        if h:
+            send(t, "ax%d" % t, q + " " + q + "h", p, T["S" + p][:], T["S" + q][:])
+
+    def relay(t):
+        P = "P%d" % t
+        x0 = base(t) // 16
+        tt(P + " XW", "pe", sm("pe"), T[P][:, 0:20], T.XW[:, x0:x0 + 20], A.is_equal)
+        cp(P, P + "b", T[P][:, 20:40], T[P][:, 0:20])
+        ts("pe CFg", "pe", sm("pe"), sm("pe"), 1024.0, A.mult, G2K, A.add)
+        tt("pe " + P, "PS", T.PS[:], sm("pe"), T[P][:, 0:20], A.add)
+        for k in range(8):
+            dma("y", "ra%d" % t, "PS", "D2_%d" % k, T.D2[:, 20 * k:20 * k + 20], T.PS[16 * k:16 * k + 16, :])
+        for k in range(8):
+            dma("y", "rb%d" % t, " ".join("D2_%d" % i for i in range(8)), "PZ%d" % k, T.PZ[16 * k:16 * k + 16, :], T.D2[:])
+
+    send_half(0, T.xin, "xin0", 0)
+    ts("NI CF", "XW", T.XW[:], T.NI[:], JJ, A.add)
+    ts("CF", "CFg", G2K, GR, 2048.0, A.mult)
+    cp("vgi", "P0", T.P0[:, 0:20], T.vgi[:])
+    send_half(0, T.xin, "xin1 QX0h", 1)
+    dma("y", "lu", "", "uin", T.uin[:], T.u[:])
+    quant("Et0 Et1 Et2 Et3", "QE", T.Et)
+    relay(0)
+    dma("y", "lw", "", "QWc", T.QW[:].bitcast(dt.uint8), T.wc[:])
+    dma("y", "lw", "", "QW", T.SQW[:], T.ws[:])
+    dma("y", "lv", "", "vin", T.vin[:], T.v[:])
+
+    def unpack(t, mine, engines):
+        q = ("QX%d" if mine else "QP%d") % t
+        at = base(t) if mine else C - base(t)
+        for b in range(4):
+            mm((4 if mine else 0) + b, "QE", b, q)
+        for b in range(4):
+            k = (4 if mine else 0) + b
+            key = "F%d%d" % (b, mine)
+            out = T.Fh[:, 640 * b + at:640 * b + at + C]
+            if engines[b] == "s":
+                act("ps%d" % k, key, out, ps(k), F.Copy)
+            else:
+                cp("ps%d" % k, key, out, ps(k))
+
+    def again(mine, b):
+        k = 2 + 2 * mine + b
+        return T.tmp[:, C * k:C * k + C]
+
+    def second(mine, n):
+        for b in range(n):
+            k = (4 if mine else 0) + b
+            act("ps%d" % k, "G%d%d" % (b, mine), again(mine, b), ps(k), F.Copy)
+
+    act("xin0 xin1", "Ct", T.Ct[:], T.xin[:], F.Copy, scale=0.0)
+    unpack(0, 1, "ssss")
+    second(1, 2)
+    act("xin0 xin1", "Tin", T.Tin[:], T.xin[:, 0:672], F.Identity, scale=0.0, bias=-1.0)
+
+    iota("Wt", T.Wt[:], [[0, 1024]], 0)
+    iota("c16", T.c16[:], [[0, 20], [1, 16]], 0)
+    iota("y20", T.y20[:], [[32, 20]], 0)
+    iota("xc", T.xc[:, 0:4], [[128, 4]], 1, -256)
+    iota("xc4", T.xc[:, 4:5], [[0, 1]], 2, 256)
+    iota("one", T.one[:], [[0, BLK]], 0, 1)
+    cp("XW", "NJ", NJ, T.XW[:, 0:8])
+    ts("gv CF", "w1", T.w1[:], T.gv[:], K8, A.is_equal)
+    ts("NJ", "i1", I1, NJ, 3, shr, 7, band)
+    ts("NJ", "i2", I2, NJ, 7, band)
+    ts("NJ", "i3", I3, NJ, 4, shr)
+    ts("i1", "CUa", T.CU[:, 0:8], I1, 16.0, A.mult)
+    ts("i2", "CUb", T.CU[:, 8:16], I2, 16.0, A.mult)
+    cp("i2", "CUr", T.CU[:, 28:36], I2)
+    cp("i3", "CUg", T.CU[:, 36:44], I3)
+    ts("gv CF", "w2", T.w2[:], T.gv[:], I8, A.is_lt)
+    ts("gv CF", "w3", T.w3[:], T.gv[:], I8, A.is_equal)
+    tt("w1 w2", "w1", T.w1[:], T.w1[:], T.w2[:], A.mult)
+    ts("NJ", "i3", I3, NJ, 3, shr)
+    ts("gv CF", "gw", T.l3[:], T.gv[:], K8, A.is_gt)
+    ts("i2 CF", "l1", T.l1[:], I2, 20.0, A.mult, PAR, A.add)
+    tt("w3 gw", "w3", T.w3[:], T.w3[:], T.l3[:], A.mult)
+    ts("i3", "l2", T.l2[:], I3, 2.0, A.mult)
+    tt("w1 w3", "w1", T.w1[:], T.w1[:], T.w3[:], A.subtract)
+    tt("l1 l2", "l1", T.l1[:], T.l1[:], T.l2[:], A.add)
+    ts("i3", "l2", T.l2[:], I3, 32.0, A.mult)
+    act("w1 CUr Wt", "Wta", T.Wt[:, 0:512:4], T.w1[:].indirect(T.CU[:, 28:36]), F.Copy, scale=1024.0)
+    act("w1 CUg Wt", "Wtb", T.Wt[:, 512:1024:4], T.w1[:].indirect(T.CU[:, 36:44]), F.Copy, scale=0.5)
+    cp("l1", "CUv", T.CU[:, 16:21], T.l1[:, 0:5])
+    tt("l2 i2", "l2", T.l2[:], T.l2[:], I2, A.add)
+    quant("uin", "QU", T.uin)
+    cp("l2", "CUt", T.CU[:, 44:49], T.l2[:, 0:5])
+    for w, o, key in (("QA", T.CU[:, 0:8], "CUa"), ("QB", T.CU[:, 8:16], "CUb")):
+        cp("QU " + key, w + "c", T[w][:].bitcast(dt.uint32), T.QU[:].bitcast(dt.uint32).indirect(o))
+        act("QU " + key + " " + w + "c", w, T["S" + w][:], T.SQU[:].indirect(o), F.Copy)
+    fill("keep8", T.keep8[:], 1.0)
+    fill("keep32", T.keep32[:], 1.0)
+    fill("AZ", T.AZ[:], 0.0)
+    fill("keep8", T.keep8[:, 0:80:8], 0.0)
+    fill("keep32", T.keep32[:, 0:C:32], 0.0)
+    fill("D0c", T.D0[:, C:5 * BLK:BLK], BIG)
+    fill("MQ", T.MQ[:], 0.0)
+    fill("SA", T.SA[:], 640.0)
+    ts("NJ", "i1", I1, NJ, 1, band)
+    ts("NJ", "i2", I2, NJ, 1, shr, 1, band)
+    ts("NJ", "i3", I3, NJ, 2, shr)
+    ts("i1 CF", "l1", T.l1[:], I1, A0, A.not_equal, 10.0, A.mult)
+    ts("i2 CF", "l2", T.l2[:], I2, A1, A.not_equal, 5.0, A.mult)
+    quant("Wta Wtb", "QK", T.Wt)
+
+    def late_constants():
+        ts("y20 CF", "y20", T.y20[:], T.y20[:], J32, A.add)
+        tt("l1 l2", "l1", T.l1[:], T.l1[:], T.l2[:], A.add)
+        ts("CF", "CFm", GM5, GR, -5.0, A.add)
+        tt("l1 i3", "l1", T.l1[:], T.l1[:], I3, A.add)
+        ts("XW", "l2", T.l2[:], T.XW[:, 0:8], 20.0, A.is_ge)
+        cp("l1", "CUm", T.CU[:, 22:24], T.l1[:, 0:2])
+        fill("one", T.one[:, C:C + 1], -160.0)
+        ts("c16 CF", "diag", T.diag[:], T.c16[:], JJ, A.is_equal)
+
+    def later_constants():
+        ts("l2 CF gw", "l3 gw", T.l3[:], T.l2[:], GR, A.mult)
+        ts("XW CF", "l1", T.l1[:], T.XW[:, 0:8], 16.0, A.mult, GR, A.add)
+        ts("l2", "l2", T.l2[:], T.l2[:], -311.0, A.mult)
+        tt("l1 l3", "l1", T.l1[:], T.l1[:], T.l3[:], A.subtract)
+        act("xc xc4", "xcb", T.xc[:, 8:13], T.xc[:, 0:5], F.Copy, scale=-BIG)
+
+    def last_constants():
+        act("y20 Tin", "Ty0", T.Tin[:, 0:40:2, 9], T.y20[:], F.Copy)
+        act("y20 Tin", "Ty1", T.Tin[:, 1:40:2, 9], T.y20[:], F.Copy)
+        act("c16", "keep16", T.keep16[:], T.c16[:], F.Sign)
+        act("XW", "XQ", T.XQ[:], T.XW[:], F.Identity, bias=0.25)
+        act("XW", "P3z", T.P3[:, 20:40], T.XW[:, 0:20], F.Copy)
+        tt("l1 l2", "l1", T.l1[:], T.l1[:], T.l2[:], A.add)
+        ts("l1", "CUz", T.CU[:, 24:27], T.l1[:, 0:3], 319.0, A.min)
+
+    ALLF = ["F%d0 F%d1" % (b, b) for b in range(4)]
+
+    def blend(t, mine, direct):
+        o = ("PO%d" if mine else "PP%d") % t
+        at = base(t) if mine else C - base(t)
+
+        def win(b):
+            return T.Fh[:, 640 * b:640 * b + 640].indirect(T[o][:])
+
+        def part(b):
+            return T.Hh[:, 640 * b + at:640 * b + at + C]
+        for b in range(direct, 4):
+            act(ALLF[b] + " " + o, "tmp%d" % b, T.tmp[:, C * (b - 2):C * (b - 1)], win(b), F.Copy)
+        for b in range(direct):
+            tt(ALLF[b] + " %s G%d%d" % (o, b, mine), "H%d%d" % (b, mine), part(b), win(b), again(mine, b), A.add)
+        for b in range(direct, 4):
+            k = (4 if mine else 0) + b
+            tt("tmp%d ps%d" % (b, k), "H%d%d" % (b, mine), part(b), T.tmp[:, C * (b - 2):C * (b - 1)], ps(k), A.add)
+
+    for t in range(3):
+        B0 = base(t)
+        b0 = B0 // 32
+        bp = (C - B0) // 32
+        P, Pn = "P%d" % t, "P%d" % (t + 1)
+        VO, VP, MO, MP = "VO%d" % t, "VP%d" % t, "MO%d" % t, "MP%d" % t
+        mo = T.MO[:, 32 * t:32 * t + 20]
+        if t == 0:
+            unpack(t, 0, "vsvs")
+            second(0, 2)
+            blend(t, 1, 2)
+        else:
+            relay(t)
+            blend(t, 1, 4)
+        blend(t, 0, 2)
+        for b, q, lo, hi in ((0, "s", 0, 20), (1, "s", 0, 20), (2, "v", 0, 20), (3, "s", 0, 10), (3, "v", 10, 20)):
+            w = T.Hh[:, 640 * b:640 * b + 640].indirect(T["PO%d" % t][:, lo:hi])
+            R, W = "H%d0 H%d1 PO%d" % (b, b, t), "Y%d%s" % (b, q)
+            out = T.Yt[:, 64 * lo + b:64 * hi:4]
+            if q == "s":
+                act(R, W, out, w, F.Copy, scale=0.5)
+            else:
+                ts(R, W, out, w, 0.5, A.mult)
+        quant("Y0s Y1s Y2v Y3s Y3v", "QY", T.Yt)
+        mm(5, "QB", 0, "QY")
+        mm(4, "QA", 0, "QY")
+        for b in range(4):
+            mm(b, "QW", b, "QY")
+        act("ps5", "SB", T.SB[:], ps(5), F.Copy)
+        act("CUv PZ0 PZ1 PZ2 PZ3 PZ4 PZ5 PZ6 PZ7", "PT", T.PT[:], T.PZ[:].indirect(T.CU[:, 16:21]), F.Copy)
+        if t == 0:
+            late_constants()
+        if t == 1:
+            quant("vin", "QV", T.vin)
+        tt("ps4 SB Ct", "Ct0", T.Ct[:, 0:1280:4], ps(4), T.SB[:], A.is_gt)
+        quant("Ct0", "QC", T.Ct)
+        mm(6, "QK", 0, "QC")
+        mm(7, "QK", 1, "QC")
+        for b in range(4):
+            act("ps%d" % b, "TB%d" % b, T.TB[:, C * b:C * b + C], ps(b), F.Relu, scale=0.03125)
+        if t == 0:
+            later_constants()
+        turn("ps6", "RT", T.RT[:], ps(6))
+        tt("RT CUt PT", "V80", T.V80[:], T.RT[:].indirect(T.CU[:, 44:49]), T.PT[:], A.add)
+        scan("V80 keep8", "SM", T.SM[:], T.keep8[:], T.V80[:], 0.0, A.mult, A.max)
+        cp("V80", VO + "v", T[VO][:, 0:80], T.V80[:])
+        top = T.SM[:, 7:80:8]
+        ts("SM", "a1", sm("a1"), top, -14336.0 - 256.0, A.add)
+        ts("SM", "a2", sm("a2"), top, 2.0, A.mult, -2 * 14336.0 - 768.0, A.add)
+        ts("SM", VO, T[VO][:, 80:90], top, -14336.0, A.add)
+        tt("a1 a2", "AZ", T.AZ[:, 0:C:32], sm("a1"), sm("a2"), A.max)
+        ts("SM", "sq", sm("sq"), top, 14336.0 + 640.0, A.is_ge, 640.0, A.mult)
+        scan("AZ keep32", "AB", T.AB[:], T.keep32[:], T.AZ[:], 0.0, A.mult, A.add)
+        send(t, "av%d" % t, VO + " " + VO + "v", VP, T[VP][:], T[VO][:])
+        turn("AB", "AR", T.AR[:], T.AB[:])
+        tt("sq y20", "SA", T.SA[:, 10:20], sm("sq"), T.y20[:, b0:b0 + 10], A.max)
+        for k in range(2, 5):
+            act("AR xcb", "D0_%d" % k, T.D0[:, BLK * k:BLK * k + C], T.AR[:], F.Abs, scale=BIG, bias=T.xc[:, 8 + k:9 + k])
+        for k in range(2):
+            ts("AR xc", "D0_%d" % k, T.D0[:, BLK * k:BLK * k + C], T.AR[:], T.xc[:, k:k + 1], A.not_equal, BIG, A.mult)
+        for k in range(5):
+            scan("D0_%d D0c one" % k, "SO%d" % k, T.SO[:, BLK * k:BLK * k + C + 1], T.D0[:, BLK * k:BLK * k + C + 1],
+                 T.one[:, 0:C + 1], 1024.0, A.min, A.subtract)
+        for h in range(2):
+            act("V80 Tin", "Tv%d1" % h, T.Tin[:, 2 * b0 + h:2 * b0 + 20:2, 0:8], T.V80[:], F.Copy)
+        so = "SO0 SO1 SO2 SO3 SO4 MQ"
+        for key, po, pi, c in (("MQa", (0, 128), (0, 128), 0), ("MQb", (64, 128), (0, 64), 5), ("MQc", (0, 64), (64, 128), 5)):
+            ts(so, key, T.MQ[po[0]:po[1], c:c + 5], T.SO[pi[0]:pi[1], C:5 * BLK:BLK], 160.0 + B0, A.add, 640.0, A.min)
+        for a in range(4):
+            cp("MQa MQb MQc", "MQ%d" % a, T.MQ[32 * (a ^ 1):32 * (a ^ 1) + 32, 10:20], T.MQ[32 * a:32 * a + 32, 0:10])
+        tt("MQa MQb MQc MQ0 MQ1 MQ2 MQ3 CUm SA", MO, T.MO[:, 32 * t:32 * t + 32], T.MQ[:].indirect(T.CU[:, 22:24]),
+           T.SA[:, 10 - b0:42 - b0], A.min)
+        send(t, "am%d" % t, MO, MP, T[MP][:], mo)
+        tt("ps7 diag", "RD", T.RD[:], ps(7), T.diag[:], A.mult)
+        if t == 0:
+            last_constants()
+        for b in range(4):
+            mm(4 + b, "QE", b, "QX%d" % t)
+        if t < 2:
+            for h in range(2):
+                for b in range(4):
+                    tt("TB%d ps%d" % (b, 4 + b), "X%d%d" % (b, h), T.Xt[:, 4 * H * h + b:4 * H * (h + 1):4],
+                       T.TB[:, C * b + H * h:C * b + H * h + H], T["ps%d" % (4 + b)][:, H * h:H * h + H], A.add)
+                send_half(t + 1, T.Xt, " ".join("X%d%d" % (b, h) for b in range(4)) + (" QX%dh" % (t + 1) if h else ""), h)
+            unpack(t + 1, 1, "ssss")
+            second(1, 4)
+            unpack(t + 1, 0, "ssss")
+            second(0, 2)
+        else:
+            for b in range(4):
+                tt("TB%d ps%d" % (b, 4 + b), "X%d0 X%d1" % (b, b), T.Xt[:, b:1280:4], T.TB[:, C * b:C * b + C], ps(4 + b), A.add)
+            quant("X00 X10 X20 X30", "QX3", T.Xt)
+            mm(0, "QV", 0, "QX3")
+            dma("y", "out", "QX3", "", T.oc[:], T.QX3[:].bitcast(dt.uint8))
+            for k in range(4):
+                dma("y", "out", "QX3", "", T.osc[4 * k:4 * k + 4, :], T.SQX3[32 * k:32 * k + 4, :])
+            act("ps0", "ys", T.ys[:], ps(0), F.Copy)
+            dma("y", "out", "ys", "", T.y[:], T.ys[:])
+        scan("RD keep16", "RS", T.RS[:], T.keep16[:], T.RD[:], 0.0, A.mult, A.add)
+        ts(VO, "A20a", T.A20[:, b0:b0 + 10], T[VO][:, 80:90], 0.25, A.add)
+        ts("RS CFm", "k1", sm("k1"), T.RS[:, 15:C:16], GM5, A.add)
+        ts(VP, "A20b", T.A20[:, bp:bp + 10], T[VP][:, 80:90], 0.25, A.add)
+        tt("k1", "k2", sm("k2"), sm("k1"), sm("k1"), A.mult)
+        tt("A20a A20b y20", "Dy", sm("Dy"), T.A20[:], T.y20[:], A.subtract)
+        tt(MO + " " + MP, "low", sm("low"), mo, T[MP][:], A.min)
+        cp(VP + " Tin", "Tv00", T.Tin[:, 2 * bp:2 * bp + 20:2, 0:8], T[VP][:, 0:80])
+        tt("low y20", "ee", sm("ee"), sm("low"), T.y20[:], A.is_equal)
+        cp(VP + " Tin", "Tv10", T.Tin[:, 2 * bp + 1:2 * bp + 20:2, 0:8], T[VP][:, 0:80])
+        tt("ee Dy", "zz", sm("zz"), sm("ee"), sm("Dy"), A.mult)
+        ts("k2", "k1", sm("k1"), sm("k2"), 2.0, A.is_lt, -4096.0, A.mult)
+        for h in range(2):
+            tt("zz low Tin", "Tu%d" % h, T.Tin[:, h:40:2, 8], sm("zz"), sm("low"), A.add)
+        turn("Tu0 Tu1 Tv00 Tv01 Tv10 Tv11 Ty0 Ty1", "Tout", T.Tout[:], T.Tin[:])
+        cp("Tu0 Tu1", "OFF", T.OFF[:], T.Tin[:, 2 * b0:2 * b0 + 20, 8])
+        tt("k1 XW", "xk", sm("xk"), sm("k1"), T.XW[:, 2 * b0:2 * b0 + 20], A.add)
+        cp("Tout OFF", "GG", T.GG[:], T.Tout[:].indirect(T.OFF[:]))
+        turn("GG", "ZZ", T.ZZ[:], T.GG[:])
+        cp("ZZ CUz", "Gi", T.Gi[:], T.ZZ[:].indirect(T.CU[:, 24:27]))
+        tt("ZZ XQ", "s2", sm("s2"), T.ZZ[:, 8:C:16], T.XQ[:, 2 * b0:2 * b0 + 20], A.is_equal)
+        ts("Gi", "c1", sm("c1"), T.Gi[:, 0:20], 8192.0, A.is_lt)
+        ts("Gi", "PtT", T.PtT[:], T.Gi[:], 1023, band)
+        tt("ZZ xk", "s1", sm("s1"), T.ZZ[:, 8:C:16], sm("xk"), A.is_equal)
+        tt("c1 s2", "c1", sm("c1"), sm("c1"), sm("s2"), A.mult)
+        ts("Gi", "c2", sm("c2"), T.Gi[:, 0:20], 14336.0, A.is_ge)
+        tt("PtT %s %sb" % (P, P), "DD", T.DD[:], T.PtT[:, 0:40], T[P][:], A.subtract)
+        tt("c1 s1", "QQa", T.QQ[:, 0:20], sm("c1"), sm("s1"), A.add)
+        tt("c2 s2", "QQb", T.QQ[:, 20:40], sm("c2"), sm("s2"), A.mult)
+        tt("QQa QQb DD", "MB", T.MB[:], T.QQ[:], T.DD[:], A.mult)
+        tt("MB", "n1", sm("n1"), T.MB[:, 0:20], T.MB[:, 20:40], A.add)
+        tt("n1 " + P, Pn, T[Pn][:, 0:20], sm("n1"), T[P][:, 0:20], A.add)
+        if t < 2:
+            o = "PO%d" % (t + 1)
+            cp(Pn, o, T[o][:], T[Pn][:, 0:20])
+            send(t + 1, "ap%d" % (t + 1), o, "PP%d" % (t + 1), T["PP%d" % (t + 1)][:], T[o][:])
+        else:
+            turn("P3 P3z", "OT", T.OT[:], T.P3[:, 0:32])
+            for k in range(8):
+                dma("ys"[k % 2], "out2", "OT", "", T.ov[k, :], T.OT[32 * (k // 2):32 * (k // 2) + 20, 16 * (k % 2):16 * (k % 2) + 16])
+
+    for s, n in count.items():
+        if seen.get(s, 0) < n:
+            g.wait_ge(T.sem[s], n)

@@ -3,8 +3,12 @@ from concourse.mybir import dt, AluOpType as A, ActivationFunctionType as F
 C = 320
 STEP = [2, 1, 3]
 CODE = "float8_e4m3fn_x4"
-BLK = 336
+SEG = 97
 BIG = 16384.0
+LAST = 14336.0
+NONE = 1048576.0 + 640.0
+ON_V = 6
+SCANS = ((0, 6), (6, 13), (13, 18), (18, 20))
 
 SCRATCH = {}
 
@@ -15,33 +19,30 @@ def _buf(name, n, dtype, where="sbuf"):
 
 for _k in range(8):
     _buf("ps%d" % _k, 512, "float32", "psum")
-for _n, _w in (("xin", 1280), ("uin", 512), ("vin", 512), ("Xt", 1280), ("Yt", 1280), ("Ct", 1280), ("Et", 2048), ("Wt", 1024),
-               ("Fh", 2560), ("Hh", 2560), ("tmp", 2560), ("D0", 5 * BLK), ("SO", 5 * BLK), ("one", BLK), ("diag", C), ("RD", C),
-               ("RS", C), ("keep16", C), ("c16", C), ("AZ", C), ("AB", C), ("AR", C), ("keep32", C)):
+for _n, _w in (("xin", 1280), ("uin", 512), ("vin", 512), ("Xt", 1280), ("Yt", 1536), ("Z", 1040), ("D0", 20 * SEG), ("SO", 20 * SEG),
+               ("ST", 7 * SEG), ("keep24", 24), ("D", 192), ("Mm", 192), ("SC", 192)):
     _buf(_n, _w, "bfloat16")
-for _n, _w in (("QX0", C), ("QX1", C), ("QX2", C), ("QX3", C), ("QP0", C), ("QP1", C), ("QP2", C), ("QY", C), ("QC", C), ("QE", 512),
-               ("QK", 256), ("QW", 512), ("QU", 128), ("QA", 128), ("QB", 128), ("QV", 128)):
+for _n, _w in (("QF0", 640), ("QF1", 640), ("QF2", 640), ("G0", 1280), ("G1", 1280), ("G2", 1280), ("B0", 640), ("B1", 640), ("B2", 640),
+               ("QX3", C), ("QY", 384), ("QE", 1024), ("QW", 512), ("QU", 128), ("QAB", 128), ("QV", 128)):
     _buf(_n, _w, CODE)
     _buf("S" + _n, _w, "uint8")
-for _n, _w in (("TB", 1280), ("SB", C), ("V80", 80), ("SM", 80), ("keep8", 80), ("MQ", 32), ("SA", 48), ("A20", 20),
-               ("Tout", 672), ("GG", C), ("ZZ", C), ("PZ", 160), ("PS", 20), ("RT", C), ("PT", 80),
-               ("CF", 12), ("gv", 8), ("w1", 8), ("w2", 8), ("w3", 8), ("idm", 128), ("y20", 20), ("XW", 40), ("XQ", 40),
-               ("xc", 16), ("QQ", 40), ("DD", 40), ("MB", 40), ("ys", C), ("OT", 32), ("l1", 8), ("l2", 8), ("l3", 8),
-               ("P0", 40), ("P1", 40), ("P2", 40), ("P3", 40), ("MO", 96), ("MP0", 20), ("MP1", 20), ("MP2", 20)):
+for _n, _w in (("TB", 1280), ("SL", 192), ("PT", 32), ("VR", 48), ("SM", 24), ("AB", 96), ("AR", 96), ("KK", 42),
+               ("M0", 42), ("M1", 20), ("SK", 48), ("sk", 8), ("MO", 60), ("MP0", 20), ("MP1", 20), ("MP2", 20),
+               ("VV0", 192), ("VV1", 192), ("VV2", 192), ("Tin", [42, 16]), ("Tout", 672), ("GG", C), ("ZZ", [20, 16]),
+               ("VF", 96), ("ZY", 64), ("va", 48), ("vh", 48), ("vv", 48), ("dd", 48), ("T1", 32), ("Z3", [4, 16]), ("ZT", 64),
+               ("ZO", [20, 2]), ("W2", [20, 2]), ("q2", 40), ("Q3", 120), ("S3", 120), ("PN", 120),
+               ("ne", 40), ("PZ", 256), ("PA", 96), ("OI", 64), ("OT", 64), ("ys", C),
+               ("idm", 128), ("CF", 26), ("NI", 8), ("NJ", 8), ("t8", 8), ("CL", 24), ("l1", 8), ("xc", 20), ("xcb", 20),
+               ("YJ", 80), ("Y16", 40), ("C1", 48), ("CZ", 48), ("CK", 6)):
     _buf(_n, _w, "float32")
-SMALL = ["pe", "k1", "k2", "s1", "s2", "c1", "c2", "n1", "low", "ee", "zz", "xk", "Dy", "sq", "a1", "a2"]
-_buf("SMA", 20 * len(SMALL), "float32")
-_buf("Tin", [42, 16], "float32")
-for _n, _w in (("vgi", 20), ("PI", 1), ("II", 24), ("CI", 8), ("NI", 40), ("Gi", 48), ("PtT", 48)):
+for _n, _w in (("Vi", 60), ("PI", 2), ("CI", 16), ("I1", 20), ("I2", 20)):
     _buf(_n, _w, "int32")
-for _n, _w in (("CU", 50), ("OFF", 20), ("PO0", 20), ("PO1", 20), ("PO2", 20), ("PP0", 20), ("PP1", 20), ("PP2", 20),
-               ("VO0", 90), ("VO1", 90), ("VO2", 90), ("VP0", 90), ("VP1", 90), ("VP2", 90)):
+for _n, _w in (("CU", 24), ("CP", 4), ("OFF", 20), ("PO0", 48), ("PO1", 40), ("PO2", 40), ("PP0", 40), ("PP1", 40), ("PP2", 40)):
     _buf(_n, _w, "uint16")
-SCRATCH["D2"] = ("dram", [16, 160], "float32")
 
 SEMAPHORES = ["cv", "cs", "ct", "cg", "sent", "lx0", "lx1", "lg", "lu", "lw", "lv", "out", "out2"]
 for _t in range(3):
-    SEMAPHORES += ["ax%d" % _t, "ap%d" % _t, "av%d" % _t, "am%d" % _t, "ra%d" % _t, "rb%d" % _t]
+    SEMAPHORES += ["ax%d" % _t, "ap%d" % _t, "av%d" % _t, "am%d" % _t]
 
 
 def rank_program(g, core, T, topo):
@@ -133,344 +134,318 @@ def rank_program(g, core, T, topo):
     def fill(W, ap, c):
         op("v", "", W, V.memset, ap, c)
 
-    def act(R, W, out, a, f, **kw):
+    def act(R, W, out, a, f=F.Copy, **kw):
         op("s", R, W, S.activation, out, a, f, **kw)
 
-    def quant(R, name, tile, lo=0, hi=None, key=None):
-        hi = hi or T[name].shape[1]
-        op("v", R, key or name, V.quantize_mx, T[name][:, lo:hi], T["S" + name][:, lo:hi], tile[:, 4 * lo:4 * hi])
+    def sfill(W, ap, n, c):
+        act("xin0", W, ap, T.xin[:, 0:n], F.Identity, scale=0.0, bias=c)
 
-    def mm(bank, w, b, x):
-        op("t", w + " " + x, "ps%d" % bank, PE.matmul_mx, T["ps%d" % bank][:, 0:C], T[w][:, 128 * b:128 * b + 128],
-           T["S" + w][:, 128 * b:128 * b + 128], T[x][:], T["S" + x][:], True, True)
+    def quant(R, W, name, lo, hi, tile):
+        op("v", R, W, V.quantize_mx, T[name][:, lo:hi], T["S" + name][:, lo:hi], tile)
+
+    def mm(bank, w, at, x, lo, n, R, start=True, stop=True):
+        op("t", R, "ps%d" % bank, PE.matmul_mx, T["ps%d" % bank][:, 0:n], T[w][:, at:at + 128], T["S" + w][:, at:at + 128],
+           T[x][:, lo:lo + n], T["S" + x][:, lo:lo + n], start, stop)
 
     def iota(W, out, pat, cm, first=0):
         op("g", "", W, g.iota, out, pat, first, cm, allow_small_or_imprecise_dtypes=True)
 
-    def ps(k):
-        return T["ps%d" % k][:, 0:C]
+    def ps(k, n=C):
+        return T["ps%d" % k][:, 0:n]
 
-    def sm(name):
-        k = 20 * SMALL.index(name)
-        return T.SMA[:, k:k + (10 if name in ("sq", "a1", "a2") else 20)]
+    def upper(t):
+        return int(r > (r ^ STEP[t]))
 
-    def base(t):
-        return 0 if r < (r ^ STEP[t]) else C
+    def words(ap):
+        return ap.bitcast(dt.uint32)
 
-    JJ, GR, PAR, A0, A1, I8, K8, J32, G2K, GM5 = [T.CF[:, k:k + 1] for k in range(10)]
-    I1, I2, I3, NJ = T.II[:, 0:8], T.II[:, 8:16], T.II[:, 16:24], T.NI[:, 0:8]
+    def pick(R, W, dst, at, src, lo, off, q="vs"):
+        n = 16 * off.shape[1]
+        if "v" in q:
+            cp(R, W + "c", words(T[dst][:, at:at + n]), words(T[src][:, lo:lo + 640]).indirect(off))
+        if "s" in q:
+            act(R, W + "s", T["S" + dst][:, at:at + n], T["S" + src][:, lo:lo + 640].indirect(off))
+
+    def spread(key, buf, n, pitch):
+        act(key, key + "a", buf[0:64, pitch:pitch + n], buf[64:128, 0:n])
+        act(key, key + "b", buf[64:128, pitch:pitch + n], buf[0:64, 0:n])
+        for a in range(4):
+            act("%s %sa %sb" % (key, key, key), "%s_%d" % (key, a), buf[32 * (a ^ 1):32 * (a ^ 1) + 32, 2 * pitch:3 * pitch + n],
+                buf[32 * a:32 * a + 32, 0:pitch + n])
+        return " ".join("%s_%d" % (key, a) for a in range(4))
+
     shr, band = A.logical_shift_right, A.bitwise_and
+    DIGITS = (("h16", 0, 16), ("i", 0, 15), ("i8", 0, 8), ("k7", 0, 7), ("r32", 0, 96), ("e", 0, 1), ("m", 0, 31), ("p112", 0, 112),
+              ("k0", 1, 1), ("r0", 5, 1), ("k1", 2, 1), ("r1", 6, 1), ("k8", 0, 7))
+    MORE = ("lowh", "h", "even", "x0", "sg", "dR", "dT", "dV", "dS", "end", "g0", "g1")
+    col = {n: T.CF[:, k:k + 1] for k, n in enumerate([d[0] for d in DIGITS] + list(MORE))}
+    CAB, CR, CT, CV, CS = (0, 8), (8, 11), (12, 14), (14, 17), (18, 20)
+
+    def cl(c):
+        return T.CL[:, c[0]:c[1]]
+
+    def cu(c):
+        return T.CU[:, c[0]:c[1]]
     H = C // 2
 
+    def send_state(t, lo, hi, R):
+        q, at = "QF%d" % t, C * upper(t)
+        send(t, "ax%d" % t, R, q + "p", T[q][:, at + lo:at + hi].bitcast(dt.uint8), T[q][:, at + lo:at + hi].bitcast(dt.uint8))
+        if hi == C:
+            send(t, "ax%d" % t, R, q + "p", T["S" + q][:, at:at + C], T["S" + q][:, at:at + C])
+
     dma("y", "lx0", "", "xin0", T.xin[:, 0:4 * H], T.x[:, 0:4 * H])
-    dma("s", "lg", "", "vgi", T.vgi[:], T.vg[:])
     dma("y", "lx1", "", "xin1", T.xin[:, 4 * H:4 * C], T.x[:, 4 * H:4 * C])
-
-    iota("PI", T.PI[:], [[0, 1]], 1)
-    iota("idm", T.idm[:], [[-1, 128]], 1)
-    iota("NI", T.NI[:], [[16, 40]], 0)
-    iota("gv", T.gv[:], [[1, 8]], 0)
-    fill("Et", T.Et[:], 0.0)
-    for k, (sh, m) in enumerate(((0, 15), (4, 7), (4, 1), (5, 1), (6, 1), (3, 7), (0, 7), (0, 31))):
-        ts("PI", "CI%d" % k, T.CI[:, k:k + 1], T.PI[:], sh, shr, m, band)
-    cp("vgi", "PO0", T.PO0[:], T.vgi[:])
-    send(0, "ap0", "PO0", "PP0", T.PP0[:], T.PO0[:])
-    for b in range(4):
-        ts("idm Et", "Et%d" % b, T.Et[:, 512 * b + b:512 * b + 512:4], T.idm[:], 0.0, A.is_equal)
-    cp("CI0 CI1 CI2 CI3 CI4 CI5 CI6 CI7", "CF", T.CF[:, 0:8], T.CI[:])
-
-    def send_half(t, tile, R, h):
-        q, p = "QX%d" % t, "QP%d" % t
-        quant(R, q, tile, H * h, H * h + H, q if h else q + "h")
-        send(t, "ax%d" % t, q if h else q + "h", p, T[p][:, H * h:H * h + H].bitcast(dt.uint8), T[q][:, H * h:H * h + H].bitcast(dt.uint8))
-        if h:
-            send(t, "ax%d" % t, q + " " + q + "h", p, T["S" + p][:], T["S" + q][:])
-
-    def relay(t):
-        P = "P%d" % t
-        x0 = base(t) // 16
-        tt(P + " XW", "pe", sm("pe"), T[P][:, 0:20], T.XW[:, x0:x0 + 20], A.is_equal)
-        cp(P, P + "b", T[P][:, 20:40], T[P][:, 0:20])
-        ts("pe CFg", "pe", sm("pe"), sm("pe"), 1024.0, A.mult, G2K, A.add)
-        tt("pe " + P, "PS", T.PS[:], sm("pe"), T[P][:, 0:20], A.add)
-        for k in range(8):
-            dma("y", "ra%d" % t, "PS", "D2_%d" % k, T.D2[:, 20 * k:20 * k + 20], T.PS[16 * k:16 * k + 16, :])
-        for k in range(8):
-            dma("y", "rb%d" % t, " ".join("D2_%d" % i for i in range(8)), "PZ%d" % k, T.PZ[16 * k:16 * k + 16, :], T.D2[:])
-
-    send_half(0, T.xin, "xin0", 0)
-    ts("NI CF", "XW", T.XW[:], T.NI[:], JJ, A.add)
-    ts("CF", "CFg", G2K, GR, 2048.0, A.mult)
-    cp("vgi", "P0", T.P0[:, 0:20], T.vgi[:])
-    send_half(0, T.xin, "xin1 QX0h", 1)
+    dma("y", "lg", "", "Vi", T.Vi[:, 20:40], T.vg[:])
+    dma("y", "lg", "", "Vi1", T.Vi[16:128, 0:20], T.vg[0:112, :])
+    dma("y", "lg", "", "Vi2", T.Vi[0:112, 40:60], T.vg[16:128, :])
     dma("y", "lu", "", "uin", T.uin[:], T.u[:])
-    quant("Et0 Et1 Et2 Et3", "QE", T.Et)
-    relay(0)
-    dma("y", "lw", "", "QWc", T.QW[:].bitcast(dt.uint8), T.wc[:])
-    dma("y", "lw", "", "QW", T.SQW[:], T.ws[:])
+
+    iota("PI", T.PI[:], [[1, 2]], 1)
+    iota("NI", T.NI[:], [[16, 8]], 0)
+    iota("idm", T.idm[:], [[-1, 128]], 1)
+    fill("Z", T.Z[:], 0.0)
+    for k, (n, sh, m) in enumerate(DIGITS):
+        ts("PI", "CI%d" % k, T.CI[:, k:k + 1], T.PI[:, 1:2] if n == "k8" else T.PI[:, 0:1], sh, shr, m, band)
+    cp(" ".join("CI%d" % k for k in range(13)), "CF h16 i", T.CF[:, 0:13], T.CI[:, 0:13])
+    fill("Ypad", T.Yt[:, 1024:1536], 0.0)
+    ts("NI i", "NJ", T.NJ[:], T.NI[:], col["i"], A.add)
+    ts("h16", "lowh", col["lowh"], col["h16"], -1.25, A.mult, 20.0, A.add)
+    at0 = C * upper(0)
+    quant("xin0", "QF0h", "QF0", at0, at0 + H, T.xin[:, 0:4 * H])
+    send_state(0, 0, H, "QF0h")
+    ts("h16", "h", col["h"], col["h16"], 0.0625, A.mult)
+    ts("h16", "even", col["even"], col["h16"], 0.0, A.is_equal)
+    ts("NJ lowh", "CP", T.CP[:, 0:3], T.NJ[:, 0:3], 39.0, A.min, col["lowh"], A.add)
+    quant("xin1", "QF0", "QF0", at0 + H, at0 + C, T.xin[:, 4 * H:4 * C])
+    send_state(0, H, C, "QF0 QF0h")
+    cp("Vi Vi1 Vi2 CP", "PO0", T.PO0[:], T.Vi[:].indirect(T.CP[:, 0:3]))
+    send(0, "ap0", "PO0", "PP0", T.PP0[:], T.PO0[:, 0:40])
+    dma("y", "lw", "QF0p", "QW", T.QW[:].bitcast(dt.uint8), T.wc[:])
+    dma("y", "lw", "", "QW2", T.SQW[:], T.ws[:])
     dma("y", "lv", "", "vin", T.vin[:], T.v[:])
 
-    def unpack(t, mine, engines):
-        q = ("QX%d" if mine else "QP%d") % t
-        at = base(t) if mine else C - base(t)
+    for par in range(2):
+        ts("idm Z h even", "Z%d" % par, T.Z[:, 520 * par + 3:520 * par + 515:4], T.idm[:], 0.0, A.is_equal,
+           col["h" if par else "even"], A.mult)
+    quant("Ypad", "QYpad", "QY", 256, 384, T.Yt[:, 1024:1536])
+    for par in range(2):
         for b in range(4):
-            mm((4 if mine else 0) + b, "QE", b, q)
-        for b in range(4):
-            k = (4 if mine else 0) + b
-            key = "F%d%d" % (b, mine)
-            out = T.Fh[:, 640 * b + at:640 * b + at + C]
-            if engines[b] == "s":
-                act("ps%d" % k, key, out, ps(k), F.Copy)
-            else:
-                cp("ps%d" % k, key, out, ps(k))
+            at = 512 * par + 128 * b
+            quant("Z%d" % par, "QE%d%d" % (par, b), "QE", at, at + 128, T.Z[:, 520 * par + 3 - b:520 * par + 515 - b])
 
-    def again(mine, b):
-        k = 2 + 2 * mine + b
-        return T.tmp[:, C * k:C * k + C]
+    iota("xc", T.xc[:], [[32, 20]], 0, int(LAST) + 1)
+    iota("YJ", T.YJ[:], [[16, 40], [0, 2]], 0, 1)
+    iota("C1", T.C1[:], [[C, 2], [32, 12], [0, 2]], 0, 1)
+    iota("CK", T.CK[:], [[C, 2], [128, 3]], 1)
+    iota("ST", T.ST[:], [[0, 7 * SEG]], 0, 1)
+    sfill("SK", T.SK[:], 48, NONE)
+    sfill("KK", T.KK[:], 42, NONE)
+    sfill("ZY", T.ZY[:], 64, 0.0)
+    sfill("OI", T.OI[:], 64, 0.0)
+    sfill("Tin", T.Tin[:, 0:21, :], 336, -1.0)
+    sfill("Tin2", T.Tin[:, 21:42, :], 336, -1.0)
+    sfill("PA", T.PA[:], 96, 0.0)
+    sfill("PZ", T.PZ[:], 256, 0.0)
+    act("h CF", "dR", col["dR"], col["e"], F.Identity, scale=19.0, bias=col["h"])
+    act("CF", "dT", col["dT"], col["p112"], F.Identity, scale=0.125, bias=col["e"])
+    act("CF", "dV", col["dV"], col["r32"], F.Identity, scale=0.0625, bias=col["e"])
+    act("CF", "dS", col["dS"], col["r32"], F.Identity, scale=-0.03125, bias=6.0)
+    act("CF", "end", col["end"], col["r32"], F.Identity, scale=-1.0, bias=-127.0)
+    for e in range(2):
+        act("CF", "g%d" % e, col["g%d" % e], col["r32"], F.Identity, scale=128.0, bias=2048.0 * e)
+    ts("CF", "x0", col["x0"], col["k0"], col["r0"], A.not_equal, 2.0, A.mult)
+    ts("NI CF", "t8", T.t8[:], T.NI[:], col["i8"], A.add, 0.125, A.mult)
+    ts("CF x0", "sg", col["sg"], col["k1"], col["r1"], A.not_equal, col["x0"], A.add)
+    ts("NJ", "l1", T.l1[:, 0:3], T.NJ[:, 0:3], 24.0, A.is_ge, 16.0, A.mult)
+    ts("t8 CF", "CLa", T.CL[:, 0:4], T.t8[:, 0:4], col["k8"], A.max, 16.0, A.mult)
+    ts("t8 CF", "CLb", T.CL[:, 4:8], T.t8[:, 0:4], col["k7"], A.min, 16.0, A.mult)
+    act("sg dT", "dT", col["dT"], col["sg"], F.Identity, scale=64.0, bias=col["dT"])
+    act("sg dV", "dV", col["dV"], col["sg"], F.Identity, scale=48.0, bias=col["dV"])
+    act("NJ dS", "CLs", cl(CS), T.NJ[:, 0:2], F.Identity, bias=col["dS"])
+    act("t8 dT", "CLt", cl(CT), T.t8[:, 0:2], F.Identity, scale=16.0, bias=col["dT"])
+    act("t8 dV", "CLv", cl(CV), T.t8[:, 0:3], F.Identity, scale=8.0, bias=col["dV"])
+    act("l1 dR", "l1", T.l1[:, 0:3], T.l1[:, 0:3], F.Identity, bias=col["dR"])
+    quant("uin", "QU", "QU", 0, 128, T.uin[:])
+    cp("CLa CLb", "CAB", cu(CAB), cl(CAB))
+    tt("l1 NJ", "CLr", cl(CR), T.l1[:, 0:3], T.NJ[:, 0:3], A.add)
+    cp("QU CAB", "QABc", words(T.QAB[:]), words(T.QU[:]).indirect(cu(CAB)))
+    act("QU CAB", "QABs", T.SQAB[:], T.SQU[:].indirect(cu(CAB)))
+    for c, k in ((CR, "CLr"), (CT, "CLt"), (CV, "CLv"), (CS, "CLs")):
+        cp(k, "CU" + k[2], cu(c), cl(c))
+    ts("YJ i", "YJ", T.YJ[:], T.YJ[:], col["i"], A.add)
+    for e in range(2):
+        ts("PO0", "PN%d" % e, T.PN[:, 3 * e + 2:120:6], T.PO0[:, 20 * e:20 * e + 20], 1.0, A.add)
 
-    def second(mine, n):
-        for b in range(n):
-            k = (4 if mine else 0) + b
-            act("ps%d" % k, "G%d%d" % (b, mine), again(mine, b), ps(k), F.Copy)
+    def pointers(t):
+        u = upper(t)
+        pn = T.PN[:, 2:120:3]
+        tt("PN0 PN1 YJ", "ne", T.ne[:], pn, T.YJ[:, 40 * u:40 * u + 40], A.not_equal)
+        ts("PO%d PA" % t, "PAo", T.PA[:, 40 * u:40 * u + 40], T["PO%d" % t][:, 0:40], 1.0, A.add)
+        tt("ne PN0 PN1", "PZ", T.PZ[:, 0:40], T.ne[:], pn, A.mult)
+        for e in range(2):
+            act("PZ g%d" % e, "PZ", T.PZ[:, e:40:2], T.PZ[:, e:40:2], F.Identity, bias=col["g%d" % e])
+        k = spread("PZ", T.PZ, 40, 64)
+        act(k + " CUt", "PT", T.PT[:], T.PZ[:].indirect(cu(CT)))
 
-    act("xin0 xin1", "Ct", T.Ct[:], T.xin[:], F.Copy, scale=0.0)
-    unpack(0, 1, "ssss")
-    second(1, 2)
-    act("xin0 xin1", "Tin", T.Tin[:], T.xin[:, 0:672], F.Identity, scale=0.0, bias=-1.0)
-
-    iota("Wt", T.Wt[:], [[0, 1024]], 0)
-    iota("c16", T.c16[:], [[0, 20], [1, 16]], 0)
-    iota("y20", T.y20[:], [[32, 20]], 0)
-    iota("xc", T.xc[:, 0:4], [[128, 4]], 1, -256)
-    iota("xc4", T.xc[:, 4:5], [[0, 1]], 2, 256)
-    iota("one", T.one[:], [[0, BLK]], 0, 1)
-    cp("XW", "NJ", NJ, T.XW[:, 0:8])
-    ts("gv CF", "w1", T.w1[:], T.gv[:], K8, A.is_equal)
-    ts("NJ", "i1", I1, NJ, 3, shr, 7, band)
-    ts("NJ", "i2", I2, NJ, 7, band)
-    ts("NJ", "i3", I3, NJ, 4, shr)
-    ts("i1", "CUa", T.CU[:, 0:8], I1, 16.0, A.mult)
-    ts("i2", "CUb", T.CU[:, 8:16], I2, 16.0, A.mult)
-    cp("i2", "CUr", T.CU[:, 28:36], I2)
-    cp("i3", "CUg", T.CU[:, 36:44], I3)
-    ts("gv CF", "w2", T.w2[:], T.gv[:], I8, A.is_lt)
-    ts("gv CF", "w3", T.w3[:], T.gv[:], I8, A.is_equal)
-    tt("w1 w2", "w1", T.w1[:], T.w1[:], T.w2[:], A.mult)
-    ts("NJ", "i3", I3, NJ, 3, shr)
-    ts("gv CF", "gw", T.l3[:], T.gv[:], K8, A.is_gt)
-    ts("i2 CF", "l1", T.l1[:], I2, 20.0, A.mult, PAR, A.add)
-    tt("w3 gw", "w3", T.w3[:], T.w3[:], T.l3[:], A.mult)
-    ts("i3", "l2", T.l2[:], I3, 2.0, A.mult)
-    tt("w1 w3", "w1", T.w1[:], T.w1[:], T.w3[:], A.subtract)
-    tt("l1 l2", "l1", T.l1[:], T.l1[:], T.l2[:], A.add)
-    ts("i3", "l2", T.l2[:], I3, 32.0, A.mult)
-    act("w1 CUr Wt", "Wta", T.Wt[:, 0:512:4], T.w1[:].indirect(T.CU[:, 28:36]), F.Copy, scale=1024.0)
-    act("w1 CUg Wt", "Wtb", T.Wt[:, 512:1024:4], T.w1[:].indirect(T.CU[:, 36:44]), F.Copy, scale=0.5)
-    cp("l1", "CUv", T.CU[:, 16:21], T.l1[:, 0:5])
-    tt("l2 i2", "l2", T.l2[:], T.l2[:], I2, A.add)
-    quant("uin", "QU", T.uin)
-    cp("l2", "CUt", T.CU[:, 44:49], T.l2[:, 0:5])
-    for w, o, key in (("QA", T.CU[:, 0:8], "CUa"), ("QB", T.CU[:, 8:16], "CUb")):
-        cp("QU " + key, w + "c", T[w][:].bitcast(dt.uint32), T.QU[:].bitcast(dt.uint32).indirect(o))
-        act("QU " + key + " " + w + "c", w, T["S" + w][:], T.SQU[:].indirect(o), F.Copy)
-    fill("keep8", T.keep8[:], 1.0)
-    fill("keep32", T.keep32[:], 1.0)
-    fill("AZ", T.AZ[:], 0.0)
-    fill("keep8", T.keep8[:, 0:80:8], 0.0)
-    fill("keep32", T.keep32[:, 0:C:32], 0.0)
-    fill("D0c", T.D0[:, C:5 * BLK:BLK], BIG)
-    fill("MQ", T.MQ[:], 0.0)
-    fill("SA", T.SA[:], 640.0)
-    ts("NJ", "i1", I1, NJ, 1, band)
-    ts("NJ", "i2", I2, NJ, 1, shr, 1, band)
-    ts("NJ", "i3", I3, NJ, 2, shr)
-    ts("i1 CF", "l1", T.l1[:], I1, A0, A.not_equal, 10.0, A.mult)
-    ts("i2 CF", "l2", T.l2[:], I2, A1, A.not_equal, 5.0, A.mult)
-    quant("Wta Wtb", "QK", T.Wt)
-
-    def late_constants():
-        ts("y20 CF", "y20", T.y20[:], T.y20[:], J32, A.add)
-        tt("l1 l2", "l1", T.l1[:], T.l1[:], T.l2[:], A.add)
-        ts("CF", "CFm", GM5, GR, -5.0, A.add)
-        tt("l1 i3", "l1", T.l1[:], T.l1[:], I3, A.add)
-        ts("XW", "l2", T.l2[:], T.XW[:, 0:8], 20.0, A.is_ge)
-        cp("l1", "CUm", T.CU[:, 22:24], T.l1[:, 0:2])
-        fill("one", T.one[:, C:C + 1], -160.0)
-        ts("c16 CF", "diag", T.diag[:], T.c16[:], JJ, A.is_equal)
-
-    def later_constants():
-        ts("l2 CF gw", "l3 gw", T.l3[:], T.l2[:], GR, A.mult)
-        ts("XW CF", "l1", T.l1[:], T.XW[:, 0:8], 16.0, A.mult, GR, A.add)
-        ts("l2", "l2", T.l2[:], T.l2[:], -311.0, A.mult)
-        tt("l1 l3", "l1", T.l1[:], T.l1[:], T.l3[:], A.subtract)
-        act("xc xc4", "xcb", T.xc[:, 8:13], T.xc[:, 0:5], F.Copy, scale=-BIG)
-
-    def last_constants():
-        act("y20 Tin", "Ty0", T.Tin[:, 0:40:2, 9], T.y20[:], F.Copy)
-        act("y20 Tin", "Ty1", T.Tin[:, 1:40:2, 9], T.y20[:], F.Copy)
-        act("c16", "keep16", T.keep16[:], T.c16[:], F.Sign)
-        act("XW", "XQ", T.XQ[:], T.XW[:], F.Identity, bias=0.25)
-        act("XW", "P3z", T.P3[:, 20:40], T.XW[:, 0:20], F.Copy)
-        tt("l1 l2", "l1", T.l1[:], T.l1[:], T.l2[:], A.add)
-        ts("l1", "CUz", T.CU[:, 24:27], T.l1[:, 0:3], 319.0, A.min)
-
-    ALLF = ["F%d0 F%d1" % (b, b) for b in range(4)]
-
-    def blend(t, mine, direct):
-        o = ("PO%d" if mine else "PP%d") % t
-        at = base(t) if mine else C - base(t)
-
-        def win(b):
-            return T.Fh[:, 640 * b:640 * b + 640].indirect(T[o][:])
-
-        def part(b):
-            return T.Hh[:, 640 * b + at:640 * b + at + C]
-        for b in range(direct, 4):
-            act(ALLF[b] + " " + o, "tmp%d" % b, T.tmp[:, C * (b - 2):C * (b - 1)], win(b), F.Copy)
-        for b in range(direct):
-            tt(ALLF[b] + " %s G%d%d" % (o, b, mine), "H%d%d" % (b, mine), part(b), win(b), again(mine, b), A.add)
-        for b in range(direct, 4):
-            k = (4 if mine else 0) + b
-            tt("tmp%d ps%d" % (b, k), "H%d%d" % (b, mine), part(b), T.tmp[:, C * (b - 2):C * (b - 1)], ps(k), A.add)
+    pointers(0)
+    act("C1 CF", "C1", T.C1[:], T.C1[:], F.Identity, bias=col["m"])
+    act("xc CF", "xc", T.xc[:], T.xc[:], F.Identity, bias=col["m"])
+    act("C1", "CZ", T.CZ[:], T.C1[:], F.Identity, scale=1024.0, bias=3072.0)
+    act("xc", "xcb", T.xcb[:], T.xc[:], scale=-BIG)
+    act("CK", "CK", T.CK[:], T.CK[:], F.Identity, scale=1024.0, bias=-LAST - 1.0)
+    act("YJ", "Y16", T.Y16[:], T.YJ[:, 0:80:2], F.Identity, bias=-4097.0)
+    fill("Mm", T.Mm[:], 1.0)
+    fill("keep24", T.keep24[:], 1.0)
+    fill("Q30", T.Q3[:, 0:120:3], 0.0)
+    fill("D0r", T.D0[:, SEG - 1:20 * SEG:SEG], BIG)
+    fill("Mm", T.Mm[:, 0:192:8], 0.0)
+    fill("keep24", T.keep24[:, 0:24:8], 0.0)
+    fill("Mm9", T.Mm[:, 7:192:8], 2048.0)
+    for k in range(3):
+        fill("Mm%d" % k, T.Mm[:, 64 * k + 9:64 * k + 63:9], -1.0)
+    fill("Mm9", T.Mm[:, 63:192:64], -2048.0)
+    for k, c in ((31, 97.0), (63, 97.0), (96, -4096.0)):
+        op("v", "ST", "ST%d" % k, V.memset, T.ST[:, k:7 * SEG:SEG], c)
+    ts("ST end", "ST95", T.ST[:, 95:7 * SEG:SEG], T.ST[:, 95:7 * SEG:SEG], col["end"], A.mult)
+    op("v", "Tin2", "Tpad", V.memset, T.Tin[:, 40:42, 6], 0.5)
 
     for t in range(3):
-        B0 = base(t)
-        b0 = B0 // 32
-        bp = (C - B0) // 32
-        P, Pn = "P%d" % t, "P%d" % (t + 1)
-        VO, VP, MO, MP = "VO%d" % t, "VP%d" % t, "MO%d" % t, "MP%d" % t
-        mo = T.MO[:, 32 * t:32 * t + 20]
-        if t == 0:
-            unpack(t, 0, "vsvs")
-            second(0, 2)
-            blend(t, 1, 2)
-        else:
-            relay(t)
-            blend(t, 1, 4)
-        blend(t, 0, 2)
-        for b, q, lo, hi in ((0, "s", 0, 20), (1, "s", 0, 20), (2, "v", 0, 20), (3, "s", 0, 10), (3, "v", 10, 20)):
-            w = T.Hh[:, 640 * b:640 * b + 640].indirect(T["PO%d" % t][:, lo:hi])
-            R, W = "H%d0 H%d1 PO%d" % (b, b, t), "Y%d%s" % (b, q)
-            out = T.Yt[:, 64 * lo + b:64 * hi:4]
-            if q == "s":
-                act(R, W, out, w, F.Copy, scale=0.5)
-            else:
-                ts(R, W, out, w, 0.5, A.mult)
-        quant("Y0s Y1s Y2v Y3s Y3v", "QY", T.Yt)
-        mm(5, "QB", 0, "QY")
-        mm(4, "QA", 0, "QY")
-        for b in range(4):
-            mm(b, "QW", b, "QY")
-        act("ps5", "SB", T.SB[:], ps(5), F.Copy)
-        act("CUv PZ0 PZ1 PZ2 PZ3 PZ4 PZ5 PZ6 PZ7", "PT", T.PT[:], T.PZ[:].indirect(T.CU[:, 16:21]), F.Copy)
-        if t == 0:
-            late_constants()
-        if t == 1:
-            quant("vin", "QV", T.vin)
-        tt("ps4 SB Ct", "Ct0", T.Ct[:, 0:1280:4], ps(4), T.SB[:], A.is_gt)
-        quant("Ct0", "QC", T.Ct)
-        mm(6, "QK", 0, "QC")
-        mm(7, "QK", 1, "QC")
-        for b in range(4):
-            act("ps%d" % b, "TB%d" % b, T.TB[:, C * b:C * b + C], ps(b), F.Relu, scale=0.03125)
-        if t == 0:
-            later_constants()
-        turn("ps6", "RT", T.RT[:], ps(6))
-        tt("RT CUt PT", "V80", T.V80[:], T.RT[:].indirect(T.CU[:, 44:49]), T.PT[:], A.add)
-        scan("V80 keep8", "SM", T.SM[:], T.keep8[:], T.V80[:], 0.0, A.mult, A.max)
-        cp("V80", VO + "v", T[VO][:, 0:80], T.V80[:])
-        top = T.SM[:, 7:80:8]
-        ts("SM", "a1", sm("a1"), top, -14336.0 - 256.0, A.add)
-        ts("SM", "a2", sm("a2"), top, 2.0, A.mult, -2 * 14336.0 - 768.0, A.add)
-        ts("SM", VO, T[VO][:, 80:90], top, -14336.0, A.add)
-        tt("a1 a2", "AZ", T.AZ[:, 0:C:32], sm("a1"), sm("a2"), A.max)
-        ts("SM", "sq", sm("sq"), top, 14336.0 + 640.0, A.is_ge, 640.0, A.mult)
-        scan("AZ keep32", "AB", T.AB[:], T.keep32[:], T.AZ[:], 0.0, A.mult, A.add)
-        send(t, "av%d" % t, VO + " " + VO + "v", VP, T[VP][:], T[VO][:])
-        turn("AB", "AR", T.AR[:], T.AB[:])
-        tt("sq y20", "SA", T.SA[:, 10:20], sm("sq"), T.y20[:, b0:b0 + 10], A.max)
-        for k in range(2, 5):
-            act("AR xcb", "D0_%d" % k, T.D0[:, BLK * k:BLK * k + C], T.AR[:], F.Abs, scale=BIG, bias=T.xc[:, 8 + k:9 + k])
-        for k in range(2):
-            ts("AR xc", "D0_%d" % k, T.D0[:, BLK * k:BLK * k + C], T.AR[:], T.xc[:, k:k + 1], A.not_equal, BIG, A.mult)
-        for k in range(5):
-            scan("D0_%d D0c one" % k, "SO%d" % k, T.SO[:, BLK * k:BLK * k + C + 1], T.D0[:, BLK * k:BLK * k + C + 1],
-                 T.one[:, 0:C + 1], 1024.0, A.min, A.subtract)
-        for h in range(2):
-            act("V80 Tin", "Tv%d1" % h, T.Tin[:, 2 * b0 + h:2 * b0 + 20:2, 0:8], T.V80[:], F.Copy)
-        so = "SO0 SO1 SO2 SO3 SO4 MQ"
-        for key, po, pi, c in (("MQa", (0, 128), (0, 128), 0), ("MQb", (64, 128), (0, 64), 5), ("MQc", (0, 64), (64, 128), 5)):
-            ts(so, key, T.MQ[po[0]:po[1], c:c + 5], T.SO[pi[0]:pi[1], C:5 * BLK:BLK], 160.0 + B0, A.add, 640.0, A.min)
-        for a in range(4):
-            cp("MQa MQb MQc", "MQ%d" % a, T.MQ[32 * (a ^ 1):32 * (a ^ 1) + 32, 10:20], T.MQ[32 * a:32 * a + 32, 0:10])
-        tt("MQa MQb MQc MQ0 MQ1 MQ2 MQ3 CUm SA", MO, T.MO[:, 32 * t:32 * t + 32], T.MQ[:].indirect(T.CU[:, 22:24]),
-           T.SA[:, 10 - b0:42 - b0], A.min)
-        send(t, "am%d" % t, MO, MP, T[MP][:], mo)
-        tt("ps7 diag", "RD", T.RD[:], ps(7), T.diag[:], A.mult)
-        if t == 0:
-            last_constants()
-        for b in range(4):
-            mm(4 + b, "QE", b, "QX%d" % t)
-        if t < 2:
-            for h in range(2):
-                for b in range(4):
-                    tt("TB%d ps%d" % (b, 4 + b), "X%d%d" % (b, h), T.Xt[:, 4 * H * h + b:4 * H * (h + 1):4],
-                       T.TB[:, C * b + H * h:C * b + H * h + H], T["ps%d" % (4 + b)][:, H * h:H * h + H], A.add)
-                send_half(t + 1, T.Xt, " ".join("X%d%d" % (b, h) for b in range(4)) + (" QX%dh" % (t + 1) if h else ""), h)
-            unpack(t + 1, 1, "ssss")
-            second(1, 4)
-            unpack(t + 1, 0, "ssss")
-            second(0, 2)
-        else:
+        u = upper(t)
+        B0, Bp, b0 = C * u, C - C * u, 10 * u
+        QF, G, B, PO, PP, VV, MP = ["%s%d" % (n, t) for n in ("QF", "G", "B", "PO", "PP", "VV", "MP")]
+        mo = T.MO[:, 20 * t:20 * t + 20]
+        win = "%s %sp %sh" % (QF, QF, QF)
+        for e in range(2):
+            pick(win + " " + PO, "Go%d" % e, G, 640 * e + B0, QF, 0, T[PO][:, 20 * e:20 * e + 20])
             for b in range(4):
-                tt("TB%d ps%d" % (b, 4 + b), "X%d0 X%d1" % (b, b), T.Xt[:, b:1280:4], T.TB[:, C * b:C * b + C], ps(4 + b), A.add)
-            quant("X00 X10 X20 X30", "QX3", T.Xt)
-            mm(0, "QV", 0, "QX3")
+                mm(b, "QE", 512 * e + 128 * b, G, 640 * e + B0, C, "QE%d%d Go%dc Go%ds" % (e, b, e, e), e == 0, False)
+        for e in range(2):
+            pick(win + " " + PP, "Gp%d" % e, G, 640 * e + Bp, QF, 0, T[PP][:, 20 * e:20 * e + 20])
+            pick("Go%dc Gp%dc %s" % (e, e, PO), "B%d" % e, B, C * e, G, 640 * e, T[PO][:, 20 * e:20 * e + 20], "v")
+            pick("Go%ds Gp%ds %s" % (e, e, PO), "B%d" % e, B, C * e, G, 640 * e, T[PO][:, 20 * e:20 * e + 20], "s")
+            for b in range(4):
+                mm(b, "QE", 512 * e + 128 * b, B, C * e, C, "B%dc B%ds" % (e, e), False, e == 1)
+        ts(PP + " PA", "PAp", T.PA[:, 40 - 40 * u:80 - 40 * u], T[PP][:], 1.0, A.add)
+        act("PN0 PN1", "S3p", T.S3[:, 2:120:3], T.PN[:, 2:120:3])
+        for b in range(4):
+            if b % 2:
+                act("ps%d QYpad" % b, "Y%d" % b, T.Yt[:, b:1280:4], ps(b), scale=0.5)
+            else:
+                op("v", "ps%d QYpad" % b, "Y%d" % b, V.tensor_scalar, T.Yt[:, b:1280:4], ps(b), 0.5, None, A.mult)
+        quant("Y0 Y1 Y2 Y3", "QY", "QY", 0, C, T.Yt[:, 0:1280])
+        for k in range(3):
+            mm(4 + k, "QY", 128 * k, "QAB", 0, 128, "QY QABc QABs")
+        for b in range(4):
+            mm(b, "QW", 128 * b, "QY", 0, C, "QW QW2 QY")
+        act("PAo PAp CUr", "VR", T.VR[:], T.PA[:].indirect(cu(CR)))
+        for k in range(3):
+            act("ps%d" % (4 + k), "SL%d" % k, T.SL[:, 64 * k:64 * k + 64], T["ps%d" % (4 + k)][:, 64:128])
+        if t == 1:
+            quant("vin", "QV", "QV", 0, 128, T.vin[:])
+        tt("C1 VR", "dd", T.dd[:], T.VR[:], T.C1[:], A.subtract)
+        for k in range(3):
+            tt("ps%d SL%d" % (4 + k, k), "D%d" % k, T.D[:, 64 * k:64 * k + 64], ps(4 + k, 64), T.SL[:, 64 * k:64 * k + 64], A.is_gt)
+        for e in range(2):
+            for b in range(4):
+                mm(4 + b, "QE", 512 * e + 128 * b, QF, B0, C, "QE%d%d %s %sh" % (e, b, QF, QF), e == 0, e == 1)
+        scan("D0 D1 D2 Mm Mm9 Mm0 Mm1 Mm2", "SC", T.SC[:], T.Mm[:], T.D[:], 0.0, A.mult, A.add)
+        for b in range(2):
+            act("ps%d" % b, "TB%d" % b, T.TB[:, C * b:C * b + C], ps(b), F.Relu, scale=0.03125)
+        vv = T[VV][:, 24 * u:24 * u + 24]
+        tt("SC PT", VV, vv, T.SC[:, 7:192:8], T.PT[:, 0:24], A.add)
+        send(t, "av%d" % t, VV, VV + "p", vv, vv)
+        scan(VV + " keep24", "SM", T.SM[:], T.keep24[:], vv, 0.0, A.mult, A.max)
+        top = T.SM[:, 7:24:8]
+        for k in range(3):
+            ts("SM Ypad", "AB%d" % k, T.AB[:, 32 * k:32 * k + 32], T.Yt[:, 1280:1312], T.SM[:, 8 * k + 7:8 * k + 8], A.add)
+        turn("AB0 AB1 AB2", "AR", T.AR[:], T.AB[:])
+        tt("SM CK", "sk0", T.sk[:, 0:3], top, T.CK[:, 3 * u:3 * u + 3], A.add)
+        ts("SM", "sk1", T.sk[:, 4:7], top, LAST, A.is_le, NONE, A.mult)
+        for j in range(ON_V, 20):
+            act("AR xcb", "D0_%d" % j, T.D0[:, SEG * j:SEG * j + 96], T.AR[:], F.Abs, scale=BIG, bias=T.xcb[:, j:j + 1])
+        for j in range(ON_V):
+            ts("AR xc", "D0_%d" % j, T.D0[:, SEG * j:SEG * j + 96], T.AR[:], T.xc[:, j:j + 1], A.not_equal, BIG, A.mult)
+        tt("sk0 sk1 SK", "SKs", T.SK[:, 16:25:4], T.sk[:, 0:3], T.sk[:, 4:7], A.max)
+        for lo, hi in SCANS:
+            scan(" ".join("D0_%d" % j for j in range(lo, hi)) + " D0r ST31 ST63 ST95 ST96", "SO%d" % lo, T.SO[:, SEG * lo:SEG * hi],
+                 T.D0[:, SEG * lo:SEG * hi], T.ST[:, 0:SEG * (hi - lo)], 4096.0, A.min, A.subtract)
+        ts(" ".join("SO%d" % lo for lo, hi in SCANS) + " KK", "KKs", T.KK[:, 10:30], T.SO[:, 95:20 * SEG:SEG], 160.0 + B0, A.add,
+           1025.0, A.mult)
+        tt("KKs SKs CUs", "M0", T.M0[:, b0:b0 + 32], T.SK[:].indirect(cu(CS)), T.KK[:, b0:b0 + 32], A.min)
+        tt("M0", "M1", T.M1[0:64, :], T.M0[0:64, 10:30], T.M0[64:128, 10:30], A.min)
+        for a in range(4):
+            tt("M1", "MO%d" % a, T.MO[32 * a:32 * a + 32, 20 * t:20 * t + 20], T.M1[0:32, :], T.M1[32:64, :], A.min)
+        send(t, "am%d" % t, "MO0 MO1 MO2 MO3", MP, T[MP][:], mo)
+        order("s", [VV + "p"], [])
+        k = spread(VV, T[VV], 48, 48)
+        act(k + " CUv", "va", T.va[:], T[VV][:].indirect(cu(CV)), F.Abs, bias=-11263.5)
+        act(k + " CUv", "vh", T.vh[:], T[VV][:].indirect(cu(CV)))
+        for b in range(2, 4):
+            act("ps%d" % b, "TB%d" % b, T.TB[:, C * b:C * b + C], ps(b), F.Relu, scale=0.03125)
+
+        def state(b):
+            tt("TB%d ps%d" % (b, 4 + b), "X%d" % b, T.Xt[:, b:1280:4], T.TB[:, C * b:C * b + C], ps(4 + b), A.add)
+        state(0)
+        state(1)
+        ts("va", "vv", T.vv[:], T.va[:], 3072.0, A.is_ge)
+        ts("vh", "vh", T.vh[:], T.vh[:], LAST, A.is_ge)
+        tt("vv CZ ZY", "ZYs", T.ZY[:, 0:48], T.vv[:], T.CZ[:], A.mult)
+        tt("vh dd", "VFr", T.VF[:, 0:96:2], T.vh[:], T.dd[:], A.mult)
+        turn("ZYs", "T1", T.T1[:], T.ZY[:, 24 * u:24 * u + 32])
+        tt("VR VFr", "VFg", T.VF[:, 1:96:2], T.VR[:], T.VF[:, 0:96:2], A.subtract)
+        for h in range(2):
+            act("T1", "Z3%d" % h, T.Z3[:, h:4:2, :], T.T1[:])
+        for w in range(2):
+            for h in range(2):
+                act("VFr VFg Tin Tin2", "Ta%d%d" % (w, h), T.Tin[:, 20 * w + h:20 * w + 20:2, 0:4], T.VF[:, 48 * w:48 * w + 40])
+                act("ZYs Tin Tin2", "Tb%d%d" % (w, h), T.Tin[:, 20 * w + h:20 * w + 20:2, 4:6], T.ZY[:, 24 * w:24 * w + 20])
+        state(2)
+        state(3)
+        if t < 2:
+            n = C * upper(t + 1)
+            quant("X0 X1 X2 X3", "QF%d" % (t + 1), "QF%d" % (t + 1), n, n + C, T.Xt[:])
+            send_state(t + 1, 0, C, "QF%d" % (t + 1))
+        else:
+            quant("X0 X1 X2 X3", "QX3", "QX3", 0, C, T.Xt[:])
+            mm(0, "QV", 0, "QX3", 0, C, "QV QX3")
             dma("y", "out", "QX3", "", T.oc[:], T.QX3[:].bitcast(dt.uint8))
             for k in range(4):
                 dma("y", "out", "QX3", "", T.osc[4 * k:4 * k + 4, :], T.SQX3[32 * k:32 * k + 4, :])
-            act("ps0", "ys", T.ys[:], ps(0), F.Copy)
+            act("ps0", "ys", T.ys[:], ps(0))
             dma("y", "out", "ys", "", T.y[:], T.ys[:])
-        scan("RD keep16", "RS", T.RS[:], T.keep16[:], T.RD[:], 0.0, A.mult, A.add)
-        ts(VO, "A20a", T.A20[:, b0:b0 + 10], T[VO][:, 80:90], 0.25, A.add)
-        ts("RS CFm", "k1", sm("k1"), T.RS[:, 15:C:16], GM5, A.add)
-        ts(VP, "A20b", T.A20[:, bp:bp + 10], T[VP][:, 80:90], 0.25, A.add)
-        tt("k1", "k2", sm("k2"), sm("k1"), sm("k1"), A.mult)
-        tt("A20a A20b y20", "Dy", sm("Dy"), T.A20[:], T.y20[:], A.subtract)
-        tt(MO + " " + MP, "low", sm("low"), mo, T[MP][:], A.min)
-        cp(VP + " Tin", "Tv00", T.Tin[:, 2 * bp:2 * bp + 20:2, 0:8], T[VP][:, 0:80])
-        tt("low y20", "ee", sm("ee"), sm("low"), T.y20[:], A.is_equal)
-        cp(VP + " Tin", "Tv10", T.Tin[:, 2 * bp + 1:2 * bp + 20:2, 0:8], T[VP][:, 0:80])
-        tt("ee Dy", "zz", sm("zz"), sm("ee"), sm("Dy"), A.mult)
-        ts("k2", "k1", sm("k1"), sm("k2"), 2.0, A.is_lt, -4096.0, A.mult)
+        turn("Z30 Z31", "ZT", T.ZT[:], T.Z3[:])
         for h in range(2):
-            tt("zz low Tin", "Tu%d" % h, T.Tin[:, h:40:2, 8], sm("zz"), sm("low"), A.add)
-        turn("Tu0 Tu1 Tv00 Tv01 Tv10 Tv11 Ty0 Ty1", "Tout", T.Tout[:], T.Tin[:])
-        cp("Tu0 Tu1", "OFF", T.OFF[:], T.Tin[:, 2 * b0:2 * b0 + 20, 8])
-        tt("k1 XW", "xk", sm("xk"), sm("k1"), T.XW[:, 2 * b0:2 * b0 + 20], A.add)
+            act("ZT", "ZO%d" % h, T.ZO[:, h:20:2, :], T.ZT[:, 32 * h:32 * h + 20])
+        for h in range(2):
+            tt("MO0 MO1 MO2 MO3 Tin Tin2 " + MP, "Tk%d" % h, T.Tin[:, h:40:2, 6], mo, T[MP][:], A.min)
+        cp("Tk0 Tk1", "I1", T.I1[:], T.Tin[:, 2 * b0:2 * b0 + 20, 6])
+        turn("Tk0 Tk1 Tpad Ta00 Ta01 Ta10 Ta11 Tb00 Tb01 Tb10 Tb11", "Tout", T.Tout[:], T.Tin[:])
+        ts("I1", "I2", T.I2[:], T.I1[:], 1023, band)
+        cp("I2", "OFF", T.OFF[:], T.I2[:])
         cp("Tout OFF", "GG", T.GG[:], T.Tout[:].indirect(T.OFF[:]))
         turn("GG", "ZZ", T.ZZ[:], T.GG[:])
-        cp("ZZ CUz", "Gi", T.Gi[:], T.ZZ[:].indirect(T.CU[:, 24:27]))
-        tt("ZZ XQ", "s2", sm("s2"), T.ZZ[:, 8:C:16], T.XQ[:, 2 * b0:2 * b0 + 20], A.is_equal)
-        ts("Gi", "c1", sm("c1"), T.Gi[:, 0:20], 8192.0, A.is_lt)
-        ts("Gi", "PtT", T.PtT[:], T.Gi[:], 1023, band)
-        tt("ZZ xk", "s1", sm("s1"), T.ZZ[:, 8:C:16], sm("xk"), A.is_equal)
-        tt("c1 s2", "c1", sm("c1"), sm("c1"), sm("s2"), A.mult)
-        ts("Gi", "c2", sm("c2"), T.Gi[:, 0:20], 14336.0, A.is_ge)
-        tt("PtT %s %sb" % (P, P), "DD", T.DD[:], T.PtT[:, 0:40], T[P][:], A.subtract)
-        tt("c1 s1", "QQa", T.QQ[:, 0:20], sm("c1"), sm("s1"), A.add)
-        tt("c2 s2", "QQb", T.QQ[:, 20:40], sm("c2"), sm("s2"), A.mult)
-        tt("QQa QQb DD", "MB", T.MB[:], T.QQ[:], T.DD[:], A.mult)
-        tt("MB", "n1", sm("n1"), T.MB[:, 0:20], T.MB[:, 20:40], A.add)
-        tt("n1 " + P, Pn, T[Pn][:, 0:20], sm("n1"), T[P][:, 0:20], A.add)
+        for e in range(2):
+            tt("ZZ Y16", "W2%d" % e, T.W2[:, :, e], T.ZZ[:, :, 6], T.Y16[:, 2 * b0:2 * b0 + 20], A.subtract)
+        cp("ZZ", "S30", T.S3[:, 0:120:3], T.ZZ[:, :, 0:4:2])
+        tt("W20 W21 ZO0 ZO1", "Q31", T.Q3[:, 1:120:3], T.W2[:], T.ZO[:], A.is_equal)
+        tt("W20 W21 ZZ", "q2", T.q2[:], T.W2[:], T.ZZ[:, :, 4:6], A.is_equal)
+        tt("ZZ PN0 PN1", "S31", T.S3[:, 1:120:3], T.ZZ[:, :, 1:4:2], T.PN[:, 2:120:3], A.subtract)
+        tt("Q31 q2", "Q32", T.Q3[:, 2:120:3], T.Q3[:, 1:120:3], T.q2[:], A.add)
+        scan("S30 S31 S3p Q30 Q31 Q32", "PN0 PN1", T.PN[:], T.Q3[:], T.S3[:], 0.0, A.mult, A.add)
         if t < 2:
             o = "PO%d" % (t + 1)
-            cp(Pn, o, T[o][:], T[Pn][:, 0:20])
+            for e in range(2):
+                ts("PN0", o + "ab"[e], T[o][:, 20 * e:20 * e + 20], T.PN[:, 3 * e + 2:120:6], -1.0, A.add)
+            wrote[o] = wrote[o + "b"]
             send(t + 1, "ap%d" % (t + 1), o, "PP%d" % (t + 1), T["PP%d" % (t + 1)][:], T[o][:])
+            pointers(t + 1)
         else:
-            turn("P3 P3z", "OT", T.OT[:], T.P3[:, 0:32])
+            for e in range(2):
+                ts("PN0 OI", "OI%d" % e, T.OI[:, 32 * e:32 * e + 20], T.PN[:, 3 * e + 2:120:6], -1.0, A.add)
+            turn("OI0 OI1", "OT", T.OT[:], T.OI[:])
             for k in range(8):
-                dma("ys"[k % 2], "out2", "OT", "", T.ov[k, :], T.OT[32 * (k // 2):32 * (k // 2) + 20, 16 * (k % 2):16 * (k % 2) + 16])
+                dma("ys"[k % 2], "out2", "OT", "", T.ov[k, :], T.OT[32 * (k // 2):32 * (k // 2) + 20, 32 * (k % 2):32 * (k % 2) + 16])
 
     for s, n in count.items():
         if seen.get(s, 0) < n:

@@ -8,7 +8,10 @@ BIG = 16384.0
 LAST = 14336.0
 NONE = 1048576.0 + 640.0
 ON_V = 6
-SCANS = ((0, 6), (6, 13), (13, 18), (18, 20))
+SCANS = ((6, 10), (0, 6), (10, 17), (17, 20))
+COPY = ("vsvs", "svsv")
+EARLY = 3
+XAT = (0, 2, 2, 2)
 
 SCRATCH = {}
 
@@ -20,22 +23,22 @@ def _buf(name, n, dtype, where="sbuf"):
 for _k in range(8):
     _buf("ps%d" % _k, 512, "float32", "psum")
 for _n, _w in (("xin", 1280), ("uin", 512), ("vin", 512), ("Xt", 1280), ("Yt", 1536), ("Z", 1040), ("D0", 20 * SEG), ("SO", 20 * SEG),
-               ("ST", 7 * SEG), ("keep24", 24), ("D", 192), ("Mm", 192), ("SC", 192)):
+               ("ST", 7 * SEG), ("D", 192), ("Mm", 192), ("SC", 192)):
     _buf(_n, _w, "bfloat16")
 for _n, _w in (("QF0", 640), ("QF1", 640), ("QF2", 640), ("G0", 1280), ("G1", 1280), ("G2", 1280), ("B0", 640), ("B1", 640), ("B2", 640),
                ("QX3", C), ("QY", 384), ("QE", 1024), ("QW", 512), ("QU", 128), ("QAB", 128), ("QV", 128)):
     _buf(_n, _w, CODE)
     _buf("S" + _n, _w, "uint8")
-for _n, _w in (("TB", 1280), ("SL", 192), ("PT", 32), ("VR", 48), ("SM", 24), ("AB", 96), ("AR", 96), ("KK", 42),
-               ("M0", 42), ("M1", 20), ("SK", 48), ("sk", 8), ("MO", 60), ("MP0", 20), ("MP1", 20), ("MP2", 20),
-               ("VV0", 192), ("VV1", 192), ("VV2", 192), ("Tin", [42, 16]), ("Tout", 672), ("GG", C), ("ZZ", [20, 16]),
-               ("VF", 96), ("ZY", 64), ("va", 48), ("vh", 48), ("vv", 48), ("dd", 48), ("T1", 32), ("Z3", [4, 16]), ("ZT", 64),
-               ("ZO", [20, 2]), ("W2", [20, 2]), ("q2", 40), ("Q3", 120), ("S3", 120), ("PN", 120),
+for _n, _w in (("TB", 1280), ("SL", 192), ("PT", 32), ("VR", 48), ("VW", [3, 40]), ("SW", [3, 40]), ("AR", 96), ("KK", 20),
+               ("M1", 20), ("SK", 32), ("sk", 8), ("MO", 60), ("MQ", 20), ("MP0", 20), ("MP1", 20), ("MP2", 20),
+               ("VV0", 224), ("VV1", 224), ("VV2", 224), ("Tin", [42, 16]), ("Tout", 672), ("GG", C), ("ZZ", [20, 16]),
+               ("VF", 168), ("va", 48), ("vh", 48), ("vv", 48), ("dd", 48), ("T1", 32), ("Z3", [4, 16]), ("ZT", 64),
+               ("ZO", [20, 2]), ("q2", 40), ("Q3", 120), ("S3", 120), ("PN", 120),
                ("ne", 40), ("PZ", 256), ("PA", 96), ("OI", 64), ("OT", 64), ("ys", C),
-               ("idm", 128), ("CF", 26), ("NI", 8), ("NJ", 8), ("t8", 8), ("CL", 24), ("l1", 8), ("xc", 20), ("xcb", 20),
-               ("YJ", 80), ("Y16", 40), ("C1", 48), ("CZ", 48), ("CK", 6)):
+               ("idm", 128), ("CF", 32), ("NI", 8), ("NJ", 8), ("t8", 8), ("CL", 24), ("l1", 8), ("xc", 20), ("xcb", 20),
+               ("YJ", 80), ("YR", 640), ("C1", 48), ("CZ", 48), ("CK", 6)):
     _buf(_n, _w, "float32")
-for _n, _w in (("Vi", 60), ("PI", 2), ("CI", 16), ("I1", 20), ("I2", 20)):
+for _n, _w in (("Vi", 60), ("PI", 2), ("CI", 16), ("I1", 10), ("I2", 10)):
     _buf(_n, _w, "int32")
 for _n, _w in (("CU", 24), ("CP", 4), ("OFF", 20), ("PO0", 48), ("PO1", 40), ("PO2", 40), ("PP0", 40), ("PP1", 40), ("PP2", 40)):
     _buf(_n, _w, "uint16")
@@ -131,14 +134,17 @@ def rank_program(g, core, T, topo):
     def turn(R, W, out, a):
         op("v", R, W, V.transpose, out, a)
 
-    def fill(W, ap, c):
-        op("v", "", W, V.memset, ap, c)
+    def fill(W, ap, c, R=""):
+        op("v", R, W, V.memset, ap, c)
 
     def act(R, W, out, a, f=F.Copy, **kw):
         op("s", R, W, S.activation, out, a, f, **kw)
 
+    def aff(R, W, out, a, scale, bias):
+        act(R, W, out, a, F.Identity, scale=scale, bias=bias)
+
     def sfill(W, ap, n, c):
-        act("xin0", W, ap, T.xin[:, 0:n], F.Identity, scale=0.0, bias=c)
+        aff("xin0", W, ap, T.xin[:, 0:n], 0.0, c)
 
     def quant(R, W, name, lo, hi, tile):
         op("v", R, W, V.quantize_mx, T[name][:, lo:hi], T["S" + name][:, lo:hi], tile)
@@ -153,31 +159,36 @@ def rank_program(g, core, T, topo):
     def ps(k, n=C):
         return T["ps%d" % k][:, 0:n]
 
+    def keys(form, *ranges):
+        out = [()]
+        for n in ranges:
+            out = [o + (i,) for o in out for i in (range(n) if isinstance(n, int) else n)]
+        return " ".join(form % o for o in out)
+
     def upper(t):
         return int(r > (r ^ STEP[t]))
 
     def words(ap):
         return ap.bitcast(dt.uint32)
 
-    def pick(R, W, dst, at, src, lo, off, q="vs"):
+    def pick(R, W, dst, at, src, lo, off):
         n = 16 * off.shape[1]
-        if "v" in q:
-            cp(R, W + "c", words(T[dst][:, at:at + n]), words(T[src][:, lo:lo + 640]).indirect(off))
-        if "s" in q:
-            act(R, W + "s", T["S" + dst][:, at:at + n], T["S" + src][:, lo:lo + 640].indirect(off))
+        cp(R.replace("#", "c"), W + "c", words(T[dst][:, at:at + n]), words(T[src][:, lo:lo + 640]).indirect(off))
+        act(R.replace("#", "s"), W + "s", T["S" + dst][:, at:at + n], T["S" + src][:, lo:lo + 640].indirect(off))
 
-    def spread(key, buf, n, pitch):
-        act(key, key + "a", buf[0:64, pitch:pitch + n], buf[64:128, 0:n])
-        act(key, key + "b", buf[64:128, pitch:pitch + n], buf[0:64, 0:n])
+    def spread1(R, key, buf, n, pitch):
+        act(R, key + "a", buf[0:64, pitch:pitch + n], buf[64:128, 0:n])
+        act(R, key + "b", buf[64:128, pitch:pitch + n], buf[0:64, 0:n])
+
+    def spread2(key, buf, n, pitch):
         for a in range(4):
-            act("%s %sa %sb" % (key, key, key), "%s_%d" % (key, a), buf[32 * (a ^ 1):32 * (a ^ 1) + 32, 2 * pitch:3 * pitch + n],
+            act("%sa %sb" % (key, key), "%s_%d" % (key, a), buf[32 * (a ^ 1):32 * (a ^ 1) + 32, 2 * pitch:3 * pitch + n],
                 buf[32 * a:32 * a + 32, 0:pitch + n])
-        return " ".join("%s_%d" % (key, a) for a in range(4))
 
     shr, band = A.logical_shift_right, A.bitwise_and
     DIGITS = (("h16", 0, 16), ("i", 0, 15), ("i8", 0, 8), ("k7", 0, 7), ("r32", 0, 96), ("e", 0, 1), ("m", 0, 31), ("p112", 0, 112),
-              ("k0", 1, 1), ("r0", 5, 1), ("k1", 2, 1), ("r1", 6, 1), ("k8", 0, 7))
-    MORE = ("lowh", "h", "even", "x0", "sg", "dR", "dT", "dV", "dS", "end", "g0", "g1")
+              ("k0", 1, 1), ("r0", 5, 1), ("k1", 2, 1), ("r1", 6, 1), ("k8", 0, 7), ("q4", 2, 3))
+    MORE = ("lowh", "h", "even", "x0", "sg", "x1", "sh", "dR", "dT", "dV", "dS", "end", "g0", "g1", "m6", "hm")
     col = {n: T.CF[:, k:k + 1] for k, n in enumerate([d[0] for d in DIGITS] + list(MORE))}
     CAB, CR, CT, CV, CS = (0, 8), (8, 11), (12, 14), (14, 17), (18, 20)
 
@@ -207,242 +218,268 @@ def rank_program(g, core, T, topo):
     fill("Z", T.Z[:], 0.0)
     for k, (n, sh, m) in enumerate(DIGITS):
         ts("PI", "CI%d" % k, T.CI[:, k:k + 1], T.PI[:, 1:2] if n == "k8" else T.PI[:, 0:1], sh, shr, m, band)
-    cp(" ".join("CI%d" % k for k in range(13)), "CF h16 i", T.CF[:, 0:13], T.CI[:, 0:13])
+    cp(keys("CI%d", 14), "CF", T.CF[:, 0:14], T.CI[:, 0:14])
     fill("Ypad", T.Yt[:, 1024:1536], 0.0)
-    ts("NI i", "NJ", T.NJ[:], T.NI[:], col["i"], A.add)
-    ts("h16", "lowh", col["lowh"], col["h16"], -1.25, A.mult, 20.0, A.add)
+    ts("NI CF", "NJ", T.NJ[:], T.NI[:], col["i"], A.add)
+    ts("CF", "lowh", col["lowh"], col["h16"], -1.25, A.mult, 20.0, A.add)
+    ts("CF", "h", col["h"], col["h16"], 0.0625, A.mult)
+    ts("CF", "even", col["even"], col["h16"], 0.0, A.is_equal)
     at0 = C * upper(0)
     quant("xin0", "QF0h", "QF0", at0, at0 + H, T.xin[:, 0:4 * H])
     send_state(0, 0, H, "QF0h")
-    ts("h16", "h", col["h"], col["h16"], 0.0625, A.mult)
-    ts("h16", "even", col["even"], col["h16"], 0.0, A.is_equal)
     ts("NJ lowh", "CP", T.CP[:, 0:3], T.NJ[:, 0:3], 39.0, A.min, col["lowh"], A.add)
-    quant("xin1", "QF0", "QF0", at0 + H, at0 + C, T.xin[:, 4 * H:4 * C])
-    send_state(0, H, C, "QF0 QF0h")
-    cp("Vi Vi1 Vi2 CP", "PO0", T.PO0[:], T.Vi[:].indirect(T.CP[:, 0:3]))
-    send(0, "ap0", "PO0", "PP0", T.PP0[:], T.PO0[:, 0:40])
-    dma("y", "lw", "QF0p", "QW", T.QW[:].bitcast(dt.uint8), T.wc[:])
-    dma("y", "lw", "", "QW2", T.SQW[:], T.ws[:])
-    dma("y", "lv", "", "vin", T.vin[:], T.v[:])
-
     for par in range(2):
         ts("idm Z h even", "Z%d" % par, T.Z[:, 520 * par + 3:520 * par + 515:4], T.idm[:], 0.0, A.is_equal,
            col["h" if par else "even"], A.mult)
+    quant("xin1", "QF0", "QF0", at0 + H, at0 + C, T.xin[:, 4 * H:4 * C])
+    send_state(0, H, C, "QF0 QF0h")
     quant("Ypad", "QYpad", "QY", 256, 384, T.Yt[:, 1024:1536])
     for par in range(2):
         for b in range(4):
             at = 512 * par + 128 * b
             quant("Z%d" % par, "QE%d%d" % (par, b), "QE", at, at + 128, T.Z[:, 520 * par + 3 - b:520 * par + 515 - b])
+        if par == 0:
+            cp("Vi Vi1 Vi2 CP", "PO0a PO0b", T.PO0[:], T.Vi[:].indirect(T.CP[:, 0:3]))
+            send(0, "ap0", "PO0a", "PP0", T.PP0[:], T.PO0[:, 0:40])
+    dma("y", "lw", "QF0p", "QW", T.QW[:].bitcast(dt.uint8), T.wc[:])
+    dma("y", "lw", "", "QW2", T.SQW[:], T.ws[:])
+    dma("y", "lv", "", "vin", T.vin[:], T.v[:])
 
-    iota("xc", T.xc[:], [[32, 20]], 0, int(LAST) + 1)
     iota("YJ", T.YJ[:], [[16, 40], [0, 2]], 0, 1)
+    iota("xc", T.xc[:], [[32, 20]], 0, int(LAST) + 1)
     iota("C1", T.C1[:], [[C, 2], [32, 12], [0, 2]], 0, 1)
     iota("CK", T.CK[:], [[C, 2], [128, 3]], 1)
     iota("ST", T.ST[:], [[0, 7 * SEG]], 0, 1)
-    sfill("SK", T.SK[:], 48, NONE)
-    sfill("KK", T.KK[:], 42, NONE)
-    sfill("ZY", T.ZY[:], 64, 0.0)
+    iota("YR", T.YR[:], [[32, 20], [0, 2], [1, 16]], 0, -4096)
+    aff("h CF", "dR", col["dR"], col["e"], 19.0, col["h"])
+    aff("CF", "dT", col["dT"], col["p112"], 0.125, col["e"])
+    aff("CF", "dV", col["dV"], col["r32"], 0.0625, col["e"])
+    aff("CF", "end", col["end"], col["r32"], -1.0, -127.0)
+    for e in range(2):
+        aff("CF", "g%d" % e, col["g%d" % e], col["r32"], 128.0, 2048.0 * e)
+    sfill("VF", T.VF[:], 168, 0.0)
     sfill("OI", T.OI[:], 64, 0.0)
-    sfill("Tin", T.Tin[:, 0:21, :], 336, -1.0)
-    sfill("Tin2", T.Tin[:, 21:42, :], 336, -1.0)
+    sfill("VW", T.VW[:], 120, 0.0)
+    sfill("sk", T.sk[:], 8, 0.0)
     sfill("PA", T.PA[:], 96, 0.0)
     sfill("PZ", T.PZ[:], 256, 0.0)
-    act("h CF", "dR", col["dR"], col["e"], F.Identity, scale=19.0, bias=col["h"])
-    act("CF", "dT", col["dT"], col["p112"], F.Identity, scale=0.125, bias=col["e"])
-    act("CF", "dV", col["dV"], col["r32"], F.Identity, scale=0.0625, bias=col["e"])
-    act("CF", "dS", col["dS"], col["r32"], F.Identity, scale=-0.03125, bias=6.0)
-    act("CF", "end", col["end"], col["r32"], F.Identity, scale=-1.0, bias=-127.0)
-    for e in range(2):
-        act("CF", "g%d" % e, col["g%d" % e], col["r32"], F.Identity, scale=128.0, bias=2048.0 * e)
+    sfill("Tin", T.Tin[:, 0:21, :], 336, -1.0)
+    sfill("Tin2", T.Tin[:, 21:42, :], 336, -1.0)
     ts("CF", "x0", col["x0"], col["k0"], col["r0"], A.not_equal, 2.0, A.mult)
+    ts("CF", "x1", col["x1"], col["e"], col["r0"], A.not_equal, 2.0, A.mult)
     ts("NI CF", "t8", T.t8[:], T.NI[:], col["i8"], A.add, 0.125, A.mult)
-    ts("CF x0", "sg", col["sg"], col["k1"], col["r1"], A.not_equal, col["x0"], A.add)
     ts("NJ", "l1", T.l1[:, 0:3], T.NJ[:, 0:3], 24.0, A.is_ge, 16.0, A.mult)
-    ts("t8 CF", "CLa", T.CL[:, 0:4], T.t8[:, 0:4], col["k8"], A.max, 16.0, A.mult)
-    ts("t8 CF", "CLb", T.CL[:, 4:8], T.t8[:, 0:4], col["k7"], A.min, 16.0, A.mult)
-    act("sg dT", "dT", col["dT"], col["sg"], F.Identity, scale=64.0, bias=col["dT"])
-    act("sg dV", "dV", col["dV"], col["sg"], F.Identity, scale=48.0, bias=col["dV"])
-    act("NJ dS", "CLs", cl(CS), T.NJ[:, 0:2], F.Identity, bias=col["dS"])
-    act("t8 dT", "CLt", cl(CT), T.t8[:, 0:2], F.Identity, scale=16.0, bias=col["dT"])
-    act("t8 dV", "CLv", cl(CV), T.t8[:, 0:3], F.Identity, scale=8.0, bias=col["dV"])
-    act("l1 dR", "l1", T.l1[:, 0:3], T.l1[:, 0:3], F.Identity, bias=col["dR"])
+    ts("CF", "m6", col["m6"], col["i"], 6.0, A.is_equal)
+    ts("CF x0", "sg", col["sg"], col["k1"], col["r1"], A.not_equal, col["x0"], A.add)
+    ts("CF x1", "sh", col["sh"], col["k0"], col["r1"], A.not_equal, col["x1"], A.add)
+    ts("t8 CF", "CAa", T.CU[:, 0:4], T.t8[:, 0:4], col["k8"], A.max, 16.0, A.mult)
+    ts("t8 CF", "CAb", T.CU[:, 4:8], T.t8[:, 0:4], col["k7"], A.min, 16.0, A.mult)
+    ts("CF m6", "hm", col["hm"], col["h16"], col["m6"], A.mult)
+    aff("sg dT", "dT", col["dT"], col["sg"], 64.0, col["dT"])
+    aff("sg dV", "dV", col["dV"], col["sg"], 56.0, col["dV"])
+    aff("sh CF", "dS", col["dS"], col["sh"], 56.0, col["q4"])
+    aff("l1 dR", "l1r", T.CL[:, 20:23], T.l1[:, 0:3], 1.0, col["dR"])
+    aff("t8 dV", "l1v", T.l1[:, 4:7], T.t8[:, 0:3], 8.0, col["dV"])
     quant("uin", "QU", "QU", 0, 128, T.uin[:])
-    cp("CLa CLb", "CAB", cu(CAB), cl(CAB))
-    tt("l1 NJ", "CLr", cl(CR), T.l1[:, 0:3], T.NJ[:, 0:3], A.add)
-    cp("QU CAB", "QABc", words(T.QAB[:]), words(T.QU[:]).indirect(cu(CAB)))
-    act("QU CAB", "QABs", T.SQAB[:], T.SQU[:].indirect(cu(CAB)))
-    for c, k in ((CR, "CLr"), (CT, "CLt"), (CV, "CLv"), (CS, "CLs")):
-        cp(k, "CU" + k[2], cu(c), cl(c))
-    ts("YJ i", "YJ", T.YJ[:], T.YJ[:], col["i"], A.add)
+    ts("YJ CF", "YJ", T.YJ[:], T.YJ[:], col["i"], A.add)
     for e in range(2):
-        ts("PO0", "PN%d" % e, T.PN[:, 3 * e + 2:120:6], T.PO0[:, 20 * e:20 * e + 20], 1.0, A.add)
-
-    def pointers(t):
-        u = upper(t)
-        pn = T.PN[:, 2:120:3]
-        tt("PN0 PN1 YJ", "ne", T.ne[:], pn, T.YJ[:, 40 * u:40 * u + 40], A.not_equal)
-        ts("PO%d PA" % t, "PAo", T.PA[:, 40 * u:40 * u + 40], T["PO%d" % t][:, 0:40], 1.0, A.add)
-        tt("ne PN0 PN1", "PZ", T.PZ[:, 0:40], T.ne[:], pn, A.mult)
-        for e in range(2):
-            act("PZ g%d" % e, "PZ", T.PZ[:, e:40:2], T.PZ[:, e:40:2], F.Identity, bias=col["g%d" % e])
-        k = spread("PZ", T.PZ, 40, 64)
-        act(k + " CUt", "PT", T.PT[:], T.PZ[:].indirect(cu(CT)))
-
-    pointers(0)
-    act("C1 CF", "C1", T.C1[:], T.C1[:], F.Identity, bias=col["m"])
-    act("xc CF", "xc", T.xc[:], T.xc[:], F.Identity, bias=col["m"])
-    act("C1", "CZ", T.CZ[:], T.C1[:], F.Identity, scale=1024.0, bias=3072.0)
-    act("xc", "xcb", T.xcb[:], T.xc[:], scale=-BIG)
-    act("CK", "CK", T.CK[:], T.CK[:], F.Identity, scale=1024.0, bias=-LAST - 1.0)
-    act("YJ", "Y16", T.Y16[:], T.YJ[:, 0:80:2], F.Identity, bias=-4097.0)
+        ts("PO0a", "PN", T.PN[:, 3 * e + 2:120:6], T.PO0[:, 20 * e:20 * e + 20], 1.0, A.add)
+    cp("QU CAa CAb", "QABc", words(T.QAB[:]), words(T.QU[:]).indirect(cu(CAB)))
+    act("QU CAa CAb", "QABs", T.SQAB[:], T.SQU[:].indirect(cu(CAB)))
+    ts("t8 dT", "CUt", cu(CT), T.t8[:, 0:2], 16.0, A.mult, col["dT"], A.add)
+    ts("l1", "l1q", T.CL[:, 0:3], T.l1[:, 0:3], 0.25, A.mult)
+    ts("NI dS", "l1s", T.CL[:, 4:6], T.NI[:, 0:2], 1.75, A.mult, col["dS"], A.add)
+    tt("l1r NJ", "CLr", cl(CR), T.CL[:, 20:23], T.NJ[:, 0:3], A.add)
+    tt("l1q l1v", "CLv", cl(CV), T.CL[:, 0:3], T.l1[:, 4:7], A.add)
+    ts("l1s", "CUs", cu(CS), T.CL[:, 4:6], 24.0, A.add)
     fill("Mm", T.Mm[:], 1.0)
-    fill("keep24", T.keep24[:], 1.0)
+    cp("CLr", "CUr", cu(CR), cl(CR))
+    cp("CLv", "CUv", cu(CV), cl(CV))
     fill("Q30", T.Q3[:, 0:120:3], 0.0)
     fill("D0r", T.D0[:, SEG - 1:20 * SEG:SEG], BIG)
-    fill("Mm", T.Mm[:, 0:192:8], 0.0)
-    fill("keep24", T.keep24[:, 0:24:8], 0.0)
-    fill("Mm9", T.Mm[:, 7:192:8], 2048.0)
+    fill("Mma", T.Mm[:, 0:192:8], 0.0, "Mm")
+    fill("Mmb", T.Mm[:, 7:192:8], 2048.0, "Mm")
     for k in range(3):
-        fill("Mm%d" % k, T.Mm[:, 64 * k + 9:64 * k + 63:9], -1.0)
-    fill("Mm9", T.Mm[:, 63:192:64], -2048.0)
-    for k, c in ((31, 97.0), (63, 97.0), (96, -4096.0)):
-        op("v", "ST", "ST%d" % k, V.memset, T.ST[:, k:7 * SEG:SEG], c)
-    ts("ST end", "ST95", T.ST[:, 95:7 * SEG:SEG], T.ST[:, 95:7 * SEG:SEG], col["end"], A.mult)
-    op("v", "Tin2", "Tpad", V.memset, T.Tin[:, 40:42, 6], 0.5)
+        fill("Mm%d" % k, T.Mm[:, 64 * k + 9:64 * k + 63:9], -1.0, "Mm")
+    fill("Tpad", T.Tin[:, 40:42, 6], 0.5, "Tin2")
+    fill("Mmb", T.Mm[:, 63:192:64], -2048.0)
+    aff("C1 CF", "C1", T.C1[:], T.C1[:], 1.0, col["m"])
+    aff("xc CF", "xc", T.xc[:], T.xc[:], 1.0, col["m"])
+    aff("CK", "CK", T.CK[:], T.CK[:], 1024.0, -LAST - 1.0)
+    aff("C1", "CZ", T.CZ[:], T.C1[:], 1024.0, 3072.0)
+    act("xc", "xcb", T.xcb[:], T.xc[:], scale=-BIG)
+
+    def late_constants():
+        for k, c in ((31, 97.0), (63, 97.0), (96, -4096.0)):
+            fill("ST%d" % k, T.ST[:, k:7 * SEG:SEG], c, "ST")
+        ts("ST end", "ST95", T.ST[:, 95:7 * SEG:SEG], T.ST[:, 95:7 * SEG:SEG], col["end"], A.mult)
+
+    pn = T.PN[:, 2:120:3]
+    tt("PN YJ", "ne", T.ne[:], pn, T.YJ[:, 40 * upper(0):40 * upper(0) + 40], A.not_equal)
 
     for t in range(3):
         u = upper(t)
         B0, Bp, b0 = C * u, C - C * u, 10 * u
         QF, G, B, PO, PP, VV, MP = ["%s%d" % (n, t) for n in ("QF", "G", "B", "PO", "PP", "VV", "MP")]
         mo = T.MO[:, 20 * t:20 * t + 20]
-        win = "%s %sp %sh" % (QF, QF, QF)
-        for e in range(2):
-            pick(win + " " + PO, "Go%d" % e, G, 640 * e + B0, QF, 0, T[PO][:, 20 * e:20 * e + 20])
+        win = "%s %sp %sh " % (QF, QF, QF)
+
+        def unpack(h, e, x, at, R, start, stop):
             for b in range(4):
-                mm(b, "QE", 512 * e + 128 * b, G, 640 * e + B0, C, "QE%d%d Go%dc Go%ds" % (e, b, e, e), e == 0, False)
+                mm(4 * h + b, "QE", 512 * e + 128 * b, x, at + H * h, H, "QE%d%d %s" % (e, b, R), start, stop)
         for e in range(2):
-            pick(win + " " + PP, "Gp%d" % e, G, 640 * e + Bp, QF, 0, T[PP][:, 20 * e:20 * e + 20])
-            pick("Go%dc Gp%dc %s" % (e, e, PO), "B%d" % e, B, C * e, G, 640 * e, T[PO][:, 20 * e:20 * e + 20], "v")
-            pick("Go%ds Gp%ds %s" % (e, e, PO), "B%d" % e, B, C * e, G, 640 * e, T[PO][:, 20 * e:20 * e + 20], "s")
-            for b in range(4):
-                mm(b, "QE", 512 * e + 128 * b, B, C * e, C, "B%dc B%ds" % (e, e), False, e == 1)
+            pick(win + PO + "ab"[e], "Go%d" % e, G, 640 * e + B0, QF, 0, T[PO][:, 20 * e:20 * e + 20])
+            for h in range(2):
+                unpack(h, e, G, 640 * e + B0, "Go%dc Go%ds" % (e, e), e == 0, False)
+        tt("ne PN", "PZ", T.PZ[:, 0:40], T.ne[:], pn, A.mult)
+        ts("%sa %sb PA" % (PO, PO), "PAo", T.PA[:, 40 * u:40 * u + 40], T[PO][:, 0:40], 1.0, A.add)
+        for e in range(2):
+            aff("PZ g%d" % e, "PZ%d" % e, T.PZ[:, e:40:2], T.PZ[:, e:40:2], 1.0, col["g%d" % e])
+        act("PN", "S3p", T.S3[:, 2:120:3], pn)
+        spread1("PZ0 PZ1", "PZ", T.PZ, 40, 64)
+        pick(win + PP, "Gp0", G, Bp, QF, 0, T[PP][:, 0:20])
         ts(PP + " PA", "PAp", T.PA[:, 40 - 40 * u:80 - 40 * u], T[PP][:], 1.0, A.add)
-        act("PN0 PN1", "S3p", T.S3[:, 2:120:3], T.PN[:, 2:120:3])
-        for b in range(4):
-            if b % 2:
-                act("ps%d QYpad" % b, "Y%d" % b, T.Yt[:, b:1280:4], ps(b), scale=0.5)
-            else:
-                op("v", "ps%d QYpad" % b, "Y%d" % b, V.tensor_scalar, T.Yt[:, b:1280:4], ps(b), 0.5, None, A.mult)
-        quant("Y0 Y1 Y2 Y3", "QY", "QY", 0, C, T.Yt[:, 0:1280])
+        pick("Go0# Gp0# " + PO + "a", "B0", B, 0, G, 0, T[PO][:, 0:20])
+        for h in range(2):
+            unpack(h, 0, B, 0, "B0c B0s", False, False)
+        pick(win + PP, "Gp1", G, 640 + Bp, QF, 0, T[PP][:, 20:40])
+        for h in range(2):
+            pick("Go1# Gp1# " + PO + "b", "B1%d" % h, B, C + H * h, G, 640, T[PO][:, 20 + 10 * h:30 + 10 * h])
+            unpack(h, 1, B, C, "B1%dc B1%ds" % (h, h), False, True)
+        if t == 0:
+            late_constants()
+        for h in range(2):
+            for b in range(4):
+                k, out = 4 * h + b, T.Yt[:, 4 * H * h + b:4 * H * (h + 1):4]
+                if COPY[h][b] == "s":
+                    act("ps%d QYpad" % k, "Y%d" % k, out, ps(k, H), scale=0.5)
+                else:
+                    ts("ps%d QYpad" % k, "Y%d" % k, out, ps(k, H), 0.5, A.mult)
+            quant(keys("Y%d", range(4 * h, 4 * h + 4)), "QY%d" % h, "QY", H * h, H * h + H, T.Yt[:, 4 * H * h:4 * H * (h + 1)])
+        spread2("PZ", T.PZ, 40, 64)
+        act(keys("PZ_%d", 4) + " CUt", "PT", T.PT[:], T.PZ[:].indirect(cu(CT)))
         for k in range(3):
-            mm(4 + k, "QY", 128 * k, "QAB", 0, 128, "QY QABc QABs")
-        for b in range(4):
-            mm(b, "QW", 128 * b, "QY", 0, C, "QW QW2 QY")
-        act("PAo PAp CUr", "VR", T.VR[:], T.PA[:].indirect(cu(CR)))
+            mm(k, "QY", 128 * k, "QAB", 0, 128, ("QY0 QY1" if k else "QY0") + " QABc QABs")
+            act("ps%d" % k, "SL%d" % k, T.SL[:, 64 * k:64 * k + 64], T["ps%d" % k][:, 64:128])
         for k in range(3):
-            act("ps%d" % (4 + k), "SL%d" % k, T.SL[:, 64 * k:64 * k + 64], T["ps%d" % (4 + k)][:, 64:128])
+            tt("ps%d SL%d" % (k, k), "D%d" % k, T.D[:, 64 * k:64 * k + 64], ps(k, 64), T.SL[:, 64 * k:64 * k + 64], A.is_gt)
+        for b in range(4):
+            mm(4 + b, "QW", 128 * b, "QY", 0, C, "QW QW2 QY0 QY1")
+
+
+        def relu(lo, hi):
+            for b in range(lo, hi):
+                act("ps%d" % (4 + b), "TB%d" % b, T.TB[:, C * b:C * b + C], ps(4 + b), F.Relu, scale=0.03125)
+        relu(0, EARLY)
+        for b in range(4):
+            for e in range(2):
+                mm((3 + b) % 4, "QE", 512 * e + 128 * b, QF, B0, C, "QE%d%d %s %sh" % (e, b, QF, QF), e == 0, e == 1)
+        scan("D0 D1 D2 Mma Mmb Mm0 Mm1 Mm2", "SC", T.SC[:], T.Mm[:], T.D[:], 0.0, A.mult, A.add)
         if t == 1:
             quant("vin", "QV", "QV", 0, 128, T.vin[:])
-        tt("C1 VR", "dd", T.dd[:], T.VR[:], T.C1[:], A.subtract)
+        tt("SC PT VW", "VWs", T.VW[:, :, 0:8], T.SC[:, 7:192:8], T.PT[:, 0:24], A.add)
         for k in range(3):
-            tt("ps%d SL%d" % (4 + k, k), "D%d" % k, T.D[:, 64 * k:64 * k + 64], ps(4 + k, 64), T.SL[:, 64 * k:64 * k + 64], A.is_gt)
-        for e in range(2):
-            for b in range(4):
-                mm(4 + b, "QE", 512 * e + 128 * b, QF, B0, C, "QE%d%d %s %sh" % (e, b, QF, QF), e == 0, e == 1)
-        scan("D0 D1 D2 Mm Mm9 Mm0 Mm1 Mm2", "SC", T.SC[:], T.Mm[:], T.D[:], 0.0, A.mult, A.add)
-        for b in range(2):
-            act("ps%d" % b, "TB%d" % b, T.TB[:, C * b:C * b + C], ps(b), F.Relu, scale=0.03125)
-        vv = T[VV][:, 24 * u:24 * u + 24]
-        tt("SC PT", VV, vv, T.SC[:, 7:192:8], T.PT[:, 0:24], A.add)
-        send(t, "av%d" % t, VV, VV + "p", vv, vv)
-        scan(VV + " keep24", "SM", T.SM[:], T.keep24[:], vv, 0.0, A.mult, A.max)
-        top = T.SM[:, 7:24:8]
-        for k in range(3):
-            ts("SM Ypad", "AB%d" % k, T.AB[:, 32 * k:32 * k + 32], T.Yt[:, 1280:1312], T.SM[:, 8 * k + 7:8 * k + 8], A.add)
-        turn("AB0 AB1 AB2", "AR", T.AR[:], T.AB[:])
-        tt("SM CK", "sk0", T.sk[:, 0:3], top, T.CK[:, 3 * u:3 * u + 3], A.add)
-        ts("SM", "sk1", T.sk[:, 4:7], top, LAST, A.is_le, NONE, A.mult)
+            scan("VWs", "SW%d" % k, T.SW[:, k, :], T.VW[:, k, :], T.VW[:, k, :], 0.0, A.max, A.max)
+        top = T.SW[:, :, 39]
+        cp("VWs", VV + "v", T[VV][:, 28 * u:28 * u + 24], T.VW[:, :, 0:8])
+        turn("SW0 SW1 SW2", "AR", T.AR[:], T.SW[:, :, 8:40])
+        tt("SW0 SW1 SW2 CK sk", "sk0", T.sk[:, 0:3], top, T.CK[:, 3 * u:3 * u + 3], A.add)
+        ts("SW0 SW1 SW2 sk", "sk1", T.sk[:, 4:7], top, LAST, A.is_le, NONE, A.mult)
         for j in range(ON_V, 20):
             act("AR xcb", "D0_%d" % j, T.D0[:, SEG * j:SEG * j + 96], T.AR[:], F.Abs, scale=BIG, bias=T.xcb[:, j:j + 1])
+        relu(EARLY, 4)
         for j in range(ON_V):
             ts("AR xc", "D0_%d" % j, T.D0[:, SEG * j:SEG * j + 96], T.AR[:], T.xc[:, j:j + 1], A.not_equal, BIG, A.mult)
-        tt("sk0 sk1 SK", "SKs", T.SK[:, 16:25:4], T.sk[:, 0:3], T.sk[:, 4:7], A.max)
+            if j == 0:
+                tt("sk0 sk1", VV, T[VV][:, 28 * u + 24:28 * u + 28], T.sk[:, 0:4], T.sk[:, 4:8], A.max)
+                send(t, "av%d" % t, "%s %sv" % (VV, VV), VV + "p", T[VV][:, 28 * u:28 * u + 28], T[VV][:, 28 * u:28 * u + 28])
         for lo, hi in SCANS:
-            scan(" ".join("D0_%d" % j for j in range(lo, hi)) + " D0r ST31 ST63 ST95 ST96", "SO%d" % lo, T.SO[:, SEG * lo:SEG * hi],
+            scan(keys("D0_%d", range(lo, hi)) + " D0r ST31 ST63 ST95 ST96", "SO%d" % lo, T.SO[:, SEG * lo:SEG * hi],
                  T.D0[:, SEG * lo:SEG * hi], T.ST[:, 0:SEG * (hi - lo)], 4096.0, A.min, A.subtract)
-        ts(" ".join("SO%d" % lo for lo, hi in SCANS) + " KK", "KKs", T.KK[:, 10:30], T.SO[:, 95:20 * SEG:SEG], 160.0 + B0, A.add,
-           1025.0, A.mult)
-        tt("KKs SKs CUs", "M0", T.M0[:, b0:b0 + 32], T.SK[:].indirect(cu(CS)), T.KK[:, b0:b0 + 32], A.min)
-        tt("M0", "M1", T.M1[0:64, :], T.M0[0:64, 10:30], T.M0[64:128, 10:30], A.min)
+
+        def state(at):
+            for b in range(4):
+                if XAT[b] == at:
+                    k = (3 + b) % 4
+                    tt("TB%d ps%d" % (b, k), "X%d" % b, T.Xt[:, b:1280:4], T.TB[:, C * b:C * b + C], ps(k), A.add)
+        state(-1)
+        ts(keys("SO%d", [lo for lo, hi in SCANS]), "KK", T.KK[:], T.SO[:, 95:20 * SEG:SEG], 160.0 + B0, A.add, 1025.0, A.mult)
+        state(0)
+        tt("KK", "M1", T.M1[0:64, :], T.KK[0:64, :], T.KK[64:128, :], A.min)
+        state(1)
         for a in range(4):
             tt("M1", "MO%d" % a, T.MO[32 * a:32 * a + 32, 20 * t:20 * t + 20], T.M1[0:32, :], T.M1[32:64, :], A.min)
-        send(t, "am%d" % t, "MO0 MO1 MO2 MO3", MP, T[MP][:], mo)
-        order("s", [VV + "p"], [])
-        k = spread(VV, T[VV], 48, 48)
+        send(t, "am%d" % t, keys("MO%d", 4), MP, T[MP][:], mo)
+        act("PAo PAp CUr", "VR", T.VR[:], T.PA[:].indirect(cu(CR)))
+        spread1("%s %sv %sp" % (VV, VV, VV), VV, T[VV], 56, 56)
+        if t == 0:
+            act("YR m6 hm", "YR", T.YR[:], T.YR[:], F.Identity, scale=col["m6"], bias=col["hm"])
+        spread2(VV, T[VV], 56, 56)
+        k = keys(VV + "_%d", 4)
         act(k + " CUv", "va", T.va[:], T[VV][:].indirect(cu(CV)), F.Abs, bias=-11263.5)
         act(k + " CUv", "vh", T.vh[:], T[VV][:].indirect(cu(CV)))
-        for b in range(2, 4):
-            act("ps%d" % b, "TB%d" % b, T.TB[:, C * b:C * b + C], ps(b), F.Relu, scale=0.03125)
-
-        def state(b):
-            tt("TB%d ps%d" % (b, 4 + b), "X%d" % b, T.Xt[:, b:1280:4], T.TB[:, C * b:C * b + C], ps(4 + b), A.add)
-        state(0)
-        state(1)
+        act(k + " CUs", "SK", T.SK[:], T[VV][:].indirect(cu(CS)))
+        state(2)
+        tt("C1 VR", "dd", T.dd[:], T.VR[:], T.C1[:], A.subtract)
+        if t < 2:
+            n = C * upper(t + 1)
+            quant(keys("X%d", 4), "QF%d" % (t + 1), "QF%d" % (t + 1), n, n + C, T.Xt[:])
+            send_state(t + 1, 0, C, "QF%d" % (t + 1))
+        else:
+            quant(keys("X%d", 4), "QX3", "QX3", 0, C, T.Xt[:])
+            mm(4, "QV", 0, "QX3", 0, C, "QV QX3")
+            dma("y", "out", "QX3", "", T.oc[:], T.QX3[:].bitcast(dt.uint8))
+            for k in range(4):
+                dma("y", "out", "QX3", "", T.osc[4 * k:4 * k + 4, :], T.SQX3[32 * k:32 * k + 4, :])
         ts("va", "vv", T.vv[:], T.va[:], 3072.0, A.is_ge)
         ts("vh", "vh", T.vh[:], T.vh[:], LAST, A.is_ge)
-        tt("vv CZ ZY", "ZYs", T.ZY[:, 0:48], T.vv[:], T.CZ[:], A.mult)
-        tt("vh dd", "VFr", T.VF[:, 0:96:2], T.vh[:], T.dd[:], A.mult)
-        turn("ZYs", "T1", T.T1[:], T.ZY[:, 24 * u:24 * u + 32])
-        tt("VR VFr", "VFg", T.VF[:, 1:96:2], T.VR[:], T.VF[:, 0:96:2], A.subtract)
+        for w in range(2):
+            tt(keys("MO%d", 4) + " SK", "MQ%d" % w, T.MQ[:, 10 * w:10 * w + 10], T.MO[:, 20 * t + 10 * w:20 * t + 10 * w + 10],
+               T.SK[:, 16 * w:16 * w + 10], A.min)
+        tt("vv CZ VF", "VFz", T.VF[:, 2:144:3], T.vv[:], T.CZ[:], A.mult)
+        tt("vh dd VF", "VFh", T.VF[:, 0:144:3], T.vh[:], T.dd[:], A.mult)
+        turn("VFz", "T1", T.T1[:], T.VF[:, 72 * u + 2:72 * u + 96:3])
+        tt("VR VFh", "VFg", T.VF[:, 1:144:3], T.VR[:], T.VF[:, 0:144:3], A.subtract)
         for h in range(2):
             act("T1", "Z3%d" % h, T.Z3[:, h:4:2, :], T.T1[:])
         for w in range(2):
             for h in range(2):
-                act("VFr VFg Tin Tin2", "Ta%d%d" % (w, h), T.Tin[:, 20 * w + h:20 * w + 20:2, 0:4], T.VF[:, 48 * w:48 * w + 40])
-                act("ZYs Tin Tin2", "Tb%d%d" % (w, h), T.Tin[:, 20 * w + h:20 * w + 20:2, 4:6], T.ZY[:, 24 * w:24 * w + 20])
-        state(2)
-        state(3)
-        if t < 2:
-            n = C * upper(t + 1)
-            quant("X0 X1 X2 X3", "QF%d" % (t + 1), "QF%d" % (t + 1), n, n + C, T.Xt[:])
-            send_state(t + 1, 0, C, "QF%d" % (t + 1))
-        else:
-            quant("X0 X1 X2 X3", "QX3", "QX3", 0, C, T.Xt[:])
-            mm(0, "QV", 0, "QX3", 0, C, "QV QX3")
-            dma("y", "out", "QX3", "", T.oc[:], T.QX3[:].bitcast(dt.uint8))
-            for k in range(4):
-                dma("y", "out", "QX3", "", T.osc[4 * k:4 * k + 4, :], T.SQX3[32 * k:32 * k + 4, :])
-            act("ps0", "ys", T.ys[:], ps(0))
+                act("VFz VFh VFg Tin Tin2", "Ta%d%d" % (w, h), T.Tin[:, 20 * w + h:20 * w + 20:2, 0:6], T.VF[:, 72 * w:72 * w + 60])
+        if t == 2:
+            act("ps4", "ys", T.ys[:], ps(4))
             dma("y", "out", "ys", "", T.y[:], T.ys[:])
+        tt("MQ0 MQ1 " + MP, "I1", T.I1[:], T.MQ[:, b0:b0 + 10], T[MP][:, b0:b0 + 10], A.min)
+        for h in range(2):
+            tt("MQ0 MQ1 Tin Tin2 " + MP, "Tk%d" % h, T.Tin[:, h:40:2, 6], T.MQ[:], T[MP][:], A.min)
+        ts("I1", "I2", T.I2[:], T.I1[:], 1023, band)
+        turn("Tk0 Tk1 Tpad " + keys("Ta%d%d", 2, 2), "Tout", T.Tout[:], T.Tin[:])
+        for h in range(2):
+            cp("I2", "OFF%d" % h, T.OFF[:, h:20:2], T.I2[:])
         turn("Z30 Z31", "ZT", T.ZT[:], T.Z3[:])
         for h in range(2):
             act("ZT", "ZO%d" % h, T.ZO[:, h:20:2, :], T.ZT[:, 32 * h:32 * h + 20])
         for h in range(2):
-            tt("MO0 MO1 MO2 MO3 Tin Tin2 " + MP, "Tk%d" % h, T.Tin[:, h:40:2, 6], mo, T[MP][:], A.min)
-        cp("Tk0 Tk1", "I1", T.I1[:], T.Tin[:, 2 * b0:2 * b0 + 20, 6])
-        turn("Tk0 Tk1 Tpad Ta00 Ta01 Ta10 Ta11 Tb00 Tb01 Tb10 Tb11", "Tout", T.Tout[:], T.Tin[:])
-        ts("I1", "I2", T.I2[:], T.I1[:], 1023, band)
-        cp("I2", "OFF", T.OFF[:], T.I2[:])
-        cp("Tout OFF", "GG", T.GG[:], T.Tout[:].indirect(T.OFF[:]))
-        turn("GG", "ZZ", T.ZZ[:], T.GG[:])
+            tt("Tout OFF0 OFF1 YR", "GG%d" % h, T.GG[:, H * h:H * h + H], T.Tout[:].indirect(T.OFF[:, 10 * h:10 * h + 10]),
+               T.YR[:, B0 + H * h:B0 + H * h + H], A.subtract)
+        for h in range(2):
+            turn("GG%d" % h, "ZZ%d" % h, T.ZZ[:, 10 * h:10 * h + 10, :], T.GG[:, H * h:H * h + H])
+        act("ZZ0 ZZ1", "S30", T.S3[:, 0:120:3], T.ZZ[:, :, 0:6:3])
         for e in range(2):
-            tt("ZZ Y16", "W2%d" % e, T.W2[:, :, e], T.ZZ[:, :, 6], T.Y16[:, 2 * b0:2 * b0 + 20], A.subtract)
-        cp("ZZ", "S30", T.S3[:, 0:120:3], T.ZZ[:, :, 0:4:2])
-        tt("W20 W21 ZO0 ZO1", "Q31", T.Q3[:, 1:120:3], T.W2[:], T.ZO[:], A.is_equal)
-        tt("W20 W21 ZZ", "q2", T.q2[:], T.W2[:], T.ZZ[:, :, 4:6], A.is_equal)
-        tt("ZZ PN0 PN1", "S31", T.S3[:, 1:120:3], T.ZZ[:, :, 1:4:2], T.PN[:, 2:120:3], A.subtract)
-        tt("Q31 q2", "Q32", T.Q3[:, 2:120:3], T.Q3[:, 1:120:3], T.q2[:], A.add)
-        scan("S30 S31 S3p Q30 Q31 Q32", "PN0 PN1", T.PN[:], T.Q3[:], T.S3[:], 0.0, A.mult, A.add)
+            tt("ZZ0 ZZ1 ZO0 ZO1", "Q31%d" % e, T.Q3[:, 3 * e + 1:120:6], T.ZZ[:, :, 6], T.ZO[:, :, e], A.is_equal)
+            tt("ZZ0 ZZ1", "q2%d" % e, T.q2[:, e:40:2], T.ZZ[:, :, 6], T.ZZ[:, :, 3 * e + 2], A.is_equal)
+        tt("ZZ0 ZZ1 PN", "S31", T.S3[:, 1:120:3], T.ZZ[:, :, 1:6:3], pn, A.subtract)
+        tt("Q310 Q311 q20 q21", "Q32", T.Q3[:, 2:120:3], T.Q3[:, 1:120:3], T.q2[:], A.add)
+        scan("S30 S31 S3p Q30 Q32", "PN", T.PN[:], T.Q3[:], T.S3[:], 0.0, A.mult, A.add)
         if t < 2:
             o = "PO%d" % (t + 1)
             for e in range(2):
-                ts("PN0", o + "ab"[e], T[o][:, 20 * e:20 * e + 20], T.PN[:, 3 * e + 2:120:6], -1.0, A.add)
-            wrote[o] = wrote[o + "b"]
-            send(t + 1, "ap%d" % (t + 1), o, "PP%d" % (t + 1), T["PP%d" % (t + 1)][:], T[o][:])
-            pointers(t + 1)
+                ts("PN", o + "ab"[e], T[o][:, 20 * e:20 * e + 20], T.PN[:, 3 * e + 2:120:6], -1.0, A.add)
+            send(t + 1, "ap%d" % (t + 1), "%sa %sb" % (o, o), "PP%d" % (t + 1), T["PP%d" % (t + 1)][:], T[o][:])
+            n = 40 * upper(t + 1)
+            tt("PN YJ", "ne", T.ne[:], pn, T.YJ[:, n:n + 40], A.not_equal)
         else:
             for e in range(2):
-                ts("PN0 OI", "OI%d" % e, T.OI[:, 32 * e:32 * e + 20], T.PN[:, 3 * e + 2:120:6], -1.0, A.add)
+                ts("PN OI", "OI%d" % e, T.OI[:, 32 * e:32 * e + 20], T.PN[:, 3 * e + 2:120:6], -1.0, A.add)
             turn("OI0 OI1", "OT", T.OT[:], T.OI[:])
             for k in range(8):
                 dma("ys"[k % 2], "out2", "OT", "", T.ov[k, :], T.OT[32 * (k // 2):32 * (k // 2) + 20, 32 * (k % 2):32 * (k % 2) + 16])

@@ -7,11 +7,13 @@ SEG = 97
 BIG = 16384.0
 LAST = 14336.0
 NONE = 1048576.0 + 640.0
+SHIFT = 1048576 + 4096
+STILL = 460.0
 ON_V = 6
 SCANS = ((6, 10), (0, 6), (10, 17), (17, 20))
 COPY = ("vsvs", "svsv")
 EARLY = 3
-XAT = (0, 2, 2, 2)
+XAT = (0, 1, 2, 2)
 
 SCRATCH = {}
 
@@ -29,14 +31,14 @@ for _n, _w in (("QF0", 640), ("QF1", 640), ("QF2", 640), ("G0", 1280), ("G1", 12
                ("QX3", C), ("QY", 384), ("QE", 1024), ("QW", 512), ("QU", 128), ("QAB", 128), ("QV", 128)):
     _buf(_n, _w, CODE)
     _buf("S" + _n, _w, "uint8")
-for _n, _w in (("TB", 1280), ("SL", 192), ("PT", 32), ("VR", 48), ("VW", [3, 40]), ("SW", [3, 40]), ("AR", 96), ("KK", 20),
+for _n, _w in (("TB", 1280), ("SL", 192), ("PT", 32), ("VR", 80), ("G24", 24), ("VW", [3, 40]), ("SW", [3, 40]), ("AR", 96), ("KK", 20),
                ("M1", 20), ("SK", 32), ("sk", 8), ("MO", 60), ("MQ", 20), ("MP0", 20), ("MP1", 20), ("MP2", 20),
-               ("VV0", 224), ("VV1", 224), ("VV2", 224), ("Tin", [42, 16]), ("Tout", 672), ("GG", C), ("ZZ", [20, 16]),
-               ("VF", 168), ("va", 48), ("vh", 48), ("vv", 48), ("dd", 48), ("T1", 32), ("Z3", [4, 16]), ("ZT", 64),
-               ("ZO", [20, 2]), ("q2", 40), ("Q3", 120), ("S3", 120), ("PN", 120),
-               ("ne", 40), ("PZ", 256), ("PA", 96), ("OI", 64), ("OT", 64), ("ys", C),
-               ("idm", 128), ("CF", 32), ("NI", 8), ("NJ", 8), ("t8", 8), ("CL", 24), ("l1", 8), ("xc", 20), ("xcb", 20),
-               ("YJ", 80), ("YR", 640), ("C1", 48), ("CZ", 48), ("CK", 6)):
+               ("VV0", 224), ("VV1", 224), ("VV2", 224), ("Tin", [52, 16]), ("Tout", 672), ("GG", C), ("ZZ", [20, 16]),
+               ("va", 80), ("vh", 80), ("dd", 80), ("T1", 32), ("Z3", [4, 16]), ("ZT", 64),
+               ("ZO", [20, 2]), ("q1", 40), ("Q3", 120), ("S3", 120), ("PN", 160),
+               ("ne", 40), ("PS", 40), ("PZ", 256), ("PA", 80), ("OT", 64), ("ys", C),
+               ("idm", 128), ("CF", 36), ("NI", 8), ("NJ", 8), ("t8", 8), ("CL", 16), ("l1", 8), ("xc", 20), ("xcb", 20),
+               ("YJ", 80), ("YR", 640), ("C1", 80), ("CZ", 80), ("CK", 6)):
     _buf(_n, _w, "float32")
 for _n, _w in (("Vi", 60), ("PI", 2), ("CI", 16), ("I1", 10), ("I2", 10)):
     _buf(_n, _w, "int32")
@@ -187,13 +189,10 @@ def rank_program(g, core, T, topo):
 
     shr, band = A.logical_shift_right, A.bitwise_and
     DIGITS = (("h16", 0, 16), ("i", 0, 15), ("i8", 0, 8), ("k7", 0, 7), ("r32", 0, 96), ("e", 0, 1), ("m", 0, 31), ("p112", 0, 112),
-              ("k0", 1, 1), ("r0", 5, 1), ("k1", 2, 1), ("r1", 6, 1), ("k8", 0, 7), ("q4", 2, 3))
-    MORE = ("lowh", "h", "even", "x0", "sg", "x1", "sh", "dR", "dT", "dV", "dS", "end", "g0", "g1", "m6", "hm")
+              ("k0", 1, 1), ("r0", 5, 1), ("k1", 2, 1), ("r1", 6, 1), ("k8", 0, 7), ("q4", 2, 3), ("i3", 3, 1))
+    MORE = ("lowh", "h", "even", "x0", "sg", "x1", "sh", "x2", "x3", "dR", "dT", "dV", "dS", "a1", "a2", "end", "g0", "g1", "m6", "hm")
     col = {n: T.CF[:, k:k + 1] for k, n in enumerate([d[0] for d in DIGITS] + list(MORE))}
-    CAB, CR, CT, CV, CS = (0, 8), (8, 11), (12, 14), (14, 17), (18, 20)
-
-    def cl(c):
-        return T.CL[:, c[0]:c[1]]
+    CAB, CR, CT, CV, CS = (0, 8), (8, 13), (14, 16), (16, 21), (22, 24)
 
     def cu(c):
         return T.CU[:, c[0]:c[1]]
@@ -218,7 +217,7 @@ def rank_program(g, core, T, topo):
     fill("Z", T.Z[:], 0.0)
     for k, (n, sh, m) in enumerate(DIGITS):
         ts("PI", "CI%d" % k, T.CI[:, k:k + 1], T.PI[:, 1:2] if n == "k8" else T.PI[:, 0:1], sh, shr, m, band)
-    cp(keys("CI%d", 14), "CF", T.CF[:, 0:14], T.CI[:, 0:14])
+    cp(keys("CI%d", 15), "CF", T.CF[:, 0:15], T.CI[:, 0:15])
     fill("Ypad", T.Yt[:, 1024:1536], 0.0)
     ts("NI CF", "NJ", T.NJ[:], T.NI[:], col["i"], A.add)
     ts("CF", "lowh", col["lowh"], col["h16"], -1.25, A.mult, 20.0, A.add)
@@ -239,62 +238,66 @@ def rank_program(g, core, T, topo):
             at = 512 * par + 128 * b
             quant("Z%d" % par, "QE%d%d" % (par, b), "QE", at, at + 128, T.Z[:, 520 * par + 3 - b:520 * par + 515 - b])
         if par == 0:
-            cp("Vi Vi1 Vi2 CP", "PO0a PO0b", T.PO0[:], T.Vi[:].indirect(T.CP[:, 0:3]))
-            send(0, "ap0", "PO0a", "PP0", T.PP0[:], T.PO0[:, 0:40])
+            cp("Vi Vi1 Vi2 CP", "PO0", T.PO0[:], T.Vi[:].indirect(T.CP[:, 0:3]))
+            send(0, "ap0", "PO0", "PP0", T.PP0[:], T.PO0[:, 0:40])
     dma("y", "lw", "QF0p", "QW", T.QW[:].bitcast(dt.uint8), T.wc[:])
     dma("y", "lw", "", "QW2", T.SQW[:], T.ws[:])
     dma("y", "lv", "", "vin", T.vin[:], T.v[:])
 
-    iota("YJ", T.YJ[:], [[16, 40], [0, 2]], 0, 1)
+    iota("YJ", T.YJ[:], [[C, 2], [0, 2], [16, 20]], 0, 1)
     iota("xc", T.xc[:], [[32, 20]], 0, int(LAST) + 1)
-    iota("C1", T.C1[:], [[C, 2], [32, 12], [0, 2]], 0, 1)
+    iota("C1", T.C1[:], [[32, 20], [0, 4]], 0, 1)
     iota("CK", T.CK[:], [[C, 2], [128, 3]], 1)
+    iota("G24", T.G24[:], [[0, 3], [2048, 8]], 0)
     iota("ST", T.ST[:], [[0, 7 * SEG]], 0, 1)
-    iota("YR", T.YR[:], [[32, 20], [0, 2], [1, 16]], 0, -4096)
-    aff("h CF", "dR", col["dR"], col["e"], 19.0, col["h"])
-    aff("CF", "dT", col["dT"], col["p112"], 0.125, col["e"])
+    iota("YR", T.YR[:], [[32, 20], [0, 2], [1, 16]], 0, -SHIFT)
+    aff("h CF", "dR", col["dR"], col["e"], 20.0, col["h"])
+    aff("CF", "dT", col["dT"], col["p112"], 0.0625, 0.0)
     aff("CF", "dV", col["dV"], col["r32"], 0.0625, col["e"])
     aff("CF", "end", col["end"], col["r32"], -1.0, -127.0)
     for e in range(2):
         aff("CF", "g%d" % e, col["g%d" % e], col["r32"], 128.0, 2048.0 * e)
-    sfill("VF", T.VF[:], 168, 0.0)
-    sfill("OI", T.OI[:], 64, 0.0)
+    sfill("PN0", T.PN[:], 160, 0.0)
+    aff("dR CF", "dR", col["dR"], col["q4"], 2.0, col["dR"])
+    aff("dT CF", "dT", col["dT"], col["e"], 32.0, col["dT"])
     sfill("VW", T.VW[:], 120, 0.0)
     sfill("sk", T.sk[:], 8, 0.0)
-    sfill("PA", T.PA[:], 96, 0.0)
     sfill("PZ", T.PZ[:], 256, 0.0)
-    sfill("Tin", T.Tin[:, 0:21, :], 336, -1.0)
-    sfill("Tin2", T.Tin[:, 21:42, :], 336, -1.0)
+    sfill("Tin", T.Tin[:, 0:26, :], 416, -1.0)
+    sfill("Tin2", T.Tin[:, 26:52, :], 416, -1.0)
     ts("CF", "x0", col["x0"], col["k0"], col["r0"], A.not_equal, 2.0, A.mult)
     ts("CF", "x1", col["x1"], col["e"], col["r0"], A.not_equal, 2.0, A.mult)
+    ts("CF", "x2", col["x2"], col["k1"], col["r0"], A.not_equal, 112.0, A.mult)
+    ts("CF", "x3", col["x3"], col["i3"], col["r1"], A.not_equal, 56.0, A.mult)
     ts("NI CF", "t8", T.t8[:], T.NI[:], col["i8"], A.add, 0.125, A.mult)
-    ts("NJ", "l1", T.l1[:, 0:3], T.NJ[:, 0:3], 24.0, A.is_ge, 16.0, A.mult)
+    ts("NJ", "l1", T.l1[:, 0:5], T.NJ[:, 0:5], 40.0, A.is_ge, 20.0, A.mult)
     ts("CF", "m6", col["m6"], col["i"], 6.0, A.is_equal)
     ts("CF x0", "sg", col["sg"], col["k1"], col["r1"], A.not_equal, col["x0"], A.add)
     ts("CF x1", "sh", col["sh"], col["k0"], col["r1"], A.not_equal, col["x1"], A.add)
+    ts("x2 x3 dV", "dV", col["dV"], col["x2"], col["x3"], A.add, col["dV"], A.add)
+    ts("x3 CF", "a1", col["a1"], col["x3"], -2.0, A.mult, col["i8"], A.add)
     ts("t8 CF", "CAa", T.CU[:, 0:4], T.t8[:, 0:4], col["k8"], A.max, 16.0, A.mult)
     ts("t8 CF", "CAb", T.CU[:, 4:8], T.t8[:, 0:4], col["k7"], A.min, 16.0, A.mult)
     ts("CF m6", "hm", col["hm"], col["h16"], col["m6"], A.mult)
     aff("sg dT", "dT", col["dT"], col["sg"], 64.0, col["dT"])
-    aff("sg dV", "dV", col["dV"], col["sg"], 56.0, col["dV"])
     aff("sh CF", "dS", col["dS"], col["sh"], 56.0, col["q4"])
-    aff("l1 dR", "l1r", T.CL[:, 20:23], T.l1[:, 0:3], 1.0, col["dR"])
-    aff("t8 dV", "l1v", T.l1[:, 4:7], T.t8[:, 0:3], 8.0, col["dV"])
+    aff("NI dR", "l1r", T.CL[:, 0:5], T.NI[:, 0:5], 0.5, col["dR"])
     quant("uin", "QU", "QU", 0, 128, T.uin[:])
+    ts("a1 CF", "a2", col["a2"], col["a1"], 60.0, A.add, col["i3"], A.mult)
+    ts("a1 dV", "a1", col["a1"], col["a1"], 60.0, A.add, col["dV"], A.add)
     ts("YJ CF", "YJ", T.YJ[:], T.YJ[:], col["i"], A.add)
-    for e in range(2):
-        ts("PO0a", "PN", T.PN[:, 3 * e + 2:120:6], T.PO0[:, 20 * e:20 * e + 20], 1.0, A.add)
+    ts("PO0 PN0", "PN", T.PN[:, 2:120:3], T.PO0[:, 0:40], 1.0, A.add)
     cp("QU CAa CAb", "QABc", words(T.QAB[:]), words(T.QU[:]).indirect(cu(CAB)))
     act("QU CAa CAb", "QABs", T.SQAB[:], T.SQU[:].indirect(cu(CAB)))
-    ts("t8 dT", "CUt", cu(CT), T.t8[:, 0:2], 16.0, A.mult, col["dT"], A.add)
-    ts("l1", "l1q", T.CL[:, 0:3], T.l1[:, 0:3], 0.25, A.mult)
-    ts("NI dS", "l1s", T.CL[:, 4:6], T.NI[:, 0:2], 1.75, A.mult, col["dS"], A.add)
-    tt("l1r NJ", "CLr", cl(CR), T.CL[:, 20:23], T.NJ[:, 0:3], A.add)
-    tt("l1q l1v", "CLv", cl(CV), T.CL[:, 0:3], T.l1[:, 4:7], A.add)
-    ts("l1s", "CUs", cu(CS), T.CL[:, 4:6], 24.0, A.add)
+    ts("a2 dV", "a2", col["a2"], col["a2"], col["dV"], A.add)
+    ts("t8 dT", "CUt", cu(CT), T.t8[:, 0:2], 8.0, A.mult, col["dT"], A.add)
+    ts("NI dS", "l1s", T.CL[:, 6:8], T.NI[:, 0:2], 1.75, A.mult, col["dS"], A.add)
+    tt("l1r l1", "CLr", T.CL[:, 8:13], T.CL[:, 0:5], T.l1[:, 0:5], A.add)
     fill("Mm", T.Mm[:], 1.0)
-    cp("CLr", "CUr", cu(CR), cl(CR))
-    cp("CLv", "CUv", cu(CV), cl(CV))
+    for lo, hi, a in ((0, 2, "dV"), (3, 5, "a1"), (2, 3, "a2")):
+        ts("NI " + a, "CUv%d" % lo, T.CU[:, CV[0] + lo:CV[0] + hi], T.NI[:, lo:hi], 0.5, A.mult, col[a], A.add)
+    ts("l1s", "CUs", cu(CS), T.CL[:, 6:8], 24.0, A.add)
+    cp("CLr", "CUr", cu(CR), T.CL[:, 8:13])
     fill("Q30", T.Q3[:, 0:120:3], 0.0)
     fill("D0r", T.D0[:, SEG - 1:20 * SEG:SEG], BIG)
     fill("Mma", T.Mm[:, 0:192:8], 0.0, "Mm")
@@ -306,7 +309,7 @@ def rank_program(g, core, T, topo):
     aff("C1 CF", "C1", T.C1[:], T.C1[:], 1.0, col["m"])
     aff("xc CF", "xc", T.xc[:], T.xc[:], 1.0, col["m"])
     aff("CK", "CK", T.CK[:], T.CK[:], 1024.0, -LAST - 1.0)
-    aff("C1", "CZ", T.CZ[:], T.C1[:], 1024.0, 3072.0)
+    aff("C1", "CZ", T.CZ[:], T.C1[:], 1024.0, SHIFT - 1024.0)
     act("xc", "xcb", T.xcb[:], T.xc[:], scale=-BIG)
 
     def late_constants():
@@ -328,24 +331,23 @@ def rank_program(g, core, T, topo):
             for b in range(4):
                 mm(4 * h + b, "QE", 512 * e + 128 * b, x, at + H * h, H, "QE%d%d %s" % (e, b, R), start, stop)
         for e in range(2):
-            pick(win + PO + "ab"[e], "Go%d" % e, G, 640 * e + B0, QF, 0, T[PO][:, 20 * e:20 * e + 20])
+            pick(win + PO, "Go%d" % e, G, 640 * e + B0, QF, 0, T[PO][:, 20 * e:20 * e + 20])
             for h in range(2):
                 unpack(h, e, G, 640 * e + B0, "Go%dc Go%ds" % (e, e), e == 0, False)
-        tt("ne PN", "PZ", T.PZ[:, 0:40], T.ne[:], pn, A.mult)
-        ts("%sa %sb PA" % (PO, PO), "PAo", T.PA[:, 40 * u:40 * u + 40], T[PO][:, 0:40], 1.0, A.add)
+        tt("ne PN", "PS", T.PS[:], T.ne[:], pn, A.mult)
+        ts(PO, "PAo", T.PA[:, 40 * u:40 * u + 40], T[PO][:, 0:40], 1.0, A.add)
         for e in range(2):
-            aff("PZ g%d" % e, "PZ%d" % e, T.PZ[:, e:40:2], T.PZ[:, e:40:2], 1.0, col["g%d" % e])
-        act("PN", "S3p", T.S3[:, 2:120:3], pn)
-        spread1("PZ0 PZ1", "PZ", T.PZ, 40, 64)
-        pick(win + PP, "Gp0", G, Bp, QF, 0, T[PP][:, 0:20])
-        ts(PP + " PA", "PAp", T.PA[:, 40 - 40 * u:80 - 40 * u], T[PP][:], 1.0, A.add)
-        pick("Go0# Gp0# " + PO + "a", "B0", B, 0, G, 0, T[PO][:, 0:20])
+            aff("PS PZ g%d" % e, "PZ%d" % e, T.PZ[:, 32 * e:32 * e + 20], T.PS[:, 20 * e:20 * e + 20], 1.0, col["g%d" % e])
+        aff("PN", "S3p", T.S3[:, 2:120:3], pn, 1.0, -1.0 if t == 2 else 0.0)
+        spread1("PZ0 PZ1", "PZ", T.PZ, 52, 64)
+        for e in range(2):
+            pick(win + PP, "Gp%d" % e, G, 640 * e + Bp, QF, 0, T[PP][:, 20 * e:20 * e + 20])
         for h in range(2):
-            unpack(h, 0, B, 0, "B0c B0s", False, False)
-        pick(win + PP, "Gp1", G, 640 + Bp, QF, 0, T[PP][:, 20:40])
-        for h in range(2):
-            pick("Go1# Gp1# " + PO + "b", "B1%d" % h, B, C + H * h, G, 640, T[PO][:, 20 + 10 * h:30 + 10 * h])
-            unpack(h, 1, B, C, "B1%dc B1%ds" % (h, h), False, True)
+            for e in range(2):
+                at = 20 * e + 10 * h
+                pick("Go%d# Gp%d# %s" % (e, e, PO), "B%d%d" % (e, h), B, C * e + H * h, G, 640 * e, T[PO][:, at:at + 10])
+                unpack(h, e, B, C * e, "B%d%dc B%d%ds" % (e, h, e, h), False, e == 1)
+        ts(PP, "PAp", T.PA[:, 40 - 40 * u:80 - 40 * u], T[PP][:], 1.0, A.add)
         if t == 0:
             late_constants()
         for h in range(2):
@@ -356,7 +358,7 @@ def rank_program(g, core, T, topo):
                 else:
                     ts("ps%d QYpad" % k, "Y%d" % k, out, ps(k, H), 0.5, A.mult)
             quant(keys("Y%d", range(4 * h, 4 * h + 4)), "QY%d" % h, "QY", H * h, H * h + H, T.Yt[:, 4 * H * h:4 * H * (h + 1)])
-        spread2("PZ", T.PZ, 40, 64)
+        spread2("PZ", T.PZ, 52, 64)
         act(keys("PZ_%d", 4) + " CUt", "PT", T.PT[:], T.PZ[:].indirect(cu(CT)))
         for k in range(3):
             mm(k, "QY", 128 * k, "QAB", 0, 128, ("QY0 QY1" if k else "QY0") + " QABc QABs")
@@ -365,7 +367,6 @@ def rank_program(g, core, T, topo):
             tt("ps%d SL%d" % (k, k), "D%d" % k, T.D[:, 64 * k:64 * k + 64], ps(k, 64), T.SL[:, 64 * k:64 * k + 64], A.is_gt)
         for b in range(4):
             mm(4 + b, "QW", 128 * b, "QY", 0, C, "QW QW2 QY0 QY1")
-
 
         def relu(lo, hi):
             for b in range(lo, hi):
@@ -378,10 +379,10 @@ def rank_program(g, core, T, topo):
         if t == 1:
             quant("vin", "QV", "QV", 0, 128, T.vin[:])
         tt("SC PT VW", "VWs", T.VW[:, :, 0:8], T.SC[:, 7:192:8], T.PT[:, 0:24], A.add)
+        tt("SC G24", VV + "v", T[VV][:, 28 * u:28 * u + 24], T.SC[:, 7:192:8], T.G24[:], A.add)
         for k in range(3):
             scan("VWs", "SW%d" % k, T.SW[:, k, :], T.VW[:, k, :], T.VW[:, k, :], 0.0, A.max, A.max)
         top = T.SW[:, :, 39]
-        cp("VWs", VV + "v", T[VV][:, 28 * u:28 * u + 24], T.VW[:, :, 0:8])
         turn("SW0 SW1 SW2", "AR", T.AR[:], T.SW[:, :, 8:40])
         tt("SW0 SW1 SW2 CK sk", "sk0", T.sk[:, 0:3], top, T.CK[:, 3 * u:3 * u + 3], A.add)
         ts("SW0 SW1 SW2 sk", "sk1", T.sk[:, 4:7], top, LAST, A.is_le, NONE, A.mult)
@@ -412,15 +413,16 @@ def rank_program(g, core, T, topo):
         send(t, "am%d" % t, keys("MO%d", 4), MP, T[MP][:], mo)
         act("PAo PAp CUr", "VR", T.VR[:], T.PA[:].indirect(cu(CR)))
         spread1("%s %sv %sp" % (VV, VV, VV), VV, T[VV], 56, 56)
+        act("VR Tin Tin2", "Tr", T.Tin[:, 0:40, 1:6:3], T.VR[:])
         if t == 0:
             act("YR m6 hm", "YR", T.YR[:], T.YR[:], F.Identity, scale=col["m6"], bias=col["hm"])
         spread2(VV, T[VV], 56, 56)
-        k = keys(VV + "_%d", 4)
-        act(k + " CUv", "va", T.va[:], T[VV][:].indirect(cu(CV)), F.Abs, bias=-11263.5)
-        act(k + " CUv", "vh", T.vh[:], T[VV][:].indirect(cu(CV)))
-        act(k + " CUs", "SK", T.SK[:], T[VV][:].indirect(cu(CS)))
+        k = keys(VV + "_%d", 4) + " CUv0 CUv2 CUv3 CUs"
+        act(k, "va", T.va[:], T[VV][:].indirect(cu(CV)), F.Abs, scale=STILL, bias=-5 * 2048 * STILL)
+        act(k, "vh", T.vh[:], T[VV][:].indirect(cu(CV)), F.Relu, scale=1.0 / 2048, bias=-6.0)
+        act(k, "SK", T.SK[:], T[VV][:].indirect(cu(CS)))
         state(2)
-        tt("C1 VR", "dd", T.dd[:], T.VR[:], T.C1[:], A.subtract)
+        tt("C1 VR", "dd", T.dd[:], T.C1[:], T.VR[:], A.subtract)
         if t < 2:
             n = C * upper(t + 1)
             quant(keys("X%d", 4), "QF%d" % (t + 1), "QF%d" % (t + 1), n, n + C, T.Xt[:])
@@ -431,28 +433,21 @@ def rank_program(g, core, T, topo):
             dma("y", "out", "QX3", "", T.oc[:], T.QX3[:].bitcast(dt.uint8))
             for k in range(4):
                 dma("y", "out", "QX3", "", T.osc[4 * k:4 * k + 4, :], T.SQX3[32 * k:32 * k + 4, :])
-        ts("va", "vv", T.vv[:], T.va[:], 3072.0, A.is_ge)
-        ts("vh", "vh", T.vh[:], T.vh[:], LAST, A.is_ge)
+            act("ps4", "ys", T.ys[:], ps(4))
+            dma("y", "out", "ys", "", T.y[:], T.ys[:])
+        tt("va CZ Tin Tin2", "Tz", T.Tin[:, 0:40, 2:6:3], T.va[:], T.CZ[:], A.min)
+        tt("vh dd Tin Tin2", "Th", T.Tin[:, 0:40, 0:6:3], T.vh[:], T.dd[:], A.mult)
         for w in range(2):
             tt(keys("MO%d", 4) + " SK", "MQ%d" % w, T.MQ[:, 10 * w:10 * w + 10], T.MO[:, 20 * t + 10 * w:20 * t + 10 * w + 10],
                T.SK[:, 16 * w:16 * w + 10], A.min)
-        tt("vv CZ VF", "VFz", T.VF[:, 2:144:3], T.vv[:], T.CZ[:], A.mult)
-        tt("vh dd VF", "VFh", T.VF[:, 0:144:3], T.vh[:], T.dd[:], A.mult)
-        turn("VFz", "T1", T.T1[:], T.VF[:, 72 * u + 2:72 * u + 96:3])
-        tt("VR VFh", "VFg", T.VF[:, 1:144:3], T.VR[:], T.VF[:, 0:144:3], A.subtract)
+        turn("Tz", "T1", T.T1[:], T.Tin[:, 2 * b0:2 * b0 + 32:2, 2:6:3])
         for h in range(2):
             act("T1", "Z3%d" % h, T.Z3[:, h:4:2, :], T.T1[:])
-        for w in range(2):
-            for h in range(2):
-                act("VFz VFh VFg Tin Tin2", "Ta%d%d" % (w, h), T.Tin[:, 20 * w + h:20 * w + 20:2, 0:6], T.VF[:, 72 * w:72 * w + 60])
-        if t == 2:
-            act("ps4", "ys", T.ys[:], ps(4))
-            dma("y", "out", "ys", "", T.y[:], T.ys[:])
         tt("MQ0 MQ1 " + MP, "I1", T.I1[:], T.MQ[:, b0:b0 + 10], T[MP][:, b0:b0 + 10], A.min)
         for h in range(2):
             tt("MQ0 MQ1 Tin Tin2 " + MP, "Tk%d" % h, T.Tin[:, h:40:2, 6], T.MQ[:], T[MP][:], A.min)
         ts("I1", "I2", T.I2[:], T.I1[:], 1023, band)
-        turn("Tk0 Tk1 Tpad " + keys("Ta%d%d", 2, 2), "Tout", T.Tout[:], T.Tin[:])
+        turn("Tk0 Tk1 Tpad Tr Tz Th", "Tout", T.Tout[:], T.Tin[:, 0:42, :])
         for h in range(2):
             cp("I2", "OFF%d" % h, T.OFF[:, h:20:2], T.I2[:])
         turn("Z30 Z31", "ZT", T.ZT[:], T.Z3[:])
@@ -463,26 +458,27 @@ def rank_program(g, core, T, topo):
                T.YR[:, B0 + H * h:B0 + H * h + H], A.subtract)
         for h in range(2):
             turn("GG%d" % h, "ZZ%d" % h, T.ZZ[:, 10 * h:10 * h + 10, :], T.GG[:, H * h:H * h + H])
-        act("ZZ0 ZZ1", "S30", T.S3[:, 0:120:3], T.ZZ[:, :, 0:6:3])
         for e in range(2):
-            tt("ZZ0 ZZ1 ZO0 ZO1", "Q31%d" % e, T.Q3[:, 3 * e + 1:120:6], T.ZZ[:, :, 6], T.ZO[:, :, e], A.is_equal)
-            tt("ZZ0 ZZ1", "q2%d" % e, T.q2[:, e:40:2], T.ZZ[:, :, 6], T.ZZ[:, :, 3 * e + 2], A.is_equal)
-        tt("ZZ0 ZZ1 PN", "S31", T.S3[:, 1:120:3], T.ZZ[:, :, 1:6:3], pn, A.subtract)
-        tt("Q310 Q311 q20 q21", "Q32", T.Q3[:, 2:120:3], T.Q3[:, 1:120:3], T.q2[:], A.add)
-        scan("S30 S31 S3p Q30 Q32", "PN", T.PN[:], T.Q3[:], T.S3[:], 0.0, A.mult, A.add)
+            act("ZZ0 ZZ1", "S30%d" % e, T.S3[:, 60 * e:60 * e + 60:3], T.ZZ[:, :, 3 * e])
+            tt("ZZ0 ZZ1 ZO0 ZO1", "q1%d" % e, T.q1[:, 20 * e:20 * e + 20], T.ZZ[:, :, 6], T.ZO[:, :, e], A.is_equal)
+            tt("ZZ0 ZZ1", "Q31%d" % e, T.Q3[:, 60 * e + 1:60 * e + 60:3], T.ZZ[:, :, 6], T.ZZ[:, :, 3 * e + 2], A.is_equal)
+        for e in range(2):
+            tt("ZZ0 ZZ1 PN", "S31%d" % e, T.S3[:, 60 * e + 1:60 * e + 60:3], T.ZZ[:, :, 3 * e + 1], T.PN[:, 60 * e + 2:60 * e + 60:3],
+               A.subtract)
+        tt("Q310 Q311 q10 q11", "Q32", T.Q3[:, 2:120:3], T.Q3[:, 1:120:3], T.q1[:], A.add)
+        scan("S300 S301 S310 S311 S3p Q30 Q32", "PN", T.PN[:, 0:120], T.Q3[:], T.S3[:], 0.0, A.mult, A.add)
         if t < 2:
             o = "PO%d" % (t + 1)
-            for e in range(2):
-                ts("PN", o + "ab"[e], T[o][:, 20 * e:20 * e + 20], T.PN[:, 3 * e + 2:120:6], -1.0, A.add)
-            send(t + 1, "ap%d" % (t + 1), "%sa %sb" % (o, o), "PP%d" % (t + 1), T["PP%d" % (t + 1)][:], T[o][:])
+            ts("PN", o, T[o][:], pn, -1.0, A.add)
+            send(t + 1, "ap%d" % (t + 1), o, "PP%d" % (t + 1), T["PP%d" % (t + 1)][:], T[o][:])
             n = 40 * upper(t + 1)
             tt("PN YJ", "ne", T.ne[:], pn, T.YJ[:, n:n + 40], A.not_equal)
         else:
             for e in range(2):
-                ts("PN OI", "OI%d" % e, T.OI[:, 32 * e:32 * e + 20], T.PN[:, 3 * e + 2:120:6], -1.0, A.add)
-            turn("OI0 OI1", "OT", T.OT[:], T.OI[:])
+                turn("PN", "OT%d" % e, T.OT[:, 32 * e:32 * e + 32], T.PN[:, 60 * e + 2:60 * e + 98:3])
             for k in range(8):
-                dma("ys"[k % 2], "out2", "OT", "", T.ov[k, :], T.OT[32 * (k // 2):32 * (k // 2) + 20, 32 * (k % 2):32 * (k % 2) + 16])
+                dma("ys"[k % 2], "out2", "OT%d" % (k % 2), "", T.ov[k, :],
+                    T.OT[32 * (k // 2):32 * (k // 2) + 20, 32 * (k % 2):32 * (k % 2) + 16])
 
     for s, n in count.items():
         if seen.get(s, 0) < n:

@@ -6,14 +6,14 @@ CODE = "float8_e4m3fn_x4"
 SEG = 97
 BIG = 16384.0
 LAST = 14336.0
-NONE = 1048576.0 + 640.0
-SHIFT = 1048576 + 4096
-STILL = 460.0
-ON_V = 6
-SCANS = ((6, 10), (0, 6), (10, 17), (17, 20))
-COPY = ("vsvs", "svsv")
+NONE = 1048576.0
+SHIFT = 2097152
+STILL = 800.0
+ON_V = 7
+SCANS = ((0, 3), (7, 12), (3, 7), (12, 16), (16, 18), (18, 20))
+TAIL = "v0 s1 v2 s3 s4 q0 s5 v6 s7 q1"
 EARLY = 3
-XAT = (0, 1, 2, 2)
+GAPS = (2, 4, 4, 4, 2, 2, 2)
 
 SCRATCH = {}
 
@@ -25,24 +25,24 @@ def _buf(name, n, dtype, where="sbuf"):
 for _k in range(8):
     _buf("ps%d" % _k, 512, "float32", "psum")
 for _n, _w in (("xin", 1280), ("uin", 512), ("vin", 512), ("Xt", 1280), ("Yt", 1536), ("Z", 1040), ("D0", 20 * SEG), ("SO", 20 * SEG),
-               ("ST", 7 * SEG), ("D", 192), ("Mm", 192), ("SC", 192)):
+               ("ST", 5 * SEG), ("D", 216)):
     _buf(_n, _w, "bfloat16")
 for _n, _w in (("QF0", 640), ("QF1", 640), ("QF2", 640), ("G0", 1280), ("G1", 1280), ("G2", 1280), ("B0", 640), ("B1", 640), ("B2", 640),
-               ("QX3", C), ("QY", 384), ("QE", 1024), ("QW", 512), ("QU", 128), ("QAB", 128), ("QV", 128)):
+               ("QX3", C), ("QY", 384), ("QE", 1024), ("QW", 512), ("QU", 128), ("QAB", 160), ("QV", 128)):
     _buf(_n, _w, CODE)
     _buf("S" + _n, _w, "uint8")
-for _n, _w in (("TB", 1280), ("SL", 192), ("PT", 32), ("VR", 80), ("G24", 24), ("VW", [3, 40]), ("SW", [3, 40]), ("AR", 96), ("KK", 20),
-               ("M1", 20), ("SK", 32), ("sk", 8), ("MO", 60), ("MQ", 20), ("MP0", 20), ("MP1", 20), ("MP2", 20),
-               ("VV0", 224), ("VV1", 224), ("VV2", 224), ("Tin", [52, 16]), ("Tout", 672), ("GG", C), ("ZZ", [20, 16]),
+for _n, _w in (("TB", 1280), ("SL", 216), ("Mm", 288), ("SC", 1080), ("VR", 80), ("SW", [4, 40]), ("AR", 96), ("KK", 20),
+               ("M1", 20), ("SK", 32), ("sk", 64), ("MO", 60), ("MQ", 20), ("MP0", 20), ("MP1", 20), ("MP2", 20),
+               ("VV0", 224), ("VV1", 224), ("VV2", 224), ("Tin", [52, 16]), ("Tout", 640), ("GG", C), ("ZZ", [20, 16]),
                ("va", 80), ("vh", 80), ("dd", 80), ("T1", 32), ("Z3", [4, 16]), ("ZT", 64),
                ("ZO", [20, 2]), ("q1", 40), ("Q3", 120), ("S3", 120), ("PN", 160),
                ("ne", 40), ("PS", 40), ("PZ", 256), ("PA", 80), ("OT", 64), ("ys", C),
-               ("idm", 128), ("CF", 36), ("NI", 8), ("NJ", 8), ("t8", 8), ("CL", 16), ("l1", 8), ("xc", 20), ("xcb", 20),
-               ("YJ", 80), ("YR", 640), ("C1", 80), ("CZ", 80), ("CK", 6)):
+               ("idm", 128), ("CF", 36), ("NI", 8), ("NJ", 8), ("t8", 8), ("CL", 32), ("l1", 8), ("xc", 20), ("xcb", 20),
+               ("YJ", 80), ("YR", 640), ("C1", 80), ("CZ", 80), ("CK", 32)):
     _buf(_n, _w, "float32")
-for _n, _w in (("Vi", 60), ("PI", 2), ("CI", 16), ("I1", 10), ("I2", 10)):
+for _n, _w in (("Vi", 20), ("Vp", 20), ("PI", 1), ("CI", 16), ("I1", 10), ("I2", 10), ("II", 30)):
     _buf(_n, _w, "int32")
-for _n, _w in (("CU", 24), ("CP", 4), ("OFF", 20), ("PO0", 48), ("PO1", 40), ("PO2", 40), ("PP0", 40), ("PP1", 40), ("PP2", 40)):
+for _n, _w in (("CU", 26), ("OFF", 20), ("PO0", 40), ("PO1", 40), ("PO2", 40), ("PP0", 40), ("PP1", 40), ("PP2", 40)):
     _buf(_n, _w, "uint16")
 
 SEMAPHORES = ["cv", "cs", "ct", "cg", "sent", "lx0", "lx1", "lg", "lu", "lw", "lv", "out", "out2"]
@@ -136,8 +136,8 @@ def rank_program(g, core, T, topo):
     def turn(R, W, out, a):
         op("v", R, W, V.transpose, out, a)
 
-    def fill(W, ap, c, R=""):
-        op("v", R, W, V.memset, ap, c)
+    def fill(W, ap, c):
+        op("v", "", W, V.memset, ap, c)
 
     def act(R, W, out, a, f=F.Copy, **kw):
         op("s", R, W, S.activation, out, a, f, **kw)
@@ -145,8 +145,8 @@ def rank_program(g, core, T, topo):
     def aff(R, W, out, a, scale, bias):
         act(R, W, out, a, F.Identity, scale=scale, bias=bias)
 
-    def sfill(W, ap, n, c):
-        aff("xin0", W, ap, T.xin[:, 0:n], 0.0, c)
+    def sfill(W, ap, n, c, R=""):
+        aff("idm " + R, W, ap, T.idm[:, 0:n], 0.0, c)
 
     def quant(R, W, name, lo, hi, tile):
         op("v", R, W, V.quantize_mx, T[name][:, lo:hi], T["S" + name][:, lo:hi], tile)
@@ -188,11 +188,12 @@ def rank_program(g, core, T, topo):
                 buf[32 * a:32 * a + 32, 0:pitch + n])
 
     shr, band = A.logical_shift_right, A.bitwise_and
-    DIGITS = (("h16", 0, 16), ("i", 0, 15), ("i8", 0, 8), ("k7", 0, 7), ("r32", 0, 96), ("e", 0, 1), ("m", 0, 31), ("p112", 0, 112),
-              ("k0", 1, 1), ("r0", 5, 1), ("k1", 2, 1), ("r1", 6, 1), ("k8", 0, 7), ("q4", 2, 3), ("i3", 3, 1))
-    MORE = ("lowh", "h", "even", "x0", "sg", "x1", "sh", "x2", "x3", "dR", "dT", "dV", "dS", "a1", "a2", "end", "g0", "g1", "m6", "hm")
+    DIGITS = (("h16", 0, 16), ("i", 0, 15), ("r32", 0, 96), ("e", 0, 1), ("k0", 1, 1), ("r0", 5, 1), ("k1", 2, 1), ("r1", 6, 1),
+              ("i3", 3, 1))
+    MORE = ("i8", "m", "q4", "h", "even", "x0", "sg", "x1", "sh", "x2", "x3", "dR", "dT", "dV", "dS", "a0", "a1", "a2", "a3", "end",
+            "g0", "g1", "m6", "hm", "s0")
     col = {n: T.CF[:, k:k + 1] for k, n in enumerate([d[0] for d in DIGITS] + list(MORE))}
-    CAB, CR, CT, CV, CS = (0, 8), (8, 13), (14, 16), (16, 21), (22, 24)
+    CAB, CR, CT, CV, CS = (0, 10), (10, 15), (16, 18), (18, 23), (24, 26)
 
     def cu(c):
         return T.CU[:, c[0]:c[1]]
@@ -204,121 +205,158 @@ def rank_program(g, core, T, topo):
         if hi == C:
             send(t, "ax%d" % t, R, q + "p", T["S" + q][:, at:at + C], T["S" + q][:, at:at + C])
 
+    def tile_e(par, b):
+        at = 512 * par + 128 * b
+        quant("Z%d" % par, "QE%d%d" % (par, b), "QE", at, at + 128, T.Z[:, 520 * par + 3 - b:520 * par + 515 - b])
+
+    dma("s", "lg", "", "Vi", T.Vi[:], T.vg[:])
     dma("y", "lx0", "", "xin0", T.xin[:, 0:4 * H], T.x[:, 0:4 * H])
     dma("y", "lx1", "", "xin1", T.xin[:, 4 * H:4 * C], T.x[:, 4 * H:4 * C])
-    dma("y", "lg", "", "Vi", T.Vi[:, 20:40], T.vg[:])
-    dma("y", "lg", "", "Vi1", T.Vi[16:128, 0:20], T.vg[0:112, :])
-    dma("y", "lg", "", "Vi2", T.Vi[0:112, 40:60], T.vg[16:128, :])
     dma("y", "lu", "", "uin", T.uin[:], T.u[:])
-
-    iota("PI", T.PI[:], [[1, 2]], 1)
+    iota("PI", T.PI[:], [[0, 1]], 1)
     iota("NI", T.NI[:], [[16, 8]], 0)
     iota("idm", T.idm[:], [[-1, 128]], 1)
+    send(0, "ap0", "Vi", "Vp", T.Vp[:], T.Vi[:])
+
+    def both_halves(src, dst):
+        yield cp(src + " OT", "OTa", T.OT[:, 0:20], T[src][:])
+        yield turn("OTa", "T1", T.T1[:], T.OT[:, 0:32])
+        for h in range(2):
+            act("T1", "Z3%d" % h, T.Z3[:, h:4:2, :], T.T1[:])
+        yield
+        yield turn("Z30 Z31", "ZT", T.ZT[:], T.Z3[:])
+        for e in range(2):
+            cp("ZT", dst + "ab"[e], T[dst][:, 20 * e:20 * e + 20], T.ZT[:, 32 * e:32 * e + 20])
+        wrote[dst] = wrote[dst + "b"]
+        yield
+    mine, theirs = both_halves("Vi", "PO0"), both_halves("Vp", "PP0")
+
     fill("Z", T.Z[:], 0.0)
+    fill("OT", T.OT[:, 20:32], 0.0)
     for k, (n, sh, m) in enumerate(DIGITS):
-        ts("PI", "CI%d" % k, T.CI[:, k:k + 1], T.PI[:, 1:2] if n == "k8" else T.PI[:, 0:1], sh, shr, m, band)
-    cp(keys("CI%d", 15), "CF", T.CF[:, 0:15], T.CI[:, 0:15])
+        ts("PI", "CI%d" % k, T.CI[:, k:k + 1], T.PI[:], sh, shr, m, band)
     fill("Ypad", T.Yt[:, 1024:1536], 0.0)
-    ts("NI CF", "NJ", T.NJ[:], T.NI[:], col["i"], A.add)
-    ts("CF", "lowh", col["lowh"], col["h16"], -1.25, A.mult, 20.0, A.add)
-    ts("CF", "h", col["h"], col["h16"], 0.0625, A.mult)
-    ts("CF", "even", col["even"], col["h16"], 0.0, A.is_equal)
+    cp(keys("CI%d", len(DIGITS)), "CF", T.CF[:, 0:len(DIGITS)], T.CI[:, 0:len(DIGITS)])
+    next(mine)
     at0 = C * upper(0)
     quant("xin0", "QF0h", "QF0", at0, at0 + H, T.xin[:, 0:4 * H])
     send_state(0, 0, H, "QF0h")
-    ts("NJ lowh", "CP", T.CP[:, 0:3], T.NJ[:, 0:3], 39.0, A.min, col["lowh"], A.add)
+    next(mine)
+    ts("NI CF", "NJ", T.NJ[:], T.NI[:], col["i"], A.add)
+    ts("CF", "h", col["h"], col["h16"], 0.0625, A.mult)
+    ts("CF", "even", col["even"], col["h16"], 0.0, A.is_equal)
+    ts("CF", "x0", col["x0"], col["k0"], col["r0"], A.not_equal, 2.0, A.mult)
+    ts("NI CF", "t8", T.t8[:], T.NI[:], 0.125, A.mult, col["i3"], A.add)
+    next(mine)
+    quant("xin1", "QF0", "QF0", at0 + H, at0 + C, T.xin[:, 4 * H:4 * C])
+    send_state(0, H, C, "QF0 QF0h")
+    Ii, Is, I7, Ia, Ib = [T.II[:, 6 * k:6 * k + 5] for k in range(5)]
+    ts("NJ", "If", T.CL[:, 16:21], T.NJ[:, 0:5], -4.0, A.add, 1.0 / 9, A.mult)
     for par in range(2):
         ts("idm Z h even", "Z%d" % par, T.Z[:, 520 * par + 3:520 * par + 515:4], T.idm[:], 0.0, A.is_equal,
            col["h" if par else "even"], A.mult)
-    quant("xin1", "QF0", "QF0", at0 + H, at0 + C, T.xin[:, 4 * H:4 * C])
-    send_state(0, H, C, "QF0 QF0h")
-    quant("Ypad", "QYpad", "QY", 256, 384, T.Yt[:, 1024:1536])
-    for par in range(2):
-        for b in range(4):
-            at = 512 * par + 128 * b
-            quant("Z%d" % par, "QE%d%d" % (par, b), "QE", at, at + 128, T.Z[:, 520 * par + 3 - b:520 * par + 515 - b])
-        if par == 0:
-            cp("Vi Vi1 Vi2 CP", "PO0", T.PO0[:], T.Vi[:].indirect(T.CP[:, 0:3]))
-            send(0, "ap0", "PO0", "PP0", T.PP0[:], T.PO0[:, 0:40])
+    next(mine)
+    cp("If", "Ii", Ii, T.CL[:, 16:21])
+    ts("CF x0", "sg", col["sg"], col["k1"], col["r1"], A.not_equal, col["x0"], A.add)
+    iota("YJ", T.YJ[:], [[C, 2], [0, 2], [16, 20]], 0, 1)
+    iota("PZ", T.PZ[:], [[0, 256]], 0, -8)
+    tile_e(0, 0)
+    ts("Ii", "Im", T.CL[:, 24:29], Ii, -9.0, A.mult)
+    next(mine)
+    tile_e(0, 1)
+    tt("Im NJ", "Is", Is, T.CL[:, 24:29], T.NJ[:, 0:5], A.add)
+    pn = T.PN[:, 2:120:3]
+    ts("PO0", "PN", pn, T.PO0[:, 0:40], 1.0, A.add)
+    tile_e(0, 2)
+    tile_e(0, 3)
+    ts("Is", "I7", I7, Is, 7.0, A.add)
+    ts("Is", "Ib", Ib, Is, 7, band)
+    ts("YJ CF", "YJ", T.YJ[:], T.YJ[:], col["i"], A.add)
+    tile_e(1, 0)
+    next(theirs)
+    ts("I7", "Ia", Ia, I7, 7, band)
+    tt("Ii Ib", "Ib", Ib, Ii, Ib, A.max)
+    tt("PN YJ", "ne", T.ne[:], pn, T.YJ[:, 40 * upper(0):40 * upper(0) + 40], A.not_equal)
+    tile_e(1, 1)
+    next(theirs)
+    tt("Ii Ia", "Ia", Ia, Ii, Ia, A.min)
+    ts("Ib", "CAb", T.CU[:, 5:10], Ib, 7.0, A.min, 16.0, A.mult)
+    tt("ne PN", "PS", T.PS[:], T.ne[:], pn, A.mult)
+    quant("uin", "QU", "QU", 0, 128, T.uin[:])
+    ts("Ia", "CAa", T.CU[:, 0:5], Ia, 16.0, A.mult)
+    tile_e(1, 2)
+    tile_e(1, 3)
     dma("y", "lw", "QF0p", "QW", T.QW[:].bitcast(dt.uint8), T.wc[:])
     dma("y", "lw", "", "QW2", T.SQW[:], T.ws[:])
     dma("y", "lv", "", "vin", T.vin[:], T.v[:])
 
-    iota("YJ", T.YJ[:], [[C, 2], [0, 2], [16, 20]], 0, 1)
+    iota("Mm", T.Mm[:], [[0, 288]], 0, 1)
+    iota("SC", T.SC[:], [[0, 1080]], 0)
     iota("xc", T.xc[:], [[32, 20]], 0, int(LAST) + 1)
+    iota("CK", T.CK[:], [[C, 2], [32, 16]], 0)
+    iota("ST", T.ST[:], [[0, 5 * SEG]], 0, 1)
     iota("C1", T.C1[:], [[32, 20], [0, 4]], 0, 1)
-    iota("CK", T.CK[:], [[C, 2], [128, 3]], 1)
-    iota("G24", T.G24[:], [[0, 3], [2048, 8]], 0)
-    iota("ST", T.ST[:], [[0, 7 * SEG]], 0, 1)
+    iota("Tin", T.Tin[:], [[0, 832]], 0, -1)
     iota("YR", T.YR[:], [[32, 20], [0, 2], [1, 16]], 0, -SHIFT)
+    aff("CF h", "dT", col["dT"], col["r32"], 0.0625, col["h"])
+    for e in range(2):
+        aff("CF", "g%d" % e, col["g%d" % e], col["r32"], -0.0625, 7.0 - e - 1.0 / 2048)
+    act("CF", "s0", col["s0"], col["r32"], F.Sign, bias=-1.0)
     aff("h CF", "dR", col["dR"], col["e"], 20.0, col["h"])
-    aff("CF", "dT", col["dT"], col["p112"], 0.0625, 0.0)
     aff("CF", "dV", col["dV"], col["r32"], 0.0625, col["e"])
     aff("CF", "end", col["end"], col["r32"], -1.0, -127.0)
-    for e in range(2):
-        aff("CF", "g%d" % e, col["g%d" % e], col["r32"], 128.0, 2048.0 * e)
-    sfill("PN0", T.PN[:], 160, 0.0)
-    aff("dR CF", "dR", col["dR"], col["q4"], 2.0, col["dR"])
+    aff("CF", "q4", col["q4"], col["i3"], 2.0, col["k1"])
+    aff("CF", "m", col["m"], col["h16"], 1.0, col["i"])
+    aff("CF", "i8", col["i8"], col["i3"], 8.0, 0.0)
     aff("dT CF", "dT", col["dT"], col["e"], 32.0, col["dT"])
-    sfill("VW", T.VW[:], 120, 0.0)
-    sfill("sk", T.sk[:], 8, 0.0)
-    sfill("PZ", T.PZ[:], 256, 0.0)
-    sfill("Tin", T.Tin[:, 0:26, :], 416, -1.0)
-    sfill("Tin2", T.Tin[:, 26:52, :], 416, -1.0)
-    ts("CF", "x0", col["x0"], col["k0"], col["r0"], A.not_equal, 2.0, A.mult)
-    ts("CF", "x1", col["x1"], col["e"], col["r0"], A.not_equal, 2.0, A.mult)
-    ts("CF", "x2", col["x2"], col["k1"], col["r0"], A.not_equal, 112.0, A.mult)
-    ts("CF", "x3", col["x3"], col["i3"], col["r1"], A.not_equal, 56.0, A.mult)
-    ts("NI CF", "t8", T.t8[:], T.NI[:], col["i8"], A.add, 0.125, A.mult)
-    ts("NJ", "l1", T.l1[:, 0:5], T.NJ[:, 0:5], 40.0, A.is_ge, 20.0, A.mult)
-    ts("CF", "m6", col["m6"], col["i"], 6.0, A.is_equal)
-    ts("CF x0", "sg", col["sg"], col["k1"], col["r1"], A.not_equal, col["x0"], A.add)
-    ts("CF x1", "sh", col["sh"], col["k0"], col["r1"], A.not_equal, col["x1"], A.add)
-    ts("x2 x3 dV", "dV", col["dV"], col["x2"], col["x3"], A.add, col["dV"], A.add)
-    ts("x3 CF", "a1", col["a1"], col["x3"], -2.0, A.mult, col["i8"], A.add)
-    ts("t8 CF", "CAa", T.CU[:, 0:4], T.t8[:, 0:4], col["k8"], A.max, 16.0, A.mult)
-    ts("t8 CF", "CAb", T.CU[:, 4:8], T.t8[:, 0:4], col["k7"], A.min, 16.0, A.mult)
-    ts("CF m6", "hm", col["hm"], col["h16"], col["m6"], A.mult)
+    aff("g0 s0", "g0", col["g0"], col["g0"], col["s0"], 0.0)
+    sfill("SW0", T.SW[:, 3, 39:40], 1, 0.0)
+    aff("dR q4", "dR", col["dR"], col["q4"], 2.0, col["dR"])
+    sfill("Q30", T.Q3[:, 0:120:3], 40, 0.0)
+    sfill("D0r", T.D0[:, SEG - 1:20 * SEG:SEG], 20, BIG)
+    sfill("PNpad", T.PN[:, 120:160], 40, 0.0)
+    aff("s0", "s0", col["s0"], col["s0"], 1.0 / 2048, 0.0)
     aff("sg dT", "dT", col["dT"], col["sg"], 64.0, col["dT"])
-    aff("sh CF", "dS", col["dS"], col["sh"], 56.0, col["q4"])
     aff("NI dR", "l1r", T.CL[:, 0:5], T.NI[:, 0:5], 0.5, col["dR"])
-    quant("uin", "QU", "QU", 0, 128, T.uin[:])
-    ts("a1 CF", "a2", col["a2"], col["a1"], 60.0, A.add, col["i3"], A.mult)
-    ts("a1 dV", "a1", col["a1"], col["a1"], 60.0, A.add, col["dV"], A.add)
-    ts("YJ CF", "YJ", T.YJ[:], T.YJ[:], col["i"], A.add)
-    ts("PO0 PN0", "PN", T.PN[:, 2:120:3], T.PO0[:, 0:40], 1.0, A.add)
-    cp("QU CAa CAb", "QABc", words(T.QAB[:]), words(T.QU[:]).indirect(cu(CAB)))
+    next(theirs)
     act("QU CAa CAb", "QABs", T.SQAB[:], T.SQU[:].indirect(cu(CAB)))
-    ts("a2 dV", "a2", col["a2"], col["a2"], col["dV"], A.add)
+    next(theirs)
     ts("t8 dT", "CUt", cu(CT), T.t8[:, 0:2], 8.0, A.mult, col["dT"], A.add)
-    ts("NI dS", "l1s", T.CL[:, 6:8], T.NI[:, 0:2], 1.75, A.mult, col["dS"], A.add)
-    tt("l1r l1", "CLr", T.CL[:, 8:13], T.CL[:, 0:5], T.l1[:, 0:5], A.add)
-    fill("Mm", T.Mm[:], 1.0)
-    for lo, hi, a in ((0, 2, "dV"), (3, 5, "a1"), (2, 3, "a2")):
-        ts("NI " + a, "CUv%d" % lo, T.CU[:, CV[0] + lo:CV[0] + hi], T.NI[:, lo:hi], 0.5, A.mult, col[a], A.add)
-    ts("l1s", "CUs", cu(CS), T.CL[:, 6:8], 24.0, A.add)
-    cp("CLr", "CUr", cu(CR), T.CL[:, 8:13])
-    fill("Q30", T.Q3[:, 0:120:3], 0.0)
-    fill("D0r", T.D0[:, SEG - 1:20 * SEG:SEG], BIG)
-    fill("Mma", T.Mm[:, 0:192:8], 0.0, "Mm")
-    fill("Mmb", T.Mm[:, 7:192:8], 2048.0, "Mm")
-    for k in range(3):
-        fill("Mm%d" % k, T.Mm[:, 64 * k + 9:64 * k + 63:9], -1.0, "Mm")
-    fill("Tpad", T.Tin[:, 40:42, 6], 0.5, "Tin2")
-    fill("Mmb", T.Mm[:, 63:192:64], -2048.0)
-    aff("C1 CF", "C1", T.C1[:], T.C1[:], 1.0, col["m"])
-    aff("xc CF", "xc", T.xc[:], T.xc[:], 1.0, col["m"])
-    aff("CK", "CK", T.CK[:], T.CK[:], 1024.0, -LAST - 1.0)
-    aff("C1", "CZ", T.CZ[:], T.C1[:], 1024.0, SHIFT - 1024.0)
-    act("xc", "xcb", T.xcb[:], T.xc[:], scale=-BIG)
+    quant("Ypad", "QYpad", "QY", 256, 384, T.Yt[:, 1024:1536])
+    next(theirs)
 
-    def late_constants():
-        for k, c in ((31, 97.0), (63, 97.0), (96, -4096.0)):
-            fill("ST%d" % k, T.ST[:, k:7 * SEG:SEG], c, "ST")
-        ts("ST end", "ST95", T.ST[:, 95:7 * SEG:SEG], T.ST[:, 95:7 * SEG:SEG], col["end"], A.mult)
+    def multipliers():
+        sfill("Mma", T.Mm[:, 0:216:9], 24, 0.0, "Mm")
+        sfill("Mmb", T.Mm[:, 8:216:9], 24, -2048.0, "Mm")
+        for k in range(3):
+            sfill("Mm%d" % k, T.Mm[:, 72 * k + 11:72 * k + 62:10], 6, -1.0, "Mm")
+        sfill("Mmb", T.Mm[:, 71:216:72], 3, 2048.0)
 
-    pn = T.PN[:, 2:120:3]
-    tt("PN YJ", "ne", T.ne[:], pn, T.YJ[:, 40 * upper(0):40 * upper(0) + 40], A.not_equal)
+    def lists_of_the_table():
+        yield ts("CF", "x1", col["x1"], col["e"], col["r0"], A.not_equal, 2.0, A.mult)
+        yield ts("CF", "x2", col["x2"], col["k1"], col["r0"], A.not_equal, 112.0, A.mult)
+        yield ts("CF", "x3", col["x3"], col["i3"], col["r1"], A.not_equal, 56.0, A.mult)
+        yield ts("NJ", "l1", T.l1[:, 0:5], T.NJ[:, 0:5], 40.0, A.is_ge, 20.0, A.mult)
+        yield ts("CF", "m6", col["m6"], col["i"], 6.0, A.is_equal)
+        yield ts("CF x1", "sh", col["sh"], col["k0"], col["r1"], A.not_equal, col["x1"], A.add)
+        yield ts("x2 x3 dV", "a0", col["a0"], col["x2"], col["x3"], A.add, col["dV"], A.add)
+        yield ts("x3 i8", "a3", col["a3"], col["x3"], -2.0, A.mult, col["i8"], A.add)
+        yield tt("l1r l1", "CLr", T.CL[:, 8:13], T.CL[:, 0:5], T.l1[:, 0:5], A.add)
+        yield ts("CF m6", "hm", col["hm"], col["h16"], col["m6"], A.mult)
+        yield ts("sh q4", "dS", col["dS"], col["sh"], 56.0, A.mult, col["q4"], A.add)
+        yield ts("a3 CF", "a2", col["a2"], col["a3"], 60.0, A.add, col["i3"], A.mult)
+        yield ts("a3 a0", "a1", col["a1"], col["a3"], 60.0, A.add, col["a0"], A.add)
+        yield cp("CLr", "CUr", cu(CR), T.CL[:, 8:13])
+        yield ts("NI dS", "l1s", T.CL[:, 6:8], T.NI[:, 0:2], 1.75, A.mult, col["dS"], A.add)
+        yield ts("a2 a0", "a2", col["a2"], col["a2"], col["a0"], A.add)
+        for lo, hi, a in ((0, 2, "a0"), (3, 5, "a1"), (2, 3, "a2")):
+            yield ts("NI " + a, "CUv%d" % lo, T.CU[:, CV[0] + lo:CV[0] + hi], T.NI[:, lo:hi], 0.5, A.mult, col[a], A.add)
+        yield ts("l1s", "CUs", cu(CS), T.CL[:, 6:8], 24.0, A.add)
+    late = lists_of_the_table()
+
+    def gap(k):
+        for _ in range(GAPS[k]):
+            next(late, None)
 
     for t in range(3):
         u = upper(t)
@@ -330,16 +368,24 @@ def rank_program(g, core, T, topo):
         def unpack(h, e, x, at, R, start, stop):
             for b in range(4):
                 mm(4 * h + b, "QE", 512 * e + 128 * b, x, at + H * h, H, "QE%d%d %s" % (e, b, R), start, stop)
+
+        def marked():
+            for e in range(2):
+                aff("PS PZ s0 g%d" % e, "PZ%d" % e, T.PZ[:, 32 * e:32 * e + 20], T.PS[:, 20 * e:20 * e + 20],
+                    1.0 / 2048 if e else col["s0"], col["g%d" % e])
+            aff("PN", "S3p", T.S3[:, 2:120:3], pn, 1.0, -1.0 if t == 2 else 0.0)
+        if t == 0:
+            marked()
+            gap(6)
         for e in range(2):
             pick(win + PO, "Go%d" % e, G, 640 * e + B0, QF, 0, T[PO][:, 20 * e:20 * e + 20])
             for h in range(2):
                 unpack(h, e, G, 640 * e + B0, "Go%dc Go%ds" % (e, e), e == 0, False)
-        tt("ne PN", "PS", T.PS[:], T.ne[:], pn, A.mult)
+            if e == 0 and t:
+                tt("ne PN", "PS", T.PS[:], T.ne[:], pn, A.mult)
+        if t:
+            marked()
         ts(PO, "PAo", T.PA[:, 40 * u:40 * u + 40], T[PO][:, 0:40], 1.0, A.add)
-        for e in range(2):
-            aff("PS PZ g%d" % e, "PZ%d" % e, T.PZ[:, 32 * e:32 * e + 20], T.PS[:, 20 * e:20 * e + 20], 1.0, col["g%d" % e])
-        aff("PN", "S3p", T.S3[:, 2:120:3], pn, 1.0, -1.0 if t == 2 else 0.0)
-        spread1("PZ0 PZ1", "PZ", T.PZ, 52, 64)
         for e in range(2):
             pick(win + PP, "Gp%d" % e, G, 640 * e + Bp, QF, 0, T[PP][:, 20 * e:20 * e + 20])
         for h in range(2):
@@ -347,24 +393,53 @@ def rank_program(g, core, T, topo):
                 at = 20 * e + 10 * h
                 pick("Go%d# Gp%d# %s" % (e, e, PO), "B%d%d" % (e, h), B, C * e + H * h, G, 640 * e, T[PO][:, at:at + 10])
                 unpack(h, e, B, C * e, "B%d%dc B%d%ds" % (e, h, e, h), False, e == 1)
+        spread1("PZ0 PZ1", "PZ", T.PZ, 52, 64)
         ts(PP, "PAp", T.PA[:, 40 - 40 * u:80 - 40 * u], T[PP][:], 1.0, A.add)
         if t == 0:
-            late_constants()
-        for h in range(2):
-            for b in range(4):
-                k, out = 4 * h + b, T.Yt[:, 4 * H * h + b:4 * H * (h + 1):4]
-                if COPY[h][b] == "s":
-                    act("ps%d QYpad" % k, "Y%d" % k, out, ps(k, H), scale=0.5)
-                else:
-                    ts("ps%d QYpad" % k, "Y%d" % k, out, ps(k, H), 0.5, A.mult)
-            quant(keys("Y%d", range(4 * h, 4 * h + 4)), "QY%d" % h, "QY", H * h, H * h + H, T.Yt[:, 4 * H * h:4 * H * (h + 1)])
+            cp("QU CAa CAb", "QABc", words(T.QAB[:]), words(T.QU[:]).indirect(cu(CAB)))
+        gap(0)
+        for step in TAIL.split():
+            k = int(step[1])
+            h, b = divmod(k, 4)
+            if step[0] == "q":
+                gap(1 + k)
+                quant(keys("Y%d", range(4 * k, 4 * k + 4)), "QY%d" % k, "QY", H * k, H * k + H, T.Yt[:, 4 * H * k:4 * H * (k + 1)])
+            elif step[0] == "s":
+                act("ps%d QYpad" % k, "Y%d" % k, T.Yt[:, 4 * H * h + b:4 * H * (h + 1):4], ps(k, H), scale=0.5)
+            else:
+                ts("ps%d QYpad" % k, "Y%d" % k, T.Yt[:, 4 * H * h + b:4 * H * (h + 1):4], ps(k, H), 0.5, A.mult)
+        gap(3)
         spread2("PZ", T.PZ, 52, 64)
-        act(keys("PZ_%d", 4) + " CUt", "PT", T.PT[:], T.PZ[:].indirect(cu(CT)))
         for k in range(3):
-            mm(k, "QY", 128 * k, "QAB", 0, 128, ("QY0 QY1" if k else "QY0") + " QABc QABs")
-            act("ps%d" % k, "SL%d" % k, T.SL[:, 64 * k:64 * k + 64], T["ps%d" % k][:, 64:128])
-        for k in range(3):
-            tt("ps%d SL%d" % (k, k), "D%d" % k, T.D[:, 64 * k:64 * k + 64], ps(k, 64), T.SL[:, 64 * k:64 * k + 64], A.is_gt)
+            mm(k, "QY", 128 * k, "QAB", 0, 160, ("QY0 QY1" if k else "QY0") + " QABc QABs")
+
+        def other_side(k):
+            (cp if k == 2 else act)("ps%d" % k, "SL%d" % k, T.SL[:, 72 * k:72 * k + 72], T["ps%d" % k][:, 80:152])
+
+        def compare(k):
+            tt("ps%d SL%d" % (k, k), "D%d" % k, T.D[:, 72 * k:72 * k + 72], ps(k, 72), T.SL[:, 72 * k:72 * k + 72], A.is_ge)
+
+        def places(k):
+            scan("D%d PT SC Mma Mmb Mm%d" % (k, k), "SC%d" % k, T.SC[:, 360 * k:360 * k + 72], T.Mm[:, 72 * k:72 * k + 72],
+                 T.D[:, 72 * k:72 * k + 72], 0.0, A.mult, A.add)
+
+        def largest(k):
+            v = T.SC[:, 360 * k + 8:360 * k + 360:9]
+            scan("SC%d" % k, "SW%d" % k, T.SW[:, k, :], v, v, 0.0, A.max, A.max)
+        other_side(0)
+        if t == 0:
+            multipliers()
+        act(keys("PZ_%d", 4) + " CUt Mm", "PT", T.Mm[:, 1:288:9], T.PZ[:].indirect(cu(CT)))
+        for f, k in ((compare, 0), (other_side, 1), (other_side, 2), (places, 0), (compare, 1), (compare, 2), (largest, 0),
+                     (places, 1), (places, 2)):
+            f(k)
+        if t == 1:
+            quant("vin", "QV", "QV", 0, 128, T.vin[:])
+        gap(4)
+        largest(1)
+        largest(2)
+        if t == 0:
+            aff("xc m", "xc", T.xc[:], T.xc[:], 1.0, col["m"])
         for b in range(4):
             mm(4 + b, "QW", 128 * b, "QY", 0, C, "QW QW2 QY0 QY1")
 
@@ -372,57 +447,61 @@ def rank_program(g, core, T, topo):
             for b in range(lo, hi):
                 act("ps%d" % (4 + b), "TB%d" % b, T.TB[:, C * b:C * b + C], ps(4 + b), F.Relu, scale=0.03125)
         relu(0, EARLY)
+        if t == 0:
+            act("xc", "xcb", T.xcb[:], T.xc[:], scale=-BIG)
+            for k, c in ((31, 97.0), (63, 97.0), (96, -4096.0)):
+                sfill("ST%d" % k, T.ST[:, k:5 * SEG:SEG], 5, c, "ST")
+            aff("ST end", "ST95", T.ST[:, 95:5 * SEG:SEG], T.ST[:, 95:5 * SEG:SEG], col["end"], 0.0)
         for b in range(4):
             for e in range(2):
                 mm((3 + b) % 4, "QE", 512 * e + 128 * b, QF, B0, C, "QE%d%d %s %sh" % (e, b, QF, QF), e == 0, e == 1)
-        scan("D0 D1 D2 Mma Mmb Mm0 Mm1 Mm2", "SC", T.SC[:], T.Mm[:], T.D[:], 0.0, A.mult, A.add)
-        if t == 1:
-            quant("vin", "QV", "QV", 0, 128, T.vin[:])
-        tt("SC PT VW", "VWs", T.VW[:, :, 0:8], T.SC[:, 7:192:8], T.PT[:, 0:24], A.add)
-        tt("SC G24", VV + "v", T[VV][:, 28 * u:28 * u + 24], T.SC[:, 7:192:8], T.G24[:], A.add)
         for k in range(3):
-            scan("VWs", "SW%d" % k, T.SW[:, k, :], T.VW[:, k, :], T.VW[:, k, :], 0.0, A.max, A.max)
-        top = T.SW[:, :, 39]
-        turn("SW0 SW1 SW2", "AR", T.AR[:], T.SW[:, :, 8:40])
-        tt("SW0 SW1 SW2 CK sk", "sk0", T.sk[:, 0:3], top, T.CK[:, 3 * u:3 * u + 3], A.add)
-        ts("SW0 SW1 SW2 sk", "sk1", T.sk[:, 4:7], top, LAST, A.is_le, NONE, A.mult)
+            act("SC%d" % k, "%sv%d" % (VV, k), T[VV][:, 28 * u + 8 * k:28 * u + 8 * k + 8], T.SC[:, 360 * k + 8:360 * k + 72:9])
+
+        def state(b):
+            k = (3 + b) % 4
+            tt("TB%d ps%d" % (b, k), "X%d" % b, T.Xt[:, b:1280:4], T.TB[:, C * b:C * b + C], ps(k), A.add)
+        turn("SW0 SW1 SW2", "AR", T.AR[:], T.SW[:, 0:3, 8:40])
+        act("SW0 SW1 SW2", VV, T[VV][:, 28 * u + 24:28 * u + 28], T.SW[:, :, 39])
+        send(t, "av%d" % t, VV + " " + keys(VV + "v%d", 3), VV + "p", T[VV][:, 28 * u:28 * u + 28], T[VV][:, 28 * u:28 * u + 28])
+        gap(5)
         for j in range(ON_V, 20):
             act("AR xcb", "D0_%d" % j, T.D0[:, SEG * j:SEG * j + 96], T.AR[:], F.Abs, scale=BIG, bias=T.xcb[:, j:j + 1])
         relu(EARLY, 4)
         for j in range(ON_V):
             ts("AR xc", "D0_%d" % j, T.D0[:, SEG * j:SEG * j + 96], T.AR[:], T.xc[:, j:j + 1], A.not_equal, BIG, A.mult)
-            if j == 0:
-                tt("sk0 sk1", VV, T[VV][:, 28 * u + 24:28 * u + 28], T.sk[:, 0:4], T.sk[:, 4:8], A.max)
-                send(t, "av%d" % t, "%s %sv" % (VV, VV), VV + "p", T[VV][:, 28 * u:28 * u + 28], T[VV][:, 28 * u:28 * u + 28])
         for lo, hi in SCANS:
             scan(keys("D0_%d", range(lo, hi)) + " D0r ST31 ST63 ST95 ST96", "SO%d" % lo, T.SO[:, SEG * lo:SEG * hi],
                  T.D0[:, SEG * lo:SEG * hi], T.ST[:, 0:SEG * (hi - lo)], 4096.0, A.min, A.subtract)
-
-        def state(at):
-            for b in range(4):
-                if XAT[b] == at:
-                    k = (3 + b) % 4
-                    tt("TB%d ps%d" % (b, k), "X%d" % b, T.Xt[:, b:1280:4], T.TB[:, C * b:C * b + C], ps(k), A.add)
-        state(-1)
-        ts(keys("SO%d", [lo for lo, hi in SCANS]), "KK", T.KK[:], T.SO[:, 95:20 * SEG:SEG], 160.0 + B0, A.add, 1025.0, A.mult)
         state(0)
-        tt("KK", "M1", T.M1[0:64, :], T.KK[0:64, :], T.KK[64:128, :], A.min)
+        ts(keys("SO%d", [lo for lo, hi in SCANS]), "KK", T.KK[:], T.SO[:, 95:20 * SEG:SEG], 160.0 + B0, A.add, 1025.0, A.mult)
         state(1)
+        tt("KK", "M1", T.M1[0:64, :], T.KK[0:64, :], T.KK[64:128, :], A.min)
+        state(2)
         for a in range(4):
             tt("M1", "MO%d" % a, T.MO[32 * a:32 * a + 32, 20 * t:20 * t + 20], T.M1[0:32, :], T.M1[32:64, :], A.min)
         send(t, "am%d" % t, keys("MO%d", 4), MP, T[MP][:], mo)
         act("PAo PAp CUr", "VR", T.VR[:], T.PA[:].indirect(cu(CR)))
-        spread1("%s %sv %sp" % (VV, VV, VV), VV, T[VV], 56, 56)
-        act("VR Tin Tin2", "Tr", T.Tin[:, 0:40, 1:6:3], T.VR[:])
         if t == 0:
-            act("YR m6 hm", "YR", T.YR[:], T.YR[:], F.Identity, scale=col["m6"], bias=col["hm"])
+            aff("C1 m", "C1", T.C1[:], T.C1[:], 1.0, col["m"])
+            aff("CK m", "CK", T.CK[:], T.CK[:], 1.0, col["m"])
+        spread1("%s %sp %s" % (VV, VV, keys(VV + "v%d", 3)), VV, T[VV], 56, 56)
+        act("VR Tin", "Tr", T.Tin[:, 0:40, 1:6:3], T.VR[:])
+        if t == 0:
+            aff("C1", "CZ", T.CZ[:], T.C1[:], 1024.0, SHIFT - 1024.0)
+            aff("CK", "CK", T.CK[:], T.CK[:], 1024.0, -LAST - 1.0)
         spread2(VV, T[VV], 56, 56)
         k = keys(VV + "_%d", 4) + " CUv0 CUv2 CUv3 CUs"
-        act(k, "va", T.va[:], T[VV][:].indirect(cu(CV)), F.Abs, scale=STILL, bias=-5 * 2048 * STILL)
-        act(k, "vh", T.vh[:], T[VV][:].indirect(cu(CV)), F.Relu, scale=1.0 / 2048, bias=-6.0)
         act(k, "SK", T.SK[:], T[VV][:].indirect(cu(CS)))
-        state(2)
+        act(k, "vh", T.vh[:], T[VV][:].indirect(cu(CV)), F.Sign, bias=0.5 - LAST)
+        act(k, "va", T.va[:], T[VV][:].indirect(cu(CV)), F.Abs, scale=STILL, bias=-10560 * STILL)
+        act("vh", "vh", T.vh[:], T.vh[:], F.Relu)
+        if t == 0:
+            aff("YR m6 hm", "YR", T.YR[:], T.YR[:], col["m6"], col["hm"])
+        state(3)
         tt("C1 VR", "dd", T.dd[:], T.C1[:], T.VR[:], A.subtract)
+        tt("SK CK", "sk0", T.sk[:, 0:32], T.SK[:], T.CK[:], A.add)
+        ts("SK", "sk1", T.sk[:, 32:64], T.SK[:], LAST, A.is_le, NONE, A.mult)
         if t < 2:
             n = C * upper(t + 1)
             quant(keys("X%d", 4), "QF%d" % (t + 1), "QF%d" % (t + 1), n, n + C, T.Xt[:])
@@ -435,19 +514,20 @@ def rank_program(g, core, T, topo):
                 dma("y", "out", "QX3", "", T.osc[4 * k:4 * k + 4, :], T.SQX3[32 * k:32 * k + 4, :])
             act("ps4", "ys", T.ys[:], ps(4))
             dma("y", "out", "ys", "", T.y[:], T.ys[:])
-        tt("va CZ Tin Tin2", "Tz", T.Tin[:, 0:40, 2:6:3], T.va[:], T.CZ[:], A.min)
-        tt("vh dd Tin Tin2", "Th", T.Tin[:, 0:40, 0:6:3], T.vh[:], T.dd[:], A.mult)
+        tt("sk0 sk1", "SK", T.SK[:], T.sk[:, 0:32], T.sk[:, 32:64], A.max)
+        tt("va CZ Tin", "Tz", T.Tin[:, 0:40, 2:6:3], T.va[:], T.CZ[:], A.min)
+        tt("vh dd Tin", "Th", T.Tin[:, 0:40, 0:6:3], T.vh[:], T.dd[:], A.mult)
         for w in range(2):
             tt(keys("MO%d", 4) + " SK", "MQ%d" % w, T.MQ[:, 10 * w:10 * w + 10], T.MO[:, 20 * t + 10 * w:20 * t + 10 * w + 10],
                T.SK[:, 16 * w:16 * w + 10], A.min)
+        tt("MQ0 MQ1 " + MP, "I1", T.I1[:], T.MQ[:, b0:b0 + 10], T[MP][:, b0:b0 + 10], A.min)
+        for h in range(2):
+            tt("MQ0 MQ1 Tin " + MP, "Tk%d" % h, T.Tin[:, h:40:2, 6], T.MQ[:], T[MP][:], A.min)
         turn("Tz", "T1", T.T1[:], T.Tin[:, 2 * b0:2 * b0 + 32:2, 2:6:3])
         for h in range(2):
             act("T1", "Z3%d" % h, T.Z3[:, h:4:2, :], T.T1[:])
-        tt("MQ0 MQ1 " + MP, "I1", T.I1[:], T.MQ[:, b0:b0 + 10], T[MP][:, b0:b0 + 10], A.min)
-        for h in range(2):
-            tt("MQ0 MQ1 Tin Tin2 " + MP, "Tk%d" % h, T.Tin[:, h:40:2, 6], T.MQ[:], T[MP][:], A.min)
         ts("I1", "I2", T.I2[:], T.I1[:], 1023, band)
-        turn("Tk0 Tk1 Tpad Tr Tz Th", "Tout", T.Tout[:], T.Tin[:, 0:42, :])
+        turn("Tk0 Tk1 Tr Tz Th", "Tout", T.Tout[:], T.Tin[:, 0:40, :])
         for h in range(2):
             cp("I2", "OFF%d" % h, T.OFF[:, h:20:2], T.I2[:])
         turn("Z30 Z31", "ZT", T.ZT[:], T.Z3[:])
@@ -475,7 +555,7 @@ def rank_program(g, core, T, topo):
             tt("PN YJ", "ne", T.ne[:], pn, T.YJ[:, n:n + 40], A.not_equal)
         else:
             for e in range(2):
-                turn("PN", "OT%d" % e, T.OT[:, 32 * e:32 * e + 32], T.PN[:, 60 * e + 2:60 * e + 98:3])
+                turn("PN PNpad", "OT%d" % e, T.OT[:, 32 * e:32 * e + 32], T.PN[:, 60 * e + 2:60 * e + 98:3])
             for k in range(8):
                 dma("ys"[k % 2], "out2", "OT%d" % (k % 2), "", T.ov[k, :],
                     T.OT[32 * (k // 2):32 * (k // 2) + 20, 32 * (k % 2):32 * (k % 2) + 16])

@@ -3,7 +3,8 @@ from concourse.mybir import dt, AluOpType as A, ActivationFunctionType as F
 C = 320
 STEP = [2, 1, 3]
 CODE = "float8_e4m3fn_x4"
-SEG = 97
+CUT = (0, 192, 320)
+SEG = 81
 BIG = 16384.0
 LAST = 14336.0
 NONE = 1048576.0
@@ -12,8 +13,12 @@ STILL = 800.0
 ON_V = 7
 SCANS = ((0, 3), (7, 12), (3, 7), (12, 16), (16, 18), (18, 20))
 TAIL = "v0 s1 v2 s3 s4 q0 s5 v6 s7 q1"
+ORDER = "c0 c1 p0 p1 c2 l0 l1 p2 d0 a0 a1 g4 l2 a3 a2"
 EARLY = 3
-GAPS = (2, 4, 4, 4, 2, 2, 2)
+PIECES = (0, 256, 512, 768, 1024, 1280)
+FIRST = 128
+GAPS = (7, 4, 4, 6, 1, 0)
+SGAPS = (4, 3, 3)
 
 SCRATCH = {}
 
@@ -24,20 +29,20 @@ def _buf(name, n, dtype, where="sbuf"):
 
 for _k in range(8):
     _buf("ps%d" % _k, 512, "float32", "psum")
-for _n, _w in (("xin", 1280), ("uin", 512), ("vin", 512), ("Xt", 1280), ("Yt", 1536), ("Z", 1040), ("D0", 20 * SEG), ("SO", 20 * SEG),
+for _n, _w in (("xin", 1280), ("uin", 512), ("vin", 512), ("Xt", 1280), ("Yt", 1280), ("Z", 1040), ("D0", 20 * SEG), ("SO", 20 * SEG),
                ("ST", 5 * SEG), ("D", 216)):
     _buf(_n, _w, "bfloat16")
 for _n, _w in (("QF0", 640), ("QF1", 640), ("QF2", 640), ("G0", 1280), ("G1", 1280), ("G2", 1280), ("B0", 640), ("B1", 640), ("B2", 640),
                ("QX3", C), ("QY", 384), ("QE", 1024), ("QW", 512), ("QU", 128), ("QAB", 160), ("QV", 128)):
     _buf(_n, _w, CODE)
     _buf("S" + _n, _w, "uint8")
-for _n, _w in (("TB", 1280), ("SL", 216), ("Mm", 288), ("SC", 1080), ("VR", 80), ("SW", [4, 40]), ("AR", 96), ("KK", 20),
+for _n, _w in (("TB", 1280), ("SL", 216), ("Mm", 288), ("SC", 1080), ("VR", 80), ("SW", [4, 40]), ("AR", 80), ("AT", 32), ("KK", 20),
                ("M1", 20), ("SK", 32), ("sk", 64), ("MO", 60), ("MQ", 20), ("MP0", 20), ("MP1", 20), ("MP2", 20),
                ("VV0", 224), ("VV1", 224), ("VV2", 224), ("Tin", [52, 16]), ("Tout", 640), ("GG", C), ("ZZ", [20, 16]),
                ("va", 80), ("vh", 80), ("dd", 80), ("T1", 32), ("Z3", [4, 16]), ("ZT", 64),
-               ("ZO", [20, 2]), ("q1", 40), ("Q3", 120), ("S3", 120), ("PN", 160),
+               ("ZO", [20, 2]), ("Q3", 120), ("S3", 120), ("PN", 160),
                ("ne", 40), ("PS", 40), ("PZ", 256), ("PA", 80), ("OT", 64), ("ys", C),
-               ("idm", 128), ("CF", 36), ("NI", 8), ("NJ", 8), ("t8", 8), ("CL", 32), ("l1", 8), ("xc", 20), ("xcb", 20),
+               ("idm", 128), ("CF", 38), ("NI", 8), ("NJ", 8), ("t8", 8), ("CL", 32), ("l1", 8), ("xc", 20), ("xcb", 20),
                ("YJ", 80), ("YR", 640), ("C1", 80), ("CZ", 80), ("CK", 32)):
     _buf(_n, _w, "float32")
 for _n, _w in (("Vi", 20), ("Vp", 20), ("PI", 1), ("CI", 16), ("I1", 10), ("I2", 10), ("II", 30)):
@@ -45,9 +50,9 @@ for _n, _w in (("Vi", 20), ("Vp", 20), ("PI", 1), ("CI", 16), ("I1", 10), ("I2",
 for _n, _w in (("CU", 26), ("OFF", 20), ("PO0", 40), ("PO1", 40), ("PO2", 40), ("PP0", 40), ("PP1", 40), ("PP2", 40)):
     _buf(_n, _w, "uint16")
 
-SEMAPHORES = ["cv", "cs", "ct", "cg", "sent", "lx0", "lx1", "lg", "lu", "lw", "lv", "out", "out2"]
+SEMAPHORES = ["cv", "cs", "ct", "cg", "sent", "lx", "lx1", "lg", "lu", "lw", "lv", "out", "out2"]
 for _t in range(3):
-    SEMAPHORES += ["ax%d" % _t, "ap%d" % _t, "av%d" % _t, "am%d" % _t]
+    SEMAPHORES += ["ax%d" % _t, "as%d" % _t, "ap%d" % _t, "av%d" % _t, "am%d" % _t]
 
 
 def rank_program(g, core, T, topo):
@@ -191,7 +196,7 @@ def rank_program(g, core, T, topo):
     DIGITS = (("h16", 0, 16), ("i", 0, 15), ("r32", 0, 96), ("e", 0, 1), ("k0", 1, 1), ("r0", 5, 1), ("k1", 2, 1), ("r1", 6, 1),
               ("i3", 3, 1))
     MORE = ("i8", "m", "q4", "h", "even", "x0", "sg", "x1", "sh", "x2", "x3", "dR", "dT", "dV", "dS", "a0", "a1", "a2", "a3", "end",
-            "g0", "g1", "m6", "hm", "s0")
+            "g0", "g1", "m8", "hm", "s0", "jump", "kb")
     col = {n: T.CF[:, k:k + 1] for k, n in enumerate([d[0] for d in DIGITS] + list(MORE))}
     CAB, CR, CT, CV, CS = (0, 10), (10, 15), (16, 18), (18, 23), (24, 26)
 
@@ -199,19 +204,21 @@ def rank_program(g, core, T, topo):
         return T.CU[:, c[0]:c[1]]
     H = C // 2
 
-    def send_state(t, lo, hi, R):
+    def send_codes(t, R, lo, hi):
         q, at = "QF%d" % t, C * upper(t)
-        send(t, "ax%d" % t, R, q + "p", T[q][:, at + lo:at + hi].bitcast(dt.uint8), T[q][:, at + lo:at + hi].bitcast(dt.uint8))
-        if hi == C:
-            send(t, "ax%d" % t, R, q + "p", T["S" + q][:, at:at + C], T["S" + q][:, at:at + C])
+        send(t, "ax%d" % t, R, q + "c", T[q][:, at + lo:at + hi].bitcast(dt.uint8), T[q][:, at + lo:at + hi].bitcast(dt.uint8))
+
+    def send_scales(t):
+        q, at = "QF%d" % t, C * upper(t)
+        send(t, "as%d" % t, q, q + "s", T["S" + q][:, at:at + C], T["S" + q][:, at:at + C])
 
     def tile_e(par, b):
         at = 512 * par + 128 * b
         quant("Z%d" % par, "QE%d%d" % (par, b), "QE", at, at + 128, T.Z[:, 520 * par + 3 - b:520 * par + 515 - b])
 
     dma("s", "lg", "", "Vi", T.Vi[:], T.vg[:])
-    dma("y", "lx0", "", "xin0", T.xin[:, 0:4 * H], T.x[:, 0:4 * H])
-    dma("y", "lx1", "", "xin1", T.xin[:, 4 * H:4 * C], T.x[:, 4 * H:4 * C])
+    dma("y", "lx", "", "xin0", T.xin[:, 0:4 * FIRST], T.x[:, 0:4 * FIRST])
+    dma("y", "lx1", "", "xin", T.xin[:, 4 * FIRST:1280], T.x[:, 4 * FIRST:1280])
     dma("y", "lu", "", "uin", T.uin[:], T.u[:])
     iota("PI", T.PI[:], [[0, 1]], 1)
     iota("NI", T.NI[:], [[16, 8]], 0)
@@ -235,23 +242,24 @@ def rank_program(g, core, T, topo):
     fill("OT", T.OT[:, 20:32], 0.0)
     for k, (n, sh, m) in enumerate(DIGITS):
         ts("PI", "CI%d" % k, T.CI[:, k:k + 1], T.PI[:], sh, shr, m, band)
-    fill("Ypad", T.Yt[:, 1024:1536], 0.0)
+    fill("Ypad", T.Yt[:, 0:512], 0.0)
     cp(keys("CI%d", len(DIGITS)), "CF", T.CF[:, 0:len(DIGITS)], T.CI[:, 0:len(DIGITS)])
     next(mine)
     at0 = C * upper(0)
-    quant("xin0", "QF0h", "QF0", at0, at0 + H, T.xin[:, 0:4 * H])
-    send_state(0, 0, H, "QF0h")
-    next(mine)
-    ts("NI CF", "NJ", T.NJ[:], T.NI[:], col["i"], A.add)
-    ts("CF", "h", col["h"], col["h16"], 0.0625, A.mult)
-    ts("CF", "even", col["even"], col["h16"], 0.0, A.is_equal)
+    quant("xin0", "QF0h", "QF0", at0, at0 + FIRST, T.xin[:, 0:4 * FIRST])
+    send_codes(0, "QF0h", 0, FIRST)
+    aff("NI CF", "NJ", T.NJ[:], T.NI[:], 1.0, col["i"])
+    aff("CF", "h", col["h"], col["h16"], 0.0625, 0.0)
+    aff("CF", "even", col["even"], col["h16"], -0.0625, 1.0)
+    aff("NI CF", "t8", T.t8[:], T.NI[:], 0.125, col["i3"])
+    aff("NJ", "If", T.CL[:, 16:21], T.NJ[:, 0:5], 1.0 / 9, -4.0 / 9)
     ts("CF", "x0", col["x0"], col["k0"], col["r0"], A.not_equal, 2.0, A.mult)
-    ts("NI CF", "t8", T.t8[:], T.NI[:], 0.125, A.mult, col["i3"], A.add)
     next(mine)
-    quant("xin1", "QF0", "QF0", at0 + H, at0 + C, T.xin[:, 4 * H:4 * C])
-    send_state(0, H, C, "QF0 QF0h")
+    quant("xin QF0h", "QF0", "QF0", at0 + FIRST, at0 + C, T.xin[:, 4 * FIRST:1280])
+    send_scales(0)
+    send_codes(0, "QF0", FIRST, C)
+    next(mine)
     Ii, Is, I7, Ia, Ib = [T.II[:, 6 * k:6 * k + 5] for k in range(5)]
-    ts("NJ", "If", T.CL[:, 16:21], T.NJ[:, 0:5], -4.0, A.add, 1.0 / 9, A.mult)
     for par in range(2):
         ts("idm Z h even", "Z%d" % par, T.Z[:, 520 * par + 3:520 * par + 515:4], T.idm[:], 0.0, A.is_equal,
            col["h" if par else "even"], A.mult)
@@ -259,6 +267,7 @@ def rank_program(g, core, T, topo):
     cp("If", "Ii", Ii, T.CL[:, 16:21])
     ts("CF x0", "sg", col["sg"], col["k1"], col["r1"], A.not_equal, col["x0"], A.add)
     iota("YJ", T.YJ[:], [[C, 2], [0, 2], [16, 20]], 0, 1)
+    iota("Mm", T.Mm[:], [[0, 288]], 0, 1)
     iota("PZ", T.PZ[:], [[0, 256]], 0, -8)
     tile_e(0, 0)
     ts("Ii", "Im", T.CL[:, 24:29], Ii, -9.0, A.mult)
@@ -286,16 +295,15 @@ def rank_program(g, core, T, topo):
     ts("Ia", "CAa", T.CU[:, 0:5], Ia, 16.0, A.mult)
     tile_e(1, 2)
     tile_e(1, 3)
-    dma("y", "lw", "QF0p", "QW", T.QW[:].bitcast(dt.uint8), T.wc[:])
+    dma("y", "lw", "QF0c", "QW", T.QW[:].bitcast(dt.uint8), T.wc[:])
     dma("y", "lw", "", "QW2", T.SQW[:], T.ws[:])
     dma("y", "lv", "", "vin", T.vin[:], T.v[:])
 
-    iota("Mm", T.Mm[:], [[0, 288]], 0, 1)
-    iota("SC", T.SC[:], [[0, 1080]], 0)
     iota("xc", T.xc[:], [[32, 20]], 0, int(LAST) + 1)
-    iota("CK", T.CK[:], [[C, 2], [32, 16]], 0)
     iota("ST", T.ST[:], [[0, 5 * SEG]], 0, 1)
     iota("C1", T.C1[:], [[32, 20], [0, 4]], 0, 1)
+    iota("CK", T.CK[:], [[C, 2], [32, 16]], 0)
+    iota("SC", T.SC[:], [[0, 1080]], 0)
     iota("Tin", T.Tin[:], [[0, 832]], 0, -1)
     iota("YR", T.YR[:], [[32, 20], [0, 2], [1, 16]], 0, -SHIFT)
     aff("CF h", "dT", col["dT"], col["r32"], 0.0625, col["h"])
@@ -304,7 +312,8 @@ def rank_program(g, core, T, topo):
     act("CF", "s0", col["s0"], col["r32"], F.Sign, bias=-1.0)
     aff("h CF", "dR", col["dR"], col["e"], 20.0, col["h"])
     aff("CF", "dV", col["dV"], col["r32"], 0.0625, col["e"])
-    aff("CF", "end", col["end"], col["r32"], -1.0, -127.0)
+    aff("CF", "end", col["end"], col["r32"], -1.0, -63.0)
+    aff("CF", "jump", col["jump"], col["r1"], 80.0, 33.0)
     aff("CF", "q4", col["q4"], col["i3"], 2.0, col["k1"])
     aff("CF", "m", col["m"], col["h16"], 1.0, col["i"])
     aff("CF", "i8", col["i8"], col["i3"], 8.0, 0.0)
@@ -318,65 +327,81 @@ def rank_program(g, core, T, topo):
     aff("s0", "s0", col["s0"], col["s0"], 1.0 / 2048, 0.0)
     aff("sg dT", "dT", col["dT"], col["sg"], 64.0, col["dT"])
     aff("NI dR", "l1r", T.CL[:, 0:5], T.NI[:, 0:5], 0.5, col["dR"])
+    sfill("Mmb", T.Mm[:, 8:216:9], 24, -2048.0, "Mm")
+    sfill("Mma", T.Mm[:, 0:216:9], 24, 0.0, "Mm")
+    for k in range(3):
+        sfill("Mm%d" % k, T.Mm[:, 72 * k + 11:72 * k + 62:10], 6, -1.0, "Mm")
+    sfill("Mmb", T.Mm[:, 71:216:72], 3, 2048.0)
     next(theirs)
     act("QU CAa CAb", "QABs", T.SQAB[:], T.SQU[:].indirect(cu(CAB)))
     next(theirs)
-    ts("t8 dT", "CUt", cu(CT), T.t8[:, 0:2], 8.0, A.mult, col["dT"], A.add)
-    quant("Ypad", "QYpad", "QY", 256, 384, T.Yt[:, 1024:1536])
+    cp("QU CAa CAb", "QABc", words(T.QAB[:]), words(T.QU[:]).indirect(cu(CAB)))
     next(theirs)
-
-    def multipliers():
-        sfill("Mma", T.Mm[:, 0:216:9], 24, 0.0, "Mm")
-        sfill("Mmb", T.Mm[:, 8:216:9], 24, -2048.0, "Mm")
-        for k in range(3):
-            sfill("Mm%d" % k, T.Mm[:, 72 * k + 11:72 * k + 62:10], 6, -1.0, "Mm")
-        sfill("Mmb", T.Mm[:, 71:216:72], 3, 2048.0)
+    quant("Ypad", "QYpad", "QY", 0, 128, T.Yt[:, 0:512])
+    ts("t8 dT", "CUt", cu(CT), T.t8[:, 0:2], 8.0, A.mult, col["dT"], A.add)
 
     def lists_of_the_table():
         yield ts("CF", "x1", col["x1"], col["e"], col["r0"], A.not_equal, 2.0, A.mult)
         yield ts("CF", "x2", col["x2"], col["k1"], col["r0"], A.not_equal, 112.0, A.mult)
         yield ts("CF", "x3", col["x3"], col["i3"], col["r1"], A.not_equal, 56.0, A.mult)
         yield ts("NJ", "l1", T.l1[:, 0:5], T.NJ[:, 0:5], 40.0, A.is_ge, 20.0, A.mult)
-        yield ts("CF", "m6", col["m6"], col["i"], 6.0, A.is_equal)
-        yield ts("CF x1", "sh", col["sh"], col["k0"], col["r1"], A.not_equal, col["x1"], A.add)
+        yield ts("CF", "m8", col["m8"], col["i"], 8.0, A.is_equal)
+        yield ts("CF x1", "sh", col["sh"], col["k0"], col["r1"], A.is_equal, col["x1"], A.add)
+        yield ts("CF q4", "kb", col["kb"], col["k0"], col["q4"], A.add, 3.0, A.min)
         yield ts("x2 x3 dV", "a0", col["a0"], col["x2"], col["x3"], A.add, col["dV"], A.add)
         yield ts("x3 i8", "a3", col["a3"], col["x3"], -2.0, A.mult, col["i8"], A.add)
         yield tt("l1r l1", "CLr", T.CL[:, 8:13], T.CL[:, 0:5], T.l1[:, 0:5], A.add)
-        yield ts("CF m6", "hm", col["hm"], col["h16"], col["m6"], A.mult)
-        yield ts("sh q4", "dS", col["dS"], col["sh"], 56.0, A.mult, col["q4"], A.add)
-        yield ts("a3 CF", "a2", col["a2"], col["a3"], 60.0, A.add, col["i3"], A.mult)
-        yield ts("a3 a0", "a1", col["a1"], col["a3"], 60.0, A.add, col["a0"], A.add)
+        yield ts("CF m8", "hm", col["hm"], col["h16"], col["m8"], A.mult)
+        yield ts("sh kb", "dS", col["dS"], col["sh"], 56.0, A.mult, col["kb"], A.add)
+        yield ts("a3 CF", "a2", col["a2"], col["a3"], 44.0, A.add, col["i3"], A.mult)
+        yield ts("a3 a0", "a1", col["a1"], col["a3"], 56.0, A.add, col["a0"], A.add)
         yield cp("CLr", "CUr", cu(CR), T.CL[:, 8:13])
         yield ts("NI dS", "l1s", T.CL[:, 6:8], T.NI[:, 0:2], 1.75, A.mult, col["dS"], A.add)
-        yield ts("a2 a0", "a2", col["a2"], col["a2"], col["a0"], A.add)
-        for lo, hi, a in ((0, 2, "a0"), (3, 5, "a1"), (2, 3, "a2")):
+        yield ts("a2 a1", "a2", col["a2"], col["a2"], -1.0, A.mult, col["a1"], A.add)
+        yield ts("a0 a1", "a0", col["a0"], col["a0"], 12.0, A.add)
+        for lo, hi, a in ((0, 2, "a1"), (2, 3, "a2"), (3, 5, "a0")):
             yield ts("NI " + a, "CUv%d" % lo, T.CU[:, CV[0] + lo:CV[0] + hi], T.NI[:, lo:hi], 0.5, A.mult, col[a], A.add)
         yield ts("l1s", "CUs", cu(CS), T.CL[:, 6:8], 24.0, A.add)
-    late = lists_of_the_table()
+
+    def tables():
+        yield aff("xc m", "xc", T.xc[:], T.xc[:], 1.0, col["m"])
+        yield aff("C1 m", "C1", T.C1[:], T.C1[:], 1.0, col["m"])
+        yield aff("CK m", "CK", T.CK[:], T.CK[:], 1.0, col["m"])
+        for k, c in ((47, 97.0), (80, -4096.0)):
+            yield sfill("ST%d" % k, T.ST[:, k:5 * SEG:SEG], 5, c, "ST")
+        for k, c in ((15, "jump"), (79, "end")):
+            yield aff("ST " + c, "ST%d" % k, T.ST[:, k:5 * SEG:SEG], T.ST[:, k:5 * SEG:SEG], col[c], 0.0)
+        yield act("xc", "xcb", T.xcb[:], T.xc[:], scale=-BIG)
+        yield aff("C1", "CZ", T.CZ[:], T.C1[:], 1024.0, SHIFT - 1024.0)
+        yield aff("CK", "CK", T.CK[:], T.CK[:], 1024.0, -LAST - 1.0)
+    late, later = lists_of_the_table(), tables()
 
     def gap(k):
         for _ in range(GAPS[k]):
             next(late, None)
+
+    def sgap(k):
+        for _ in range(SGAPS[k]):
+            next(later, None)
 
     for t in range(3):
         u = upper(t)
         B0, Bp, b0 = C * u, C - C * u, 10 * u
         QF, G, B, PO, PP, VV, MP = ["%s%d" % (n, t) for n in ("QF", "G", "B", "PO", "PP", "VV", "MP")]
         mo = T.MO[:, 20 * t:20 * t + 20]
-        win = "%s %sp %sh " % (QF, QF, QF)
+        win = "%s %s# " % (QF, QF)
 
         def unpack(h, e, x, at, R, start, stop):
             for b in range(4):
-                mm(4 * h + b, "QE", 512 * e + 128 * b, x, at + H * h, H, "QE%d%d %s" % (e, b, R), start, stop)
+                mm(4 * h + b, "QE", 512 * e + 128 * b, x, at + CUT[h], CUT[h + 1] - CUT[h], "QE%d%d %s" % (e, b, R), start, stop)
 
         def marked():
             for e in range(2):
-                aff("PS PZ s0 g%d" % e, "PZ%d" % e, T.PZ[:, 32 * e:32 * e + 20], T.PS[:, 20 * e:20 * e + 20],
+                aff("PS PZ s0 g%d" % e, "PZ%d" % e, T.PZ[:, 32 * e + 4:32 * e + 24], T.PS[:, 20 * e:20 * e + 20],
                     1.0 / 2048 if e else col["s0"], col["g%d" % e])
-            aff("PN", "S3p", T.S3[:, 2:120:3], pn, 1.0, -1.0 if t == 2 else 0.0)
         if t == 0:
             marked()
-            gap(6)
+            gap(5)
         for e in range(2):
             pick(win + PO, "Go%d" % e, G, 640 * e + B0, QF, 0, T[PO][:, 20 * e:20 * e + 20])
             for h in range(2):
@@ -385,36 +410,42 @@ def rank_program(g, core, T, topo):
                 tt("ne PN", "PS", T.PS[:], T.ne[:], pn, A.mult)
         if t:
             marked()
-        ts(PO, "PAo", T.PA[:, 40 * u:40 * u + 40], T[PO][:, 0:40], 1.0, A.add)
         for e in range(2):
             pick(win + PP, "Gp%d" % e, G, 640 * e + Bp, QF, 0, T[PP][:, 20 * e:20 * e + 20])
         for h in range(2):
             for e in range(2):
-                at = 20 * e + 10 * h
-                pick("Go%d# Gp%d# %s" % (e, e, PO), "B%d%d" % (e, h), B, C * e + H * h, G, 640 * e, T[PO][:, at:at + 10])
+                pick("Go%d# Gp%d# %s" % (e, e, PO), "B%d%d" % (e, h), B, C * e + CUT[h], G, 640 * e,
+                     T[PO][:, 20 * e + CUT[h] // 16:20 * e + CUT[h + 1] // 16])
                 unpack(h, e, B, C * e, "B%d%dc B%d%ds" % (e, h, e, h), False, e == 1)
-        spread1("PZ0 PZ1", "PZ", T.PZ, 52, 64)
+        spread1("PZ0 PZ1", "PZ", T.PZ, 56, 64)
+        sgap(0)
         ts(PP, "PAp", T.PA[:, 40 - 40 * u:80 - 40 * u], T[PP][:], 1.0, A.add)
-        if t == 0:
-            cp("QU CAa CAb", "QABc", words(T.QAB[:]), words(T.QU[:]).indirect(cu(CAB)))
+        ts(PO, "PAo", T.PA[:, 40 * u:40 * u + 40], T[PO][:, 0:40], 1.0, A.add)
         gap(0)
         for step in TAIL.split():
             k = int(step[1])
             h, b = divmod(k, 4)
             if step[0] == "q":
                 gap(1 + k)
-                quant(keys("Y%d", range(4 * k, 4 * k + 4)), "QY%d" % k, "QY", H * k, H * k + H, T.Yt[:, 4 * H * k:4 * H * (k + 1)])
-            elif step[0] == "s":
-                act("ps%d QYpad" % k, "Y%d" % k, T.Yt[:, 4 * H * h + b:4 * H * (h + 1):4], ps(k, H), scale=0.5)
+                quant(keys("Y%d", range(4 * k, 4 * k + 4)), "QY%d" % k, "QY", 64 + CUT[k], 64 + CUT[k + 1],
+                      T.Yt[:, 4 * CUT[k]:4 * CUT[k + 1]])
+                continue
+            out, part = T.Yt[:, 4 * CUT[h] + b:4 * CUT[h + 1]:4], ps(k, CUT[h + 1] - CUT[h])
+            if step[0] == "s":
+                act("ps%d QYpad" % k, "Y%d" % k, out, part, scale=0.5)
+                if k == 3:
+                    sgap(1)
             else:
-                ts("ps%d QYpad" % k, "Y%d" % k, T.Yt[:, 4 * H * h + b:4 * H * (h + 1):4], ps(k, H), 0.5, A.mult)
+                ts("ps%d QYpad" % k, "Y%d" % k, out, part, 0.5, A.mult)
         gap(3)
-        spread2("PZ", T.PZ, 52, 64)
+        if t == 1:
+            quant("vin", "QV", "QV", 0, 128, T.vin[:])
+        spread2("PZ", T.PZ, 56, 64)
         for k in range(3):
-            mm(k, "QY", 128 * k, "QAB", 0, 160, ("QY0 QY1" if k else "QY0") + " QABc QABs")
+            mm(k, "QY", 128 * k, "QAB", 0, 160, "QY%d QABc QABs" % (k // 2))
 
         def other_side(k):
-            (cp if k == 2 else act)("ps%d" % k, "SL%d" % k, T.SL[:, 72 * k:72 * k + 72], T["ps%d" % k][:, 80:152])
+            act("ps%d" % k, "SL%d" % k, T.SL[:, 72 * k:72 * k + 72], T["ps%d" % k][:, 80:152])
 
         def compare(k):
             tt("ps%d SL%d" % (k, k), "D%d" % k, T.D[:, 72 * k:72 * k + 72], ps(k, 72), T.SL[:, 72 * k:72 * k + 72], A.is_ge)
@@ -426,88 +457,84 @@ def rank_program(g, core, T, topo):
         def largest(k):
             v = T.SC[:, 360 * k + 8:360 * k + 360:9]
             scan("SC%d" % k, "SW%d" % k, T.SW[:, k, :], v, v, 0.0, A.max, A.max)
+
+        def differ(k):
+            tt("C1 VR", "dd", T.dd[:], T.C1[:], T.VR[:], A.subtract)
+
+        def along(k):
+            if k == 0:
+                turn("SW0", "AT", T.AT[64:128, :], T.SW[64:128, 0, 8:40])
+            elif k == 3:
+                cp("AT", "AR3", T.AR[0:64, 0:16], T.AT[64:128, 16:32])
+                cp("AT", "AR0", T.AR[64:128, 0:16], T.AT[64:128, 0:16])
+            else:
+                turn("SW%d" % k, "AR%d" % k, T.AR[:, 32 * k - 16:32 * k + 16], T.SW[:, k, 8:40])
         other_side(0)
-        if t == 0:
-            multipliers()
+        other_side(1)
         act(keys("PZ_%d", 4) + " CUt Mm", "PT", T.Mm[:, 1:288:9], T.PZ[:].indirect(cu(CT)))
-        for f, k in ((compare, 0), (other_side, 1), (other_side, 2), (places, 0), (compare, 1), (compare, 2), (largest, 0),
-                     (places, 1), (places, 2)):
-            f(k)
-        if t == 1:
-            quant("vin", "QV", "QV", 0, 128, T.vin[:])
-        gap(4)
-        largest(1)
-        largest(2)
-        if t == 0:
-            aff("xc m", "xc", T.xc[:], T.xc[:], 1.0, col["m"])
+        sgap(2)
+        other_side(2)
+        act("PAo PAp CUr", "VR", T.VR[:], T.PA[:].indirect(cu(CR)))
+        for step in ORDER.split():
+            {"c": compare, "p": places, "l": largest, "a": along, "g": gap, "d": differ}[step[0]](int(step[1]))
         for b in range(4):
-            mm(4 + b, "QW", 128 * b, "QY", 0, C, "QW QW2 QY0 QY1")
+            mm(4 + b, "QW", 128 * b, "QY", 64, C, "QW QW2 QY0 QY1")
 
         def relu(lo, hi):
             for b in range(lo, hi):
                 act("ps%d" % (4 + b), "TB%d" % b, T.TB[:, C * b:C * b + C], ps(4 + b), F.Relu, scale=0.03125)
         relu(0, EARLY)
-        if t == 0:
-            act("xc", "xcb", T.xcb[:], T.xc[:], scale=-BIG)
-            for k, c in ((31, 97.0), (63, 97.0), (96, -4096.0)):
-                sfill("ST%d" % k, T.ST[:, k:5 * SEG:SEG], 5, c, "ST")
-            aff("ST end", "ST95", T.ST[:, 95:5 * SEG:SEG], T.ST[:, 95:5 * SEG:SEG], col["end"], 0.0)
         for b in range(4):
             for e in range(2):
-                mm((3 + b) % 4, "QE", 512 * e + 128 * b, QF, B0, C, "QE%d%d %s %sh" % (e, b, QF, QF), e == 0, e == 1)
+                mm((3 + b) % 4, "QE", 512 * e + 128 * b, QF, B0, C, "QE%d%d %s" % (e, b, QF), e == 0, e == 1)
         for k in range(3):
             act("SC%d" % k, "%sv%d" % (VV, k), T[VV][:, 28 * u + 8 * k:28 * u + 8 * k + 8], T.SC[:, 360 * k + 8:360 * k + 72:9])
 
-        def state(b):
-            k = (3 + b) % 4
-            tt("TB%d ps%d" % (b, k), "X%d" % b, T.Xt[:, b:1280:4], T.TB[:, C * b:C * b + C], ps(k), A.add)
-        turn("SW0 SW1 SW2", "AR", T.AR[:], T.SW[:, 0:3, 8:40])
+        def state(n):
+            for b in range(4):
+                lo, hi = max(PIECES[n] - C * b, 0), min(PIECES[n + 1] - C * b, C)
+                if lo < hi:
+                    k = (3 + b) % 4
+                    tt("TB%d ps%d" % (b, k), "X%d%d" % (n, b), T.Xt[:, 4 * lo + b:4 * hi:4], T.TB[:, C * b + lo:C * b + hi],
+                       T["ps%d" % k][:, lo:hi], A.add)
         act("SW0 SW1 SW2", VV, T[VV][:, 28 * u + 24:28 * u + 28], T.SW[:, :, 39])
         send(t, "av%d" % t, VV + " " + keys(VV + "v%d", 3), VV + "p", T[VV][:, 28 * u:28 * u + 28], T[VV][:, 28 * u:28 * u + 28])
-        gap(5)
+        state(0)
         for j in range(ON_V, 20):
-            act("AR xcb", "D0_%d" % j, T.D0[:, SEG * j:SEG * j + 96], T.AR[:], F.Abs, scale=BIG, bias=T.xcb[:, j:j + 1])
+            act(keys("AR%d", 4) + " xcb", "D0_%d" % j, T.D0[:, SEG * j:SEG * j + 80], T.AR[:], F.Abs, scale=BIG, bias=T.xcb[:, j:j + 1])
         relu(EARLY, 4)
         for j in range(ON_V):
-            ts("AR xc", "D0_%d" % j, T.D0[:, SEG * j:SEG * j + 96], T.AR[:], T.xc[:, j:j + 1], A.not_equal, BIG, A.mult)
+            ts(keys("AR%d", 4) + " xc", "D0_%d" % j, T.D0[:, SEG * j:SEG * j + 80], T.AR[:], T.xc[:, j:j + 1], A.not_equal, BIG, A.mult)
         for lo, hi in SCANS:
-            scan(keys("D0_%d", range(lo, hi)) + " D0r ST31 ST63 ST95 ST96", "SO%d" % lo, T.SO[:, SEG * lo:SEG * hi],
+            scan(keys("D0_%d", range(lo, hi)) + " D0r ST15 ST47 ST79 ST80", "SO%d" % lo, T.SO[:, SEG * lo:SEG * hi],
                  T.D0[:, SEG * lo:SEG * hi], T.ST[:, 0:SEG * (hi - lo)], 4096.0, A.min, A.subtract)
-        state(0)
-        ts(keys("SO%d", [lo for lo, hi in SCANS]), "KK", T.KK[:], T.SO[:, 95:20 * SEG:SEG], 160.0 + B0, A.add, 1025.0, A.mult)
         state(1)
-        tt("KK", "M1", T.M1[0:64, :], T.KK[0:64, :], T.KK[64:128, :], A.min)
+        ts(keys("SO%d", [lo for lo, hi in SCANS]), "KK", T.KK[:], T.SO[:, 79:20 * SEG:SEG], 160.0 + B0, A.add, 1025.0, A.mult)
         state(2)
+        tt("KK", "M1", T.M1[0:64, :], T.KK[0:64, :], T.KK[64:128, :], A.min)
+        state(3)
         for a in range(4):
             tt("M1", "MO%d" % a, T.MO[32 * a:32 * a + 32, 20 * t:20 * t + 20], T.M1[0:32, :], T.M1[32:64, :], A.min)
         send(t, "am%d" % t, keys("MO%d", 4), MP, T[MP][:], mo)
-        act("PAo PAp CUr", "VR", T.VR[:], T.PA[:].indirect(cu(CR)))
-        if t == 0:
-            aff("C1 m", "C1", T.C1[:], T.C1[:], 1.0, col["m"])
-            aff("CK m", "CK", T.CK[:], T.CK[:], 1.0, col["m"])
         spread1("%s %sp %s" % (VV, VV, keys(VV + "v%d", 3)), VV, T[VV], 56, 56)
-        act("VR Tin", "Tr", T.Tin[:, 0:40, 1:6:3], T.VR[:])
-        if t == 0:
-            aff("C1", "CZ", T.CZ[:], T.C1[:], 1024.0, SHIFT - 1024.0)
-            aff("CK", "CK", T.CK[:], T.CK[:], 1024.0, -LAST - 1.0)
+        act("VR Tin", "Tr", T.Tin[:, 0:40, 1:8:4], T.VR[:])
         spread2(VV, T[VV], 56, 56)
         k = keys(VV + "_%d", 4) + " CUv0 CUv2 CUv3 CUs"
-        act(k, "SK", T.SK[:], T[VV][:].indirect(cu(CS)))
         act(k, "vh", T.vh[:], T[VV][:].indirect(cu(CV)), F.Sign, bias=0.5 - LAST)
         act(k, "va", T.va[:], T[VV][:].indirect(cu(CV)), F.Abs, scale=STILL, bias=-10560 * STILL)
         act("vh", "vh", T.vh[:], T.vh[:], F.Relu)
         if t == 0:
-            aff("YR m6 hm", "YR", T.YR[:], T.YR[:], col["m6"], col["hm"])
-        state(3)
-        tt("C1 VR", "dd", T.dd[:], T.C1[:], T.VR[:], A.subtract)
-        tt("SK CK", "sk0", T.sk[:, 0:32], T.SK[:], T.CK[:], A.add)
-        ts("SK", "sk1", T.sk[:, 32:64], T.SK[:], LAST, A.is_le, NONE, A.mult)
+            aff("YR m8 hm", "YR", T.YR[:], T.YR[:], col["m8"], col["hm"])
+        state(4)
+        tt(k + " CK", "sk0", T.sk[:, 0:32], T[VV][:].indirect(cu(CS)), T.CK[:], A.add)
+        ts(k, "sk1", T.sk[:, 32:64], T[VV][:].indirect(cu(CS)), LAST, A.is_le, NONE, A.mult)
         if t < 2:
-            n = C * upper(t + 1)
-            quant(keys("X%d", 4), "QF%d" % (t + 1), "QF%d" % (t + 1), n, n + C, T.Xt[:])
-            send_state(t + 1, 0, C, "QF%d" % (t + 1))
+            q, at = "QF%d" % (t + 1), C * upper(t + 1)
+            quant(keys("X%d%d", 5, 4), q, q, at, at + C, T.Xt[:])
+            send_codes(t + 1, q, 0, C)
+            send_scales(t + 1)
         else:
-            quant(keys("X%d", 4), "QX3", "QX3", 0, C, T.Xt[:])
+            quant(keys("X%d%d", 5, 4), "QX3", "QX3", 0, C, T.Xt[:])
             mm(4, "QV", 0, "QX3", 0, C, "QV QX3")
             dma("y", "out", "QX3", "", T.oc[:], T.QX3[:].bitcast(dt.uint8))
             for k in range(4):
@@ -515,19 +542,20 @@ def rank_program(g, core, T, topo):
             act("ps4", "ys", T.ys[:], ps(4))
             dma("y", "out", "ys", "", T.y[:], T.ys[:])
         tt("sk0 sk1", "SK", T.SK[:], T.sk[:, 0:32], T.sk[:, 32:64], A.max)
-        tt("va CZ Tin", "Tz", T.Tin[:, 0:40, 2:6:3], T.va[:], T.CZ[:], A.min)
-        tt("vh dd Tin", "Th", T.Tin[:, 0:40, 0:6:3], T.vh[:], T.dd[:], A.mult)
+        tt("vh dd Tin", "Th", T.Tin[:, 0:40, 0:8:4], T.vh[:], T.dd[:], A.mult)
+        tt("va CZ Tin", "Tz", T.Tin[:, 0:40, 3:8:4], T.va[:], T.CZ[:], A.min)
         for w in range(2):
             tt(keys("MO%d", 4) + " SK", "MQ%d" % w, T.MQ[:, 10 * w:10 * w + 10], T.MO[:, 20 * t + 10 * w:20 * t + 10 * w + 10],
                T.SK[:, 16 * w:16 * w + 10], A.min)
+        tt("Th VR Tin", "Tg", T.Tin[:, 0:40, 2:8:4], T.Tin[:, 0:40, 0:8:4], T.VR[:], A.add)
         tt("MQ0 MQ1 " + MP, "I1", T.I1[:], T.MQ[:, b0:b0 + 10], T[MP][:, b0:b0 + 10], A.min)
         for h in range(2):
-            tt("MQ0 MQ1 Tin " + MP, "Tk%d" % h, T.Tin[:, h:40:2, 6], T.MQ[:], T[MP][:], A.min)
-        turn("Tz", "T1", T.T1[:], T.Tin[:, 2 * b0:2 * b0 + 32:2, 2:6:3])
+            tt("MQ0 MQ1 Tin " + MP, "Tk%d" % h, T.Tin[:, h:40:2, 8], T.MQ[:], T[MP][:], A.min)
+        turn("Tz", "T1", T.T1[:], T.Tin[:, 2 * b0:2 * b0 + 32:2, 3:8:4])
         for h in range(2):
             act("T1", "Z3%d" % h, T.Z3[:, h:4:2, :], T.T1[:])
         ts("I1", "I2", T.I2[:], T.I1[:], 1023, band)
-        turn("Tk0 Tk1 Tr Tz Th", "Tout", T.Tout[:], T.Tin[:, 0:40, :])
+        turn("Tk0 Tk1 Tr Tz Th Tg", "Tout", T.Tout[:], T.Tin[:, 0:40, :])
         for h in range(2):
             cp("I2", "OFF%d" % h, T.OFF[:, h:20:2], T.I2[:])
         turn("Z30 Z31", "ZT", T.ZT[:], T.Z3[:])
@@ -539,14 +567,13 @@ def rank_program(g, core, T, topo):
         for h in range(2):
             turn("GG%d" % h, "ZZ%d" % h, T.ZZ[:, 10 * h:10 * h + 10, :], T.GG[:, H * h:H * h + H])
         for e in range(2):
-            act("ZZ0 ZZ1", "S30%d" % e, T.S3[:, 60 * e:60 * e + 60:3], T.ZZ[:, :, 3 * e])
-            tt("ZZ0 ZZ1 ZO0 ZO1", "q1%d" % e, T.q1[:, 20 * e:20 * e + 20], T.ZZ[:, :, 6], T.ZO[:, :, e], A.is_equal)
-            tt("ZZ0 ZZ1", "Q31%d" % e, T.Q3[:, 60 * e + 1:60 * e + 60:3], T.ZZ[:, :, 6], T.ZZ[:, :, 3 * e + 2], A.is_equal)
-        for e in range(2):
-            tt("ZZ0 ZZ1 PN", "S31%d" % e, T.S3[:, 60 * e + 1:60 * e + 60:3], T.ZZ[:, :, 3 * e + 1], T.PN[:, 60 * e + 2:60 * e + 60:3],
-               A.subtract)
-        tt("Q310 Q311 q10 q11", "Q32", T.Q3[:, 2:120:3], T.Q3[:, 1:120:3], T.q1[:], A.add)
-        scan("S300 S301 S310 S311 S3p Q30 Q32", "PN", T.PN[:, 0:120], T.Q3[:], T.S3[:], 0.0, A.mult, A.add)
+            lo, hi = 60 * e, 60 * e + 60
+            act("ZZ0 ZZ1", "S31%d" % e, T.S3[:, lo + 1:hi:3], T.ZZ[:, :, 4 * e])
+            aff("ZZ0 ZZ1", "S32%d" % e, T.S3[:, lo + 2:hi:3], T.ZZ[:, :, 4 * e + 1], 1.0, -1.0 if t == 2 else 0.0)
+            tt("ZZ0 ZZ1 PN", "S30%d" % e, T.S3[:, lo:hi:3], T.PN[:, lo + 2:hi:3], T.ZZ[:, :, 4 * e + 2], A.subtract)
+            tt("ZZ0 ZZ1", "Q31%d" % e, T.Q3[:, lo + 1:hi:3], T.ZZ[:, :, 8], T.ZZ[:, :, 4 * e + 3], A.not_equal)
+            tt("ZZ0 ZZ1 ZO0 ZO1", "Q32%d" % e, T.Q3[:, lo + 2:hi:3], T.ZZ[:, :, 8], T.ZO[:, :, e], A.not_equal)
+        scan(keys("S3%d%d", 3, 2) + " Q30 " + keys("Q3%d%d", (1, 2), 2), "PN", T.PN[:, 0:120], T.Q3[:], T.S3[:], 0.0, A.mult, A.add)
         if t < 2:
             o = "PO%d" % (t + 1)
             ts("PN", o, T[o][:], pn, -1.0, A.add)
@@ -556,9 +583,9 @@ def rank_program(g, core, T, topo):
         else:
             for e in range(2):
                 turn("PN PNpad", "OT%d" % e, T.OT[:, 32 * e:32 * e + 32], T.PN[:, 60 * e + 2:60 * e + 98:3])
-            for k in range(8):
-                dma("ys"[k % 2], "out2", "OT%d" % (k % 2), "", T.ov[k, :],
-                    T.OT[32 * (k // 2):32 * (k // 2) + 20, 32 * (k % 2):32 * (k % 2) + 16])
+            for e in range(2):
+                for a in range(4):
+                    dma("ys"[a % 2], "out2", "OT%d" % e, "", T.ov[2 * a + e, :], T.OT[32 * a:32 * a + 20, 32 * e:32 * e + 16])
 
     for s, n in count.items():
         if seen.get(s, 0) < n:

@@ -6,19 +6,25 @@ CODE = "float8_e4m3fn_x4"
 CUT = (0, 192, 320)
 SEG = 81
 BIG = 16384.0
-LAST = 14336.0
-NONE = 1048576.0
-SHIFT = 2097152
-STILL = 800.0
-ON_V = 7
-SCANS = ((0, 3), (7, 12), (3, 7), (12, 16), (16, 18), (18, 20))
-TAIL = "v0 s1 v2 s3 s4 q0 s5 v6 s7 q1"
-ORDER = "c0 c1 p0 p1 c2 l0 l1 p2 d0 a0 a1 g4 l2 a3 a2"
-EARLY = 3
-PIECES = (0, 256, 512, 768, 1024, 1280)
+PLACE = 1048576.0
+LAST = 7 * PLACE
+SELF = 786432
+SHIFT = 4194304
+STILL, MID = 2.875, 5.375 * PLACE
+ON_V = 8
+SCANS = ((0, 4), (8, 13), (4, 8), (13, 16), (16, 18), (18, 20))
+PIECES = (0, 224, 448, 672, 960, 1280)
 FIRST = 128
-GAPS = (7, 4, 4, 6, 1, 0)
-SGAPS = (4, 3, 3)
+WHOLE = False
+AHEAD = 22
+SGAPS = (2, 2, 1, 2)
+PICKS = ["e9 z0 A2 z1 G0 A3 z2 G1 z3 z4 V7 F0 S7 P0 P1 B0 B1 B2 B3 A7 A5 j0 e9 A6 ",
+         "z0 G0 z1 G1 z2 z3 z4 V7 S7 P0 P1 B0 B1 B2 B3 "]
+REST = ("v0 s1 s3 v2 g0 z6 q0 m0 m1 s4 s5 v6 s7 D0 z7 j1 j2 z5 q1 m5 m2 m3 "
+        "M0 M1 D2 L4 o0 o1 R0 V0 R1 M2 m6 m7 o2 l0 c0 c1 R2 l1 r0 a0 c2 m4 p0 l2 a3 p1 r1 p2 w2 a1 a2 k2 L0 x0 F1 j3 "
+        "d0 f0 g1 d1 f1 f2 f3 f4 f5 r2 x1 n0 x2 n1 L1 S0 r3 x3 n2 S2 S1 S4 x4 V3 V8 V4 S8 L2 F2 V6 V2 V1 "
+        "K1 S6 S9 K0 O0 K2 K3 K4 O1 O2 F3 K5 O3 L3 K6 t0 t1 u0 u1 h0 h1")
+ROUND = [PICKS[0] + REST, PICKS[1] + REST, PICKS[1] + REST]
 
 SCRATCH = {}
 
@@ -36,23 +42,24 @@ for _n, _w in (("QF0", 640), ("QF1", 640), ("QF2", 640), ("G0", 1280), ("G1", 12
                ("QX3", C), ("QY", 384), ("QE", 1024), ("QW", 512), ("QU", 128), ("QAB", 160), ("QV", 128)):
     _buf(_n, _w, CODE)
     _buf("S" + _n, _w, "uint8")
-for _n, _w in (("TB", 1280), ("SL", 216), ("Mm", 288), ("SC", 1080), ("VR", 80), ("SW", [4, 40]), ("AR", 80), ("AT", 32), ("KK", 20),
-               ("M1", 20), ("SK", 32), ("sk", 64), ("MO", 60), ("MQ", 20), ("MP0", 20), ("MP1", 20), ("MP2", 20),
+for _n, _w in (("TB", 1280), ("SL", 216), ("Mm", 288), ("SC", [3, 72]), ("VR", 80), ("SW", [4, 48]), ("AR", 96), ("KK", 32),
+               ("FL", [48, 4]), ("DL", [48, 4]), ("RM", [3, 8]), ("PD", 32), ("OD", 30), ("OF", 30), ("OM", 30),
+               ("M1", 20), ("MO", 60), ("MQ", [2, 16]), ("MP0", 20), ("MP1", 20), ("MP2", 20),
                ("VV0", 224), ("VV1", 224), ("VV2", 224), ("Tin", [52, 16]), ("Tout", 640), ("GG", C), ("ZZ", [20, 16]),
                ("va", 80), ("vh", 80), ("dd", 80), ("T1", 32), ("Z3", [4, 16]), ("ZT", 64),
-               ("ZO", [20, 2]), ("Q3", 120), ("S3", 120), ("PN", 160),
+               ("ZO", [20, 2]), ("Q3", 240), ("S3", 240), ("PN", [2, 192]),
                ("ne", 40), ("PS", 40), ("PZ", 256), ("PA", 80), ("OT", 64), ("ys", C),
-               ("idm", 128), ("CF", 38), ("NI", 8), ("NJ", 8), ("t8", 8), ("CL", 32), ("l1", 8), ("xc", 20), ("xcb", 20),
-               ("YJ", 80), ("YR", 640), ("C1", 80), ("CZ", 80), ("CK", 32)):
+               ("idm", 128), ("CF", 48), ("NI", 8), ("NJ", 8), ("t8", 8), ("CL", 32), ("xc", 20), ("xcb", 20),
+               ("YJ", 80), ("YR", 640), ("C1", 80), ("CZ", 80), ("CK", 8)):
     _buf(_n, _w, "float32")
-for _n, _w in (("Vi", 20), ("Vp", 20), ("PI", 1), ("CI", 16), ("I1", 10), ("I2", 10), ("II", 30)):
+for _n, _w in (("Vi", 20), ("Vp", 20), ("PI", 1), ("CI", 16), ("I1", 16), ("I2", 16), ("II", 30)):
     _buf(_n, _w, "int32")
-for _n, _w in (("CU", 26), ("OFF", 20), ("PO0", 40), ("PO1", 40), ("PO2", 40), ("PP0", 40), ("PP1", 40), ("PP2", 40)):
+for _n, _w in (("CU", 30), ("OFF", 20), ("PQ0", 80), ("PQ1", 80), ("PQ2", 80)):
     _buf(_n, _w, "uint16")
 
-SEMAPHORES = ["cv", "cs", "ct", "cg", "sent", "lx", "lx1", "lg", "lu", "lw", "lv", "out", "out2"]
+SEMAPHORES = ["cv", "cs", "ct", "cg", "sent", "lx", "lx1", "lg", "lu", "lw", "lv", "lp", "out", "out2"]
 for _t in range(3):
-    SEMAPHORES += ["ax%d" % _t, "as%d" % _t, "ap%d" % _t, "av%d" % _t, "am%d" % _t]
+    SEMAPHORES += ["ax%d" % _t, "as%d" % _t, "ap%d" % _t, "aq%d" % _t, "av%d" % _t, "am%d" % _t]
 
 
 def rank_program(g, core, T, topo):
@@ -150,9 +157,6 @@ def rank_program(g, core, T, topo):
     def aff(R, W, out, a, scale, bias):
         act(R, W, out, a, F.Identity, scale=scale, bias=bias)
 
-    def sfill(W, ap, n, c, R=""):
-        aff("idm " + R, W, ap, T.idm[:, 0:n], 0.0, c)
-
     def quant(R, W, name, lo, hi, tile):
         op("v", R, W, V.quantize_mx, T[name][:, lo:hi], T["S" + name][:, lo:hi], tile)
 
@@ -160,8 +164,12 @@ def rank_program(g, core, T, topo):
         op("t", R, "ps%d" % bank, PE.matmul_mx, T["ps%d" % bank][:, 0:n], T[w][:, at:at + 128], T["S" + w][:, at:at + 128],
            T[x][:, lo:lo + n], T["S" + x][:, lo:lo + n], start, stop)
 
-    def iota(W, out, pat, cm, first=0):
-        op("g", "", W, g.iota, out, pat, first, cm, allow_small_or_imprecise_dtypes=True)
+    def iota(W, out, pat, cm, first=0, R=""):
+        order("g", [], ["crossing"])
+        op("g", R + " staying", W, g.iota, out, pat, first, cm, allow_small_or_imprecise_dtypes=True)
+
+    def gfill(R, W, ap, n, c):
+        iota(W, ap, [[0, n]], 0, int(c), R)
 
     def ps(k, n=C):
         return T["ps%d" % k][:, 0:n]
@@ -183,22 +191,29 @@ def rank_program(g, core, T, topo):
         cp(R.replace("#", "c"), W + "c", words(T[dst][:, at:at + n]), words(T[src][:, lo:lo + 640]).indirect(off))
         act(R.replace("#", "s"), W + "s", T["S" + dst][:, at:at + n], T["S" + src][:, lo:lo + 640].indirect(off))
 
-    def spread1(R, key, buf, n, pitch):
-        act(R, key + "a", buf[0:64, pitch:pitch + n], buf[64:128, 0:n])
-        act(R, key + "b", buf[64:128, pitch:pitch + n], buf[0:64, 0:n])
+    def move(q, R, W, out, a):
+        if q == "s":
+            act(R, W, out, a)
+        else:
+            order("g", [], ["staying"])
+            op("g", R + " crossing", W, g.affine_select, out, a, [[0, a.shape[1]]], A.is_equal, 0.0, 0, 0)
 
-    def spread2(key, buf, n, pitch):
+    def spread1(R, key, buf, at, n, q):
+        move(q, R, key + "a", buf[0:64, at + n:at + 2 * n], buf[64:128, at:at + n])
+        move(q, R, key + "b", buf[64:128, at + n:at + 2 * n], buf[0:64, at:at + n])
+
+    def spread2(key, buf, at, n, q):
         for a in range(4):
-            act("%sa %sb" % (key, key), "%s_%d" % (key, a), buf[32 * (a ^ 1):32 * (a ^ 1) + 32, 2 * pitch:3 * pitch + n],
-                buf[32 * a:32 * a + 32, 0:pitch + n])
+            move(q, "%sa %sb" % (key, key), "%s_%d" % (key, a), buf[32 * (a ^ 1):32 * (a ^ 1) + 32, at + 2 * n:at + 4 * n],
+                 buf[32 * a:32 * a + 32, at:at + 2 * n])
 
     shr, band = A.logical_shift_right, A.bitwise_and
     DIGITS = (("h16", 0, 16), ("i", 0, 15), ("r32", 0, 96), ("e", 0, 1), ("k0", 1, 1), ("r0", 5, 1), ("k1", 2, 1), ("r1", 6, 1),
               ("i3", 3, 1))
     MORE = ("i8", "m", "q4", "h", "even", "x0", "sg", "x1", "sh", "x2", "x3", "dR", "dT", "dV", "dS", "a0", "a1", "a2", "a3", "end",
-            "g0", "g1", "m8", "hm", "s0", "jump", "kb")
+            "g0", "g1", "m8", "hm", "s0", "jump", "kb", "dR2", "dR3", "n0", "n1", "dU", "i7", "u0", "u1", "q1")
     col = {n: T.CF[:, k:k + 1] for k, n in enumerate([d[0] for d in DIGITS] + list(MORE))}
-    CAB, CR, CT, CV, CS = (0, 10), (10, 15), (16, 18), (18, 23), (24, 26)
+    CAB, CR, CT, CV, CS, CD = (0, 10), (10, 15), (16, 18), (18, 23), (24, 26), (28, 30)
 
     def cu(c):
         return T.CU[:, c[0]:c[1]]
@@ -223,9 +238,11 @@ def rank_program(g, core, T, topo):
     iota("PI", T.PI[:], [[0, 1]], 1)
     iota("NI", T.NI[:], [[16, 8]], 0)
     iota("idm", T.idm[:], [[-1, 128]], 1)
+    iota("YJ", T.YJ[:], [[C, 2], [0, 2], [16, 20]], 0, -SELF)
+    gfill("", "PZ", T.PZ[:, 0:64], 64, -8)
     send(0, "ap0", "Vi", "Vp", T.Vp[:], T.Vi[:])
 
-    def both_halves(src, dst):
+    def both_halves(src, dst, at):
         yield cp(src + " OT", "OTa", T.OT[:, 0:20], T[src][:])
         yield turn("OTa", "T1", T.T1[:], T.OT[:, 0:32])
         for h in range(2):
@@ -233,16 +250,16 @@ def rank_program(g, core, T, topo):
         yield
         yield turn("Z30 Z31", "ZT", T.ZT[:], T.Z3[:])
         for e in range(2):
-            cp("ZT", dst + "ab"[e], T[dst][:, 20 * e:20 * e + 20], T.ZT[:, 32 * e:32 * e + 20])
-        wrote[dst] = wrote[dst + "b"]
+            cp("ZT", dst + "ab"[e], T.PQ0[:, at + 20 * e:at + 20 * e + 20], T.ZT[:, 32 * e:32 * e + 20])
         yield
-    mine, theirs = both_halves("Vi", "PO0"), both_halves("Vp", "PP0")
+    mine, theirs = both_halves("Vi", "PO0", 40 * upper(0)), both_halves("Vp", "PP0", 40 - 40 * upper(0))
 
     fill("Z", T.Z[:], 0.0)
     fill("OT", T.OT[:, 20:32], 0.0)
+    for W, ap, n, c in (("Mm", T.Mm[:, 0:216], 216, 1.0), ("ST", T.ST[:], 5 * SEG, 1.0), ("Tin", T.Tin[:, 0:40, 11:16], 200, -1.0)):
+        aff("Z Z0 Z1", W, ap, T.Z[:, 0:n], 1.0, c)
     for k, (n, sh, m) in enumerate(DIGITS):
         ts("PI", "CI%d" % k, T.CI[:, k:k + 1], T.PI[:], sh, shr, m, band)
-    fill("Ypad", T.Yt[:, 0:512], 0.0)
     cp(keys("CI%d", len(DIGITS)), "CF", T.CF[:, 0:len(DIGITS)], T.CI[:, 0:len(DIGITS)])
     next(mine)
     at0 = C * upper(0)
@@ -264,51 +281,56 @@ def rank_program(g, core, T, topo):
         ts("idm Z h even", "Z%d" % par, T.Z[:, 520 * par + 3:520 * par + 515:4], T.idm[:], 0.0, A.is_equal,
            col["h" if par else "even"], A.mult)
     next(mine)
-    cp("If", "Ii", Ii, T.CL[:, 16:21])
     ts("CF x0", "sg", col["sg"], col["k1"], col["r1"], A.not_equal, col["x0"], A.add)
-    iota("YJ", T.YJ[:], [[C, 2], [0, 2], [16, 20]], 0, 1)
-    iota("Mm", T.Mm[:], [[0, 288]], 0, 1)
-    iota("PZ", T.PZ[:], [[0, 256]], 0, -8)
     tile_e(0, 0)
-    ts("Ii", "Im", T.CL[:, 24:29], Ii, -9.0, A.mult)
     next(mine)
+    cp("If", "Ii", Ii, T.CL[:, 16:21])
     tile_e(0, 1)
-    tt("Im NJ", "Is", Is, T.CL[:, 24:29], T.NJ[:, 0:5], A.add)
-    pn = T.PN[:, 2:120:3]
-    ts("PO0", "PN", pn, T.PO0[:, 0:40], 1.0, A.add)
+    pn = T.PN[:, :, 5:120:6]
+    ts("PO0a PO0b", "PN0 PN1", pn, T.PQ0[:, 40 * upper(0):40 * upper(0) + 40], -float(SELF), A.add)
+    ts("Ii", "Im", T.CL[:, 24:29], Ii, -9.0, A.mult)
     tile_e(0, 2)
     tile_e(0, 3)
-    ts("Is", "I7", I7, Is, 7.0, A.add)
-    ts("Is", "Ib", Ib, Is, 7, band)
-    ts("YJ CF", "YJ", T.YJ[:], T.YJ[:], col["i"], A.add)
+    next(theirs)
+    tt("Im NJ", "Is", Is, T.CL[:, 24:29], T.NJ[:, 0:5], A.add)
     tile_e(1, 0)
     next(theirs)
-    ts("I7", "Ia", Ia, I7, 7, band)
-    tt("Ii Ib", "Ib", Ib, Ii, Ib, A.max)
-    tt("PN YJ", "ne", T.ne[:], pn, T.YJ[:, 40 * upper(0):40 * upper(0) + 40], A.not_equal)
+    ts("YJ CF", "YJ", T.YJ[:], T.YJ[:], col["i"], A.add)
     tile_e(1, 1)
-    next(theirs)
-    tt("Ii Ia", "Ia", Ia, Ii, Ia, A.min)
-    ts("Ib", "CAb", T.CU[:, 5:10], Ib, 7.0, A.min, 16.0, A.mult)
-    tt("ne PN", "PS", T.PS[:], T.ne[:], pn, A.mult)
-    quant("uin", "QU", "QU", 0, 128, T.uin[:])
-    ts("Ia", "CAa", T.CU[:, 0:5], Ia, 16.0, A.mult)
     tile_e(1, 2)
-    tile_e(1, 3)
-    dma("y", "lw", "QF0c", "QW", T.QW[:].bitcast(dt.uint8), T.wc[:])
+
+    def pairs(k):
+        if k == 0:
+            ts("Is", "I7", I7, Is, 7.0, A.add)
+            ts("Is", "Ib", Ib, Is, 7, band)
+        if k == 1:
+            ts("I7", "Ia", Ia, I7, 7, band)
+            tt("Ii Ib", "Ib", Ib, Ii, Ib, A.max)
+        if k == 2:
+            tt("Ii Ia", "Ia", Ia, Ii, Ia, A.min)
+            ts("Ib", "CAb", T.CU[:, 5:10], Ib, 7.0, A.min, 16.0, A.mult)
+        if k == 3:
+            ts("Ia", "CAa", T.CU[:, 0:4], T.II[:, 18:22], 16.0, A.mult)
+            ts("i7", "CAc", T.CU[:, 4:5], col["i7"], -16.0, A.mult, 120.0, A.add)
+        if k == 4:
+            quant("uin", "QU", "QU", 0, 128, T.uin[:])
+        if k == 5:
+            act("QU CAa CAb CAc", "QABs", T.SQAB[:], T.SQU[:].indirect(cu(CAB)))
+        if k == 6:
+            cp("QU CAa CAb CAc", "QABc", words(T.QAB[:]), words(T.QU[:]).indirect(cu(CAB)))
+        if k == 7:
+            ts("t8 dT", "CUt", cu(CT), T.t8[:, 0:2], 8.0, A.mult, col["dT"], A.add)
+            ts("CF dU", "CUd0", T.CU[:, CD[0]:CD[0] + 1], col["r1"], -64.0, A.mult, col["dU"], A.add)
+            ts("q1 dU", "CUd1", T.CU[:, CD[0] + 1:CD[1]], col["q1"], 64.0, A.mult, col["dU"], A.add)
+    dma("y", "lp", "QF0c QF0", "QYpad", T.QY[:, 0:64].bitcast(dt.uint8), T.QF0[:, at0:at0 + 64].bitcast(dt.uint8))
+    dma("y", "lp", "", "QYpad2", T.SQY[:, 0:64], T.SQF0[:, at0:at0 + 64])
+    dma("y", "lw", "", "QW", T.QW[:].bitcast(dt.uint8), T.wc[:])
     dma("y", "lw", "", "QW2", T.SQW[:], T.ws[:])
     dma("y", "lv", "", "vin", T.vin[:], T.v[:])
 
-    iota("xc", T.xc[:], [[32, 20]], 0, int(LAST) + 1)
-    iota("ST", T.ST[:], [[0, 5 * SEG]], 0, 1)
-    iota("C1", T.C1[:], [[32, 20], [0, 4]], 0, 1)
-    iota("CK", T.CK[:], [[C, 2], [32, 16]], 0)
-    iota("SC", T.SC[:], [[0, 1080]], 0)
-    iota("Tin", T.Tin[:], [[0, 832]], 0, -1)
-    iota("YR", T.YR[:], [[32, 20], [0, 2], [1, 16]], 0, -SHIFT)
     aff("CF h", "dT", col["dT"], col["r32"], 0.0625, col["h"])
     for e in range(2):
-        aff("CF", "g%d" % e, col["g%d" % e], col["r32"], -0.0625, 7.0 - e - 1.0 / 2048)
+        aff("CF", "g%d" % e, col["g%d" % e], col["r32"], -0.0625, 7.0 - e + SELF / PLACE)
     act("CF", "s0", col["s0"], col["r32"], F.Sign, bias=-1.0)
     aff("h CF", "dR", col["dR"], col["e"], 20.0, col["h"])
     aff("CF", "dV", col["dV"], col["r32"], 0.0625, col["e"])
@@ -316,133 +338,192 @@ def rank_program(g, core, T, topo):
     aff("CF", "jump", col["jump"], col["r1"], 80.0, 33.0)
     aff("CF", "q4", col["q4"], col["i3"], 2.0, col["k1"])
     aff("CF", "m", col["m"], col["h16"], 1.0, col["i"])
-    aff("CF", "i8", col["i8"], col["i3"], 8.0, 0.0)
+    aff("CF", "i8", col["i8"], col["i3"], 8.0, 56.0)
     aff("dT CF", "dT", col["dT"], col["e"], 32.0, col["dT"])
     aff("g0 s0", "g0", col["g0"], col["g0"], col["s0"], 0.0)
-    sfill("SW0", T.SW[:, 3, 39:40], 1, 0.0)
     aff("dR q4", "dR", col["dR"], col["q4"], 2.0, col["dR"])
-    sfill("Q30", T.Q3[:, 0:120:3], 40, 0.0)
-    sfill("D0r", T.D0[:, SEG - 1:20 * SEG:SEG], 20, BIG)
-    sfill("PNpad", T.PN[:, 120:160], 40, 0.0)
-    aff("s0", "s0", col["s0"], col["s0"], 1.0 / 2048, 0.0)
+    aff("s0", "s0", col["s0"], col["s0"], 1.0 / PLACE, 0.0)
     aff("sg dT", "dT", col["dT"], col["sg"], 64.0, col["dT"])
-    aff("NI dR", "l1r", T.CL[:, 0:5], T.NI[:, 0:5], 0.5, col["dR"])
-    sfill("Mmb", T.Mm[:, 8:216:9], 24, -2048.0, "Mm")
-    sfill("Mma", T.Mm[:, 0:216:9], 24, 0.0, "Mm")
+    act("CF", "i7", col["i7"], col["i"], F.Abs, bias=-7.5)
+    aff("CF", "q1", col["q1"], col["r1"], 1.0, -1.0)
+    gfill("Mm", "Mmb", T.Mm[:, 8:216:9], 24, -PLACE)
+    gfill("Mm", "Mma", T.Mm[:, 0:216:9], 24, 0)
     for k in range(3):
-        sfill("Mm%d" % k, T.Mm[:, 72 * k + 11:72 * k + 62:10], 6, -1.0, "Mm")
-    sfill("Mmb", T.Mm[:, 71:216:72], 3, 2048.0)
-    next(theirs)
-    act("QU CAa CAb", "QABs", T.SQAB[:], T.SQU[:].indirect(cu(CAB)))
-    next(theirs)
-    cp("QU CAa CAb", "QABc", words(T.QAB[:]), words(T.QU[:]).indirect(cu(CAB)))
-    next(theirs)
-    quant("Ypad", "QYpad", "QY", 0, 128, T.Yt[:, 0:512])
-    ts("t8 dT", "CUt", cu(CT), T.t8[:, 0:2], 8.0, A.mult, col["dT"], A.add)
+        gfill("Mm", "Mm%d" % k, T.Mm[:, 72 * k + 11:72 * k + 62:10], 6, -1)
+    gfill("", "Mmb", T.Mm[:, 71:216:72], 3, PLACE)
+    iota("xc", T.xc[:], [[32, 20]], 0)
+    iota("C1", T.C1[:], [[32, 20], [0, 4]], 0, -SELF)
+    gfill("", "DL", T.DL[:, 16:48, :], 128, 0)
+    gfill("", "DL1", T.DL[:, 1:16:2, :], 32, PLACE)
+    gfill("", "FL", T.FL[:, 17:48, :], 124, 1)
+    gfill("", "FL0", T.FL[:, 0, :], 4, 0)
+    gfill("", "FLa", T.FL[:, 1:16:2, :], 32, 1)
+    gfill("", "CLpad", T.CL[:, 11:16:2], 3, 0)
+
+    def fills(k):
+        if k == 0:
+            iota("CK", T.CK[:], [[C, 2], [128, 4]], 1, -64)
+            gfill("", "SW0", T.SW[:, 3, 47:48], 1, 0)
+            for j, c in ((47, 97), (80, -4096)):
+                gfill("ST", "ST%d" % j, T.ST[:, j:5 * SEG:SEG], 5, c)
+            gfill("", "D0r", T.D0[:, SEG - 1:20 * SEG:SEG], 20, BIG)
+        if k == 1:
+            gfill("", "KKpad", T.KK[:, 20:32], 12, 0)
+            iota("OF", T.OF[:], [[0, 10], [1, 3]], 0)
+            gfill("", "Tin2", T.Tin[:, 40:52, 3:8:4], 24, -1)
+            gfill("", "Tin3", T.Tin[:, 0:40, 2:8:4], 80, -1)
+        if k == 2:
+            gfill("", "Q30", T.Q3[:, 0:240:6], 40, 0)
+            gfill("", "Q31", T.Q3[:, 1:240:3], 80, 1)
+        if k == 3:
+            gfill("", "PNpad", T.PN[:, :, 120:192], 144, 0)
 
     def lists_of_the_table():
-        yield ts("CF", "x1", col["x1"], col["e"], col["r0"], A.not_equal, 2.0, A.mult)
-        yield ts("CF", "x2", col["x2"], col["k1"], col["r0"], A.not_equal, 112.0, A.mult)
-        yield ts("CF", "x3", col["x3"], col["i3"], col["r1"], A.not_equal, 56.0, A.mult)
-        yield ts("NJ", "l1", T.l1[:, 0:5], T.NJ[:, 0:5], 40.0, A.is_ge, 20.0, A.mult)
-        yield ts("CF", "m8", col["m8"], col["i"], 8.0, A.is_equal)
-        yield ts("CF x1", "sh", col["sh"], col["k0"], col["r1"], A.is_equal, col["x1"], A.add)
-        yield ts("CF q4", "kb", col["kb"], col["k0"], col["q4"], A.add, 3.0, A.min)
-        yield ts("x2 x3 dV", "a0", col["a0"], col["x2"], col["x3"], A.add, col["dV"], A.add)
-        yield ts("x3 i8", "a3", col["a3"], col["x3"], -2.0, A.mult, col["i8"], A.add)
-        yield tt("l1r l1", "CLr", T.CL[:, 8:13], T.CL[:, 0:5], T.l1[:, 0:5], A.add)
-        yield ts("CF m8", "hm", col["hm"], col["h16"], col["m8"], A.mult)
-        yield ts("sh kb", "dS", col["dS"], col["sh"], 56.0, A.mult, col["kb"], A.add)
-        yield ts("a3 CF", "a2", col["a2"], col["a3"], 44.0, A.add, col["i3"], A.mult)
-        yield ts("a3 a0", "a1", col["a1"], col["a3"], 56.0, A.add, col["a0"], A.add)
-        yield cp("CLr", "CUr", cu(CR), T.CL[:, 8:13])
-        yield ts("NI dS", "l1s", T.CL[:, 6:8], T.NI[:, 0:2], 1.75, A.mult, col["dS"], A.add)
-        yield ts("a2 a1", "a2", col["a2"], col["a2"], -1.0, A.mult, col["a1"], A.add)
-        yield ts("a0 a1", "a0", col["a0"], col["a0"], 12.0, A.add)
-        for lo, hi, a in ((0, 2, "a1"), (2, 3, "a2"), (3, 5, "a0")):
-            yield ts("NI " + a, "CUv%d" % lo, T.CU[:, CV[0] + lo:CV[0] + hi], T.NI[:, lo:hi], 0.5, A.mult, col[a], A.add)
-        yield ts("l1s", "CUs", cu(CS), T.CL[:, 6:8], 24.0, A.add)
+        def line(W, a, scale, bias, f=F.Identity):
+            R = " ".join(n for n in (a, scale, bias) if isinstance(n, str))
+            act("CF " + R, W, col[W], col[a], f, scale=col.get(scale, scale), bias=col.get(bias, bias))
+
+        def entries(W, out, lo, hi, step, first):
+            aff("NI " + first, W, out, T.NI[:, lo:hi], step, col[first])
+        yield line("dR2", "i3", 20.0, "dR")
+        yield line("dR3", "dR", 1.0, 20.0)
+        yield line("n0", "r0", -1.0, 0.0)
+        yield line("n1", "r1", -1.0, 0.0)
+        yield line("dU", "r32", 0.0625, "h")
+        yield line("u1", "k0", 16.0, 224.0)
+        yield line("u0", "i3", 1.0, "n0", F.Square)
+        yield line("dU", "e", 8.0, "dU")
+        yield line("u1", "k1", -32.0, "u1")
+        for lo, hi, a in ((0, 2, "dR"), (2, 3, "dR2"), (3, 5, "dR3")):
+            yield entries("CLr%d" % lo, T.CL[:, lo:hi], lo, hi, 0.5, a)
+        yield line("dU", "u0", -128.0, "dU")
+        for W, a, n in (("x1", "e", "n0"), ("x2", "k1", "n0"), ("x3", "i3", "n1"), ("sh", "k0", "n1")):
+            yield line(W, a, 1.0, n, F.Square)
+        yield line("dU", "u1", 1.0, "dU")
+        yield line("kb", "q4", -1.0, 3.0)
+        yield line("m8", "i", 1.0, -8.0, F.Abs)
+        yield line("x2", "x2", 112.0, "dV")
+        yield line("a3", "x3", -112.0, "i8")
+        yield line("x1", "x1", 112.0, 83.0)
+        yield line("kb", "k0", -1.0, "kb", F.Relu)
+        yield line("m8", "m8", -1.0, 1.0, F.Relu)
+        yield line("a0", "x3", 56.0, "x2")
+        yield line("a2", "a3", -1.0, 12.0)
+        yield line("sh", "sh", -56.0, "x1")
+        yield line("hm", "h16", "m8", 0.0)
+        yield line("a1", "a3", 1.0, "a0")
+        yield line("a0", "a0", 1.0, 12.0)
+        yield line("dS", "kb", -1.0, "sh")
+        yield line("a2", "a2", "i3", "a1")
+        yield entries("CLv0", T.CL[:, 6:8], 0, 2, 0.5, "a1")
+        yield entries("CLv3", T.CL[:, 9:11], 3, 5, 0.5, "a0")
+        yield entries("CLs", T.CL[:, 12:15:2], 0, 2, 1.75, "dS")
+        yield entries("CLv2", T.CL[:, 8:9], 2, 3, 0.5, "a2")
 
     def tables():
         yield aff("xc m", "xc", T.xc[:], T.xc[:], 1.0, col["m"])
         yield aff("C1 m", "C1", T.C1[:], T.C1[:], 1.0, col["m"])
-        yield aff("CK m", "CK", T.CK[:], T.CK[:], 1.0, col["m"])
-        for k, c in ((47, 97.0), (80, -4096.0)):
-            yield sfill("ST%d" % k, T.ST[:, k:5 * SEG:SEG], 5, c, "ST")
+        yield act("xc", "xcb", T.xcb[:], T.xc[:], scale=-BIG)
+        yield aff("C1", "CZ", T.CZ[:], T.C1[:], 1024.0, SHIFT + 1024.0 * SELF)
+        yield aff("CK", "CK", T.CK[:], T.CK[:], 1024.0, 0.0)
         for k, c in ((15, "jump"), (79, "end")):
             yield aff("ST " + c, "ST%d" % k, T.ST[:, k:5 * SEG:SEG], T.ST[:, k:5 * SEG:SEG], col[c], 0.0)
-        yield act("xc", "xcb", T.xcb[:], T.xc[:], scale=-BIG)
-        yield aff("C1", "CZ", T.CZ[:], T.C1[:], 1024.0, SHIFT - 1024.0)
-        yield aff("CK", "CK", T.CK[:], T.CK[:], 1024.0, -LAST - 1.0)
     late, later = lists_of_the_table(), tables()
 
-    def gap(k):
-        for _ in range(GAPS[k]):
+    def some_lists(k):
+        for _ in range(k):
             next(late, None)
 
-    def sgap(k):
+    def some_tables(k):
         for _ in range(SGAPS[k]):
             next(later, None)
+
+    def as_offsets(k):
+        if k == 0:
+            cp("CLr0 CLr2 CLr3", "CUr", cu(CR), T.CL[:, 0:5])
+        else:
+            cp("CLv0 CLv2 CLv3 CLs CLpad", "CUv", T.CU[:, CV[0]:CV[0] + 10], T.CL[:, 6:16])
+    some_lists(AHEAD)
+    next(theirs)
+    pairs(0)
+    tile_e(1, 3)
+    next(theirs)
+    pairs(1)
+    pairs(4)
+    next(theirs)
 
     for t in range(3):
         u = upper(t)
         B0, Bp, b0 = C * u, C - C * u, 10 * u
-        QF, G, B, PO, PP, VV, MP = ["%s%d" % (n, t) for n in ("QF", "G", "B", "PO", "PP", "VV", "MP")]
-        mo = T.MO[:, 20 * t:20 * t + 20]
+        QF, G, B, PQ, VV, MP = ["%s%d" % (n, t) for n in ("QF", "G", "B", "PQ", "VV", "MP")]
+        PO, PP = "PO%d" % t, "PP%d" % t
         win = "%s %s# " % (QF, QF)
+        kv = keys(VV + "_%d", 4) + " CUv"
+
+        def lists(who, e, lo=0, hi=20):
+            return T[PQ][:, 40 * who + 20 * e + lo:40 * who + 20 * e + hi]
 
         def unpack(h, e, x, at, R, start, stop):
             for b in range(4):
                 mm(4 * h + b, "QE", 512 * e + 128 * b, x, at + CUT[h], CUT[h + 1] - CUT[h], "QE%d%d %s" % (e, b, R), start, stop)
 
-        def marked():
-            for e in range(2):
-                aff("PS PZ s0 g%d" % e, "PZ%d" % e, T.PZ[:, 32 * e + 4:32 * e + 24], T.PS[:, 20 * e:20 * e + 20],
-                    1.0 / 2048 if e else col["s0"], col["g%d" % e])
-        if t == 0:
-            marked()
-            gap(5)
-        for e in range(2):
-            pick(win + PO, "Go%d" % e, G, 640 * e + B0, QF, 0, T[PO][:, 20 * e:20 * e + 20])
+        def own_pick(e):
+            pick(win + PO + "ab"[e], "Go%d" % e, G, 640 * e + B0, QF, 0, lists(u, e))
             for h in range(2):
                 unpack(h, e, G, 640 * e + B0, "Go%dc Go%ds" % (e, e), e == 0, False)
-            if e == 0 and t:
-                tt("ne PN", "PS", T.PS[:], T.ne[:], pn, A.mult)
-        if t:
-            marked()
-        for e in range(2):
-            pick(win + PP, "Gp%d" % e, G, 640 * e + Bp, QF, 0, T[PP][:, 20 * e:20 * e + 20])
-        for h in range(2):
-            for e in range(2):
-                pick("Go%d# Gp%d# %s" % (e, e, PO), "B%d%d" % (e, h), B, C * e + CUT[h], G, 640 * e,
-                     T[PO][:, 20 * e + CUT[h] // 16:20 * e + CUT[h + 1] // 16])
-                unpack(h, e, B, C * e, "B%d%dc B%d%ds" % (e, h, e, h), False, e == 1)
-        spread1("PZ0 PZ1", "PZ", T.PZ, 56, 64)
-        sgap(0)
-        ts(PP, "PAp", T.PA[:, 40 - 40 * u:80 - 40 * u], T[PP][:], 1.0, A.add)
-        ts(PO, "PAo", T.PA[:, 40 * u:40 * u + 40], T[PO][:, 0:40], 1.0, A.add)
-        gap(0)
-        for step in TAIL.split():
-            k = int(step[1])
+
+        def partner_pick(e):
+            pick(win + PP + "ab"[e], "Gp%d" % e, G, 640 * e + Bp, QF, 0, lists(1 - u, e))
+
+        def second_pick(k):
+            h, e = divmod(k, 2)
+            pick("Go%d# Gp%d# %s" % (e, e, PO + "ab"[e]), "B%d%d" % (e, h), B, C * e + CUT[h], G, 640 * e,
+                 lists(u, e, CUT[h] // 16, CUT[h + 1] // 16))
+            unpack(h, e, B, C * e, "B%d%dc B%d%ds" % (e, h, e, h), False, e == 1)
+
+        def y_part(k):
             h, b = divmod(k, 4)
-            if step[0] == "q":
-                gap(1 + k)
-                quant(keys("Y%d", range(4 * k, 4 * k + 4)), "QY%d" % k, "QY", 64 + CUT[k], 64 + CUT[k + 1],
-                      T.Yt[:, 4 * CUT[k]:4 * CUT[k + 1]])
-                continue
-            out, part = T.Yt[:, 4 * CUT[h] + b:4 * CUT[h + 1]:4], ps(k, CUT[h + 1] - CUT[h])
-            if step[0] == "s":
-                act("ps%d QYpad" % k, "Y%d" % k, out, part, scale=0.5)
-                if k == 3:
-                    sgap(1)
-            else:
-                ts("ps%d QYpad" % k, "Y%d" % k, out, part, 0.5, A.mult)
-        gap(3)
-        if t == 1:
-            quant("vin", "QV", "QV", 0, 128, T.vin[:])
-        spread2("PZ", T.PZ, 56, 64)
-        for k in range(3):
-            mm(k, "QY", 128 * k, "QAB", 0, 160, "QY%d QABc QABs" % (k // 2))
+            return T.Yt[:, 4 * CUT[h] + b:4 * CUT[h + 1]:4], ps(k, CUT[h + 1] - CUT[h])
+
+        def y_vector(k):
+            ts("ps%d" % k, "Y%d" % k, *y_part(k), 0.5, A.mult)
+
+        def y_scalar(k):
+            act("ps%d" % k, "Y%d" % k, *y_part(k), scale=0.5)
+
+        def y_quant(k):
+            quant(keys("Y%d", range(4 * k, 4 * k + 4)), "QY%d" % k, "QY", 64 + CUT[k], 64 + CUT[k + 1], T.Yt[:, 4 * CUT[k]:4 * CUT[k + 1]])
+
+        def pointers(k):
+            if k == 0:
+                tt("PN0 PN1 YJ", "ne", T.ne[:], pn, T.YJ[:, 40 * u:40 * u + 40], A.not_equal)
+            if k == 1:
+                tt("ne PN0 PN1", "PS", T.PS[:], T.ne[:], pn, A.mult)
+            if k == 2:
+                for e in range(2):
+                    ts("PS PZ s0 g%d" % e, "PZ%d" % e, T.PZ[:, 32 * e + 4:32 * e + 24], T.PS[:, 20 * e:20 * e + 20],
+                       1.0 / PLACE if e else col["s0"], A.mult, col["g%d" % e], A.add)
+            if k == 3:
+                spread1("PZ0 PZ1", "PZ", T.PZ, 0, 64, "g")
+            if k == 4:
+                spread2("PZ", T.PZ, 0, 64, "g")
+            if k == 5:
+                act(keys("PZ_%d", 4) + " CUt Mm", "PT", T.Mm[:, 1:288:9], T.PZ[:].indirect(cu(CT)))
+            if k == 6:
+                ts("%sa %sb %sa %sb" % (PO, PO, PP, PP), "PA", T.PA[:], T[PQ][:], -float(SELF), A.add)
+            if k == 7:
+                act("PA CUr", "VR", T.VR[:], T.PA[:].indirect(cu(CR)))
+
+        def products(k):
+            if k < 3:
+                mm(k, "QY", 128 * k, "QAB", 0, 160, "QY%d QYpad QYpad2 QABc QABs" % (k // 2))
+            if k == 5:
+                mm(3, "QY", 256, "QAB", 32, 128, "QY1 QABc QABs")
+            for b in {3: (0, 1), 7: (2, 3)}.get(k, ()):
+                mm(4 + b, "QW", 128 * b, "QY", 64, C, "QW QW2 QY0 QY1")
+            for b in {6: (0,), 4: (1, 2, 3)}.get(k, ()):
+                for e in range(2):
+                    mm((3 + b) % 4, "QE", 512 * e + 128 * b, QF, B0, C, "QE%d%d %s" % (e, b, QF), e == 0, e == 1)
 
         def other_side(k):
             act("ps%d" % k, "SL%d" % k, T.SL[:, 72 * k:72 * k + 72], T["ps%d" % k][:, 80:152])
@@ -451,44 +532,44 @@ def rank_program(g, core, T, topo):
             tt("ps%d SL%d" % (k, k), "D%d" % k, T.D[:, 72 * k:72 * k + 72], ps(k, 72), T.SL[:, 72 * k:72 * k + 72], A.is_ge)
 
         def places(k):
-            scan("D%d PT SC Mma Mmb Mm%d" % (k, k), "SC%d" % k, T.SC[:, 360 * k:360 * k + 72], T.Mm[:, 72 * k:72 * k + 72],
+            scan("D%d PT Mma Mmb Mm%d" % (k, k), "SC%d" % k, T.SC[:, k, 0:72], T.Mm[:, 72 * k:72 * k + 72],
                  T.D[:, 72 * k:72 * k + 72], 0.0, A.mult, A.add)
 
-        def largest(k):
-            v = T.SC[:, 360 * k + 8:360 * k + 360:9]
-            scan("SC%d" % k, "SW%d" % k, T.SW[:, k, :], v, v, 0.0, A.max, A.max)
+        def least(k):
+            bank, at = ((0, 72), (1, 72), (3, 40))[k]
+            scan("ps%d DL" % bank, "RM%d" % k, T.RM[:, k, :], T["ps%d" % bank][:, at:at + 8], T.DL[:, 16:24, 0], 1e29, A.min, A.add)
 
-        def differ(k):
-            tt("C1 VR", "dd", T.dd[:], T.C1[:], T.VR[:], A.subtract)
+        def reached(k):
+            ts("RM%d" % k, "FL%d" % (k + 1), T.FL[:, 2:18:2, k], T.RM[:, k, :], T.RM[:, k, 7:8], A.is_le)
+
+        def asked(k):
+            scan("FL FL0 FLa FL%d DL DL1 DLa DLb DLc" % (k + 1), "SW%d" % k, T.SW[:, k, :], T.FL[:, :, k], T.DL[:, :, k],
+                 0.0, A.mult, A.add)
+
+        def steps_down(k):
+            if k == 0:
+                act(keys("PZ_%d", 4) + " CUd0 CUd1", "PD", T.PD[:], T.PZ[:].indirect(cu(CD)), scale=PLACE)
+            if k == 2:
+                tt("PD", "DLa", T.DL[:, 0:12:2, :], T.PD[:, 0:24], T.PD[:, 4:28], A.subtract)
+                tt("PD", "DLb", T.DL[:, 12, :], T.PD[:, 24:28], T.PD[:, 28:32], A.add)
+                ts("PD", "DLc", T.DL[:, 14, :], T.PD[:, 28:32], -1.0, A.mult, -8 * PLACE, A.add)
 
         def along(k):
             if k == 0:
-                turn("SW0", "AT", T.AT[64:128, :], T.SW[64:128, 0, 8:40])
+                turn("SW0", "AR0 AR1", T.AR[64:128, 16:48], T.SW[64:128, 0, 16:48])
             elif k == 3:
-                cp("AT", "AR3", T.AR[0:64, 0:16], T.AT[64:128, 16:32])
-                cp("AT", "AR0", T.AR[64:128, 0:16], T.AT[64:128, 0:16])
+                turn("SW0", "AR3", T.AR[0:64, 0:32], T.SW[64:128, 0, 16:48])
             else:
-                turn("SW%d" % k, "AR%d" % k, T.AR[:, 32 * k - 16:32 * k + 16], T.SW[:, k, 8:40])
-        other_side(0)
-        other_side(1)
-        act(keys("PZ_%d", 4) + " CUt Mm", "PT", T.Mm[:, 1:288:9], T.PZ[:].indirect(cu(CT)))
-        sgap(2)
-        other_side(2)
-        act("PAo PAp CUr", "VR", T.VR[:], T.PA[:].indirect(cu(CR)))
-        for step in ORDER.split():
-            {"c": compare, "p": places, "l": largest, "a": along, "g": gap, "d": differ}[step[0]](int(step[1]))
-        for b in range(4):
-            mm(4 + b, "QW", 128 * b, "QY", 64, C, "QW QW2 QY0 QY1")
+                turn("SW%d" % k, "AR%d" % k, T.AR[:, 32 * k:32 * k + 32], T.SW[:, k, 16:48])
 
-        def relu(lo, hi):
-            for b in range(lo, hi):
-                act("ps%d" % (4 + b), "TB%d" % b, T.TB[:, C * b:C * b + C], ps(4 + b), F.Relu, scale=0.03125)
-        relu(0, EARLY)
-        for b in range(4):
-            for e in range(2):
-                mm((3 + b) % 4, "QE", 512 * e + 128 * b, QF, B0, C, "QE%d%d %s" % (e, b, QF), e == 0, e == 1)
-        for k in range(3):
-            act("SC%d" % k, "%sv%d" % (VV, k), T[VV][:, 28 * u + 8 * k:28 * u + 8 * k + 8], T.SC[:, 360 * k + 8:360 * k + 72:9])
+        def relu(b):
+            act("ps%d" % (4 + b), "TB%d" % b, T.TB[:, C * b:C * b + C], ps(4 + b), F.Relu, scale=0.03125)
+
+        def v_out(k):
+            act("SC0 SC1 SC2", VV + "v", T[VV][:, 28 * u:28 * u + 24], T.SC[:, :, 8:72:9])
+
+        def key_out(k):
+            tt("SW0 SW1 SW2 CK", VV + "k", T[VV][:, 28 * u + 24:28 * u + 28], T.SW[:, :, 47], T.CK[:, 4 * u:4 * u + 4], A.add)
 
         def state(n):
             for b in range(4):
@@ -497,95 +578,166 @@ def rank_program(g, core, T, topo):
                     k = (3 + b) % 4
                     tt("TB%d ps%d" % (b, k), "X%d%d" % (n, b), T.Xt[:, 4 * lo + b:4 * hi:4], T.TB[:, C * b + lo:C * b + hi],
                        T["ps%d" % k][:, lo:hi], A.add)
-        act("SW0 SW1 SW2", VV, T[VV][:, 28 * u + 24:28 * u + 28], T.SW[:, :, 39])
-        send(t, "av%d" % t, VV + " " + keys(VV + "v%d", 3), VV + "p", T[VV][:, 28 * u:28 * u + 28], T[VV][:, 28 * u:28 * u + 28])
-        state(0)
-        for j in range(ON_V, 20):
-            act(keys("AR%d", 4) + " xcb", "D0_%d" % j, T.D0[:, SEG * j:SEG * j + 80], T.AR[:], F.Abs, scale=BIG, bias=T.xcb[:, j:j + 1])
-        relu(EARLY, 4)
-        for j in range(ON_V):
-            ts(keys("AR%d", 4) + " xc", "D0_%d" % j, T.D0[:, SEG * j:SEG * j + 80], T.AR[:], T.xc[:, j:j + 1], A.not_equal, BIG, A.mult)
-        for lo, hi in SCANS:
+
+        def match(k):
+            for j in range(ON_V, 20) if k else range(ON_V):
+                out = T.D0[:, SEG * j:SEG * j + 80]
+                if k:
+                    act(keys("AR%d", 4) + " xcb", "D0_%d" % j, out, T.AR[:, 16:96], F.Abs, scale=BIG, bias=T.xcb[:, j:j + 1])
+                else:
+                    ts(keys("AR%d", 4) + " xc", "D0_%d" % j, out, T.AR[:, 16:96], T.xc[:, j:j + 1], A.not_equal, BIG, A.mult)
+
+        def first(k):
+            lo, hi = SCANS[k]
             scan(keys("D0_%d", range(lo, hi)) + " D0r ST15 ST47 ST79 ST80", "SO%d" % lo, T.SO[:, SEG * lo:SEG * hi],
                  T.D0[:, SEG * lo:SEG * hi], T.ST[:, 0:SEG * (hi - lo)], 4096.0, A.min, A.subtract)
-        state(1)
-        ts(keys("SO%d", [lo for lo, hi in SCANS]), "KK", T.KK[:], T.SO[:, 79:20 * SEG:SEG], 160.0 + B0, A.add, 1025.0, A.mult)
-        state(2)
-        tt("KK", "M1", T.M1[0:64, :], T.KK[0:64, :], T.KK[64:128, :], A.min)
-        state(3)
-        for a in range(4):
-            tt("M1", "MO%d" % a, T.MO[32 * a:32 * a + 32, 20 * t:20 * t + 20], T.M1[0:32, :], T.M1[32:64, :], A.min)
-        send(t, "am%d" % t, keys("MO%d", 4), MP, T[MP][:], mo)
-        spread1("%s %sp %s" % (VV, VV, keys(VV + "v%d", 3)), VV, T[VV], 56, 56)
-        act("VR Tin", "Tr", T.Tin[:, 0:40, 1:8:4], T.VR[:])
-        spread2(VV, T[VV], 56, 56)
-        k = keys(VV + "_%d", 4) + " CUv0 CUv2 CUv3 CUs"
-        act(k, "vh", T.vh[:], T[VV][:].indirect(cu(CV)), F.Sign, bias=0.5 - LAST)
-        act(k, "va", T.va[:], T[VV][:].indirect(cu(CV)), F.Abs, scale=STILL, bias=-10560 * STILL)
-        act("vh", "vh", T.vh[:], T.vh[:], F.Relu)
-        if t == 0:
-            aff("YR m8 hm", "YR", T.YR[:], T.YR[:], col["m8"], col["hm"])
-        state(4)
-        tt(k + " CK", "sk0", T.sk[:, 0:32], T[VV][:].indirect(cu(CS)), T.CK[:], A.add)
-        ts(k, "sk1", T.sk[:, 32:64], T[VV][:].indirect(cu(CS)), LAST, A.is_le, NONE, A.mult)
-        if t < 2:
-            q, at = "QF%d" % (t + 1), C * upper(t + 1)
-            quant(keys("X%d%d", 5, 4), q, q, at, at + C, T.Xt[:])
-            send_codes(t + 1, q, 0, C)
-            send_scales(t + 1)
-        else:
-            quant(keys("X%d%d", 5, 4), "QX3", "QX3", 0, C, T.Xt[:])
-            mm(4, "QV", 0, "QX3", 0, C, "QV QX3")
-            dma("y", "out", "QX3", "", T.oc[:], T.QX3[:].bitcast(dt.uint8))
-            for k in range(4):
-                dma("y", "out", "QX3", "", T.osc[4 * k:4 * k + 4, :], T.SQX3[32 * k:32 * k + 4, :])
-            act("ps4", "ys", T.ys[:], ps(4))
-            dma("y", "out", "ys", "", T.y[:], T.ys[:])
-        tt("sk0 sk1", "SK", T.SK[:], T.sk[:, 0:32], T.sk[:, 32:64], A.max)
-        tt("vh dd Tin", "Th", T.Tin[:, 0:40, 0:8:4], T.vh[:], T.dd[:], A.mult)
-        tt("va CZ Tin", "Tz", T.Tin[:, 0:40, 3:8:4], T.va[:], T.CZ[:], A.min)
-        for w in range(2):
-            tt(keys("MO%d", 4) + " SK", "MQ%d" % w, T.MQ[:, 10 * w:10 * w + 10], T.MO[:, 20 * t + 10 * w:20 * t + 10 * w + 10],
-               T.SK[:, 16 * w:16 * w + 10], A.min)
-        tt("Th VR Tin", "Tg", T.Tin[:, 0:40, 2:8:4], T.Tin[:, 0:40, 0:8:4], T.VR[:], A.add)
-        tt("MQ0 MQ1 " + MP, "I1", T.I1[:], T.MQ[:, b0:b0 + 10], T[MP][:, b0:b0 + 10], A.min)
-        for h in range(2):
-            tt("MQ0 MQ1 Tin " + MP, "Tk%d" % h, T.Tin[:, h:40:2, 8], T.MQ[:], T[MP][:], A.min)
-        turn("Tz", "T1", T.T1[:], T.Tin[:, 2 * b0:2 * b0 + 32:2, 3:8:4])
-        for h in range(2):
-            act("T1", "Z3%d" % h, T.Z3[:, h:4:2, :], T.T1[:])
-        ts("I1", "I2", T.I2[:], T.I1[:], 1023, band)
-        turn("Tk0 Tk1 Tr Tz Th Tg", "Tout", T.Tout[:], T.Tin[:, 0:40, :])
-        for h in range(2):
-            cp("I2", "OFF%d" % h, T.OFF[:, h:20:2], T.I2[:])
-        turn("Z30 Z31", "ZT", T.ZT[:], T.Z3[:])
-        for h in range(2):
-            act("ZT", "ZO%d" % h, T.ZO[:, h:20:2, :], T.ZT[:, 32 * h:32 * h + 20])
-        for h in range(2):
-            tt("Tout OFF0 OFF1 YR", "GG%d" % h, T.GG[:, H * h:H * h + H], T.Tout[:].indirect(T.OFF[:, 10 * h:10 * h + 10]),
-               T.YR[:, B0 + H * h:B0 + H * h + H], A.subtract)
-        for h in range(2):
-            turn("GG%d" % h, "ZZ%d" % h, T.ZZ[:, 10 * h:10 * h + 10, :], T.GG[:, H * h:H * h + H])
-        for e in range(2):
-            lo, hi = 60 * e, 60 * e + 60
-            act("ZZ0 ZZ1", "S31%d" % e, T.S3[:, lo + 1:hi:3], T.ZZ[:, :, 4 * e])
-            aff("ZZ0 ZZ1", "S32%d" % e, T.S3[:, lo + 2:hi:3], T.ZZ[:, :, 4 * e + 1], 1.0, -1.0 if t == 2 else 0.0)
-            tt("ZZ0 ZZ1 PN", "S30%d" % e, T.S3[:, lo:hi:3], T.PN[:, lo + 2:hi:3], T.ZZ[:, :, 4 * e + 2], A.subtract)
-            tt("ZZ0 ZZ1", "Q31%d" % e, T.Q3[:, lo + 1:hi:3], T.ZZ[:, :, 8], T.ZZ[:, :, 4 * e + 3], A.not_equal)
-            tt("ZZ0 ZZ1 ZO0 ZO1", "Q32%d" % e, T.Q3[:, lo + 2:hi:3], T.ZZ[:, :, 8], T.ZO[:, :, e], A.not_equal)
-        scan(keys("S3%d%d", 3, 2) + " Q30 " + keys("Q3%d%d", (1, 2), 2), "PN", T.PN[:, 0:120], T.Q3[:], T.S3[:], 0.0, A.mult, A.add)
-        if t < 2:
-            o = "PO%d" % (t + 1)
-            ts("PN", o, T[o][:], pn, -1.0, A.add)
-            send(t + 1, "ap%d" % (t + 1), o, "PP%d" % (t + 1), T["PP%d" % (t + 1)][:], T[o][:])
-            n = 40 * upper(t + 1)
-            tt("PN YJ", "ne", T.ne[:], pn, T.YJ[:, n:n + 40], A.not_equal)
-        else:
-            for e in range(2):
-                turn("PN PNpad", "OT%d" % e, T.OT[:, 32 * e:32 * e + 32], T.PN[:, 60 * e + 2:60 * e + 98:3])
-            for e in range(2):
+
+        def lowest(k):
+            if k == 0:
+                tt(keys("SO%d", [lo for lo, hi in SCANS]), "M1", T.M1[0:64, :], T.SO[0:64, 79:20 * SEG:SEG],
+                   T.SO[64:128, 79:20 * SEG:SEG], A.min)
+            for a in range(4 * (k == 1)):
+                tt("M1", "MO%d" % a, T.MO[32 * a:32 * a + 32, 20 * t:20 * t + 20], T.M1[0:32, :], T.M1[32:64, :], A.min)
+            if k == 2:
+                ts(keys("MO%d", 4), "KK", T.KK[:, 0:20], T.MO[:, 20 * t:20 * t + 20], 160.0 + B0, A.add, 1025.0, A.mult)
+
+        def leave(k):
+            if k == 0:
+                send(t, "av%d" % t, keys(VV + "%s", "vk"), VV + "p", T[VV][:, 28 * u:28 * u + 28], T[VV][:, 28 * u:28 * u + 28])
+            if k == 1:
+                send(t, "am%d" % t, keys("MO%d", 4), MP, T[MP][:], T.MO[:, 20 * t:20 * t + 20])
+            if k == 2 and t < 2:
+                q, at = "QF%d" % (t + 1), C * upper(t + 1)
+                quant(keys("X%d%d", 5, 4), q, q, at, at + C, T.Xt[:])
+                send_codes(t + 1, q, 0, C)
+                send_scales(t + 1)
+            if k == 2 and t == 2:
+                quant(keys("X%d%d", 5, 4), "QX3", "QX3", 0, C, T.Xt[:])
+                mm(4, "QV", 0, "QX3", 0, C, "QV QX3")
+                dma("y", "out", "QX3", "", T.oc[:], T.QX3[:].bitcast(dt.uint8))
                 for a in range(4):
-                    dma("ys"[a % 2], "out2", "OT%d" % e, "", T.ov[2 * a + e, :], T.OT[32 * a:32 * a + 20, 32 * e:32 * e + 16])
+                    dma("y", "out", "QX3", "", T.osc[4 * a:4 * a + 4, :], T.SQX3[32 * a:32 * a + 4, :])
+            if k == 3 and t == 2:
+                act("ps4", "ys", T.ys[:], ps(4))
+                dma("y", "out", "ys", "", T.y[:], T.ys[:])
+            if k == 4 and t == 1:
+                quant("vin", "QV", "QV", 0, 128, T.vin[:])
+
+        def table_scalar(k):
+            if k == 0:
+                spread1("%s %sp" % (keys(VV + "%s", "vk"), VV), VV, T[VV], 0, 56, "s")
+            if k == 1:
+                act("VR", "Tr", T.Tin[:, 0:40, 1:8:4], T.VR[:])
+            if k == 2:
+                spread2(VV, T[VV], 0, 56, "s")
+            if k == 4:
+                act(kv, "va", T.va[:], T[VV][:].indirect(cu(CV)), F.Abs, scale=STILL, bias=-MID * STILL)
+            for h in range(2 * (k == 8)):
+                act("MQ0 MQ1", "Tq%d" % h, T.Tin[:, h:40:2, 8], T.MQ[:, :, 0:10])
+                aff("MQ0 MQ1", "Tt%d" % h, T.Tin[:, h:40:2, 10], T.MQ[:, :, 0:10], 1.0 / 1025, -160.0 - Bp)
+            for e in range(2 * (k == 9)):
+                p = T.PN[:, e, 5:120:6]
+                act("PN%d" % e, "S34%d" % e, T.S3[:, 120 * e + 4:120 * e + 120:6], p, scale=-1.0)
+                aff("PN%d" % e, "S35%d" % e, T.S3[:, 120 * e + 5:120 * e + 120:6], p, 1.0, float(SELF) if t == 2 else 0.0)
+            new = u not in [upper(n) for n in range(t)]
+            if k == 6 and new:
+                aff("YR%d m8 hm" % u, "YR%d" % u, T.YR[:, B0:B0 + C], T.YR[:, B0:B0 + C], col["m8"], col["hm"])
+            if k == 7 and new:
+                iota("YR%d" % u, T.YR[:, B0:B0 + C], [[32, 10], [0, 2], [1, 16]], 0, B0 - SHIFT)
+
+        def table_vector(k):
+            if k == 0:
+                tt("C1 VR", "dd", T.dd[:], T.C1[:], T.VR[:], A.subtract)
+            if k == 1:
+                tt("vh dd", "Th", T.Tin[:, 0:40, 0:8:4], T.vh[:], T.dd[:], A.mult)
+            if k == 2:
+                tt("va CZ", "Tz", T.Tin[:, 0:40, 3:8:4], T.va[:], T.CZ[:], A.min)
+            if k == 3:
+                ts(kv, "vh", T.vh[:], T[VV][:].indirect(cu(CV)), LAST, A.is_ge)
+            for w in {4: (0, 1), 8: (u,)}.get(k, ()):
+                W, out = ("MQ%d" % w, T.MQ[:, w, :]) if k == 4 else ("I1", T.I1[:])
+                tt("KK KKpad " + kv, W, out, T[VV][:].indirect(T.CU[:, CS[0] + 2 * w:CS[0] + 2 * w + 1]), T.KK[:, 10 * w:10 * w + 16], A.min)
+            if k == 6:
+                ts("I1", "I2", T.I2[:], T.I1[:], 1023, band)
+            if k == 7:
+                gfill("", "OD1", T.OD[:, 1:30:3], 10, -160 - Bp)
+
+        def own_marks(k):
+            if k == 0:
+                turn("Tz Tin2", "T1", T.T1[:], T.Tin[:, 2 * b0:2 * b0 + 32:2, 3:8:4])
+            if k == 2:
+                turn("Z30 Z31", "ZT", T.ZT[:], T.Z3[:])
+            for h in range(2):
+                if k == 1:
+                    act("T1", "Z3%d" % h, T.Z3[:, h:4:2, :], T.T1[:])
+                if k == 3:
+                    act("ZT", "ZO%d" % h, T.ZO[:, h:20:2, :], T.ZT[:, 32 * h:32 * h + 20])
+
+        def couples(k):
+            w = T[MP][:, b0:b0 + 10]
+            if k == 0:
+                tt("I2 " + MP, "OD0", T.OD[:, 0:30:3], T.I2[:, 0:10], w, A.subtract)
+                ts(MP, "OD2", T.OD[:, 2:30:3], w, 160.0 + Bp, A.add)
+                tt("Tt0 OF " + MP, "OF2", T.OF[:, 2:30:3], w, T.Tin[:, 2 * b0:2 * b0 + 20:2, 10], A.is_gt)
+            if k == 2:
+                scan("OD0 OD1 OD2 OF2", "OM", T.OM[:], T.OF[:], T.OD[:], 0.0, A.mult, A.add)
+            if k == 3:
+                turn("Tk0 Tk1 Tq0 Tq1 Tt0 Tt1 Tr Tz Th Tin Tin3", "Tout", T.Tout[:], T.Tin[:, 0:40, :])
+            for h in range(2):
+                if k == 1:
+                    act(MP, "Tk%d" % h, T.Tin[:, h:40:2, 9], T[MP][:])
+                if k == 4:
+                    ts("OM", "OFF%d" % h, T.OFF[:, h:20:2], T.OM[:, 2:30:3], 639.0, A.min)
+                if k == 5:
+                    tt("Tout OFF0 OFF1 YR%d" % u, "GG%d" % h, T.GG[:, H * h:H * h + H], T.Tout[:].indirect(T.OFF[:, 10 * h:10 * h + 10]),
+                       T.YR[:, B0 + H * h:B0 + H * h + H], A.subtract)
+                if k == 6:
+                    turn("GG%d" % h, "ZZ%d" % h, T.ZZ[:, 10 * h:10 * h + 10, :], T.GG[:, H * h:H * h + H])
+
+        def terms(e):
+            lo, hi = 120 * e, 120 * e + 120
+            p, theirs = T.PN[:, e, 5:120:6], T.ZZ[:, :, 4 * e + 1]
+            act("ZZ0 ZZ1", "S31%d" % e, T.S3[:, lo + 1:hi:6], T.ZZ[:, :, 4 * e], scale=-1.0)
+            act("ZZ0 ZZ1", "S32%d" % e, T.S3[:, lo + 2:hi:6], T.ZZ[:, :, 4 * e])
+            act("ZZ0 ZZ1", "S33%d" % e, T.S3[:, lo + 3:hi:6], theirs)
+            tt("ZZ0 ZZ1 PN%d" % e, "S30%d" % e, T.S3[:, lo:hi:6], p, theirs, A.subtract)
+            tt("ZZ0 ZZ1", "Q32%d" % e, T.Q3[:, lo + 2:hi:6], T.ZZ[:, :, 8], T.ZZ[:, :, 4 * e + 3], A.not_equal)
+            tt("ZZ0 ZZ1 ZO0 ZO1", "Q33%d" % e, T.Q3[:, lo + 3:hi:6], T.ZZ[:, :, 8], T.ZO[:, :, e], A.not_equal)
+            tt("ZZ0 ZZ1", "Q35%d" % e, T.Q3[:, lo + 5:hi:6], T.ZZ[:, :, 9], T.ZZ[:, :, 10], A.is_gt)
+
+        def swap(e):
+            lo, hi = 120 * e, 120 * e + 120
+            scan(keys("S3%d%d", 6, (e,)) + " Q30 Q31 " + keys("Q3%d%d", (2, 3, 5), (e,)), "PN%d" % e, T.PN[:, e, 0:120], T.Q3[:, lo:hi],
+                 T.S3[:, lo:hi], 0.0, A.mult, A.add)
+
+        def handed(e):
+            if t < 2 and WHOLE:
+                if e:
+                    n = t + 1
+                    new, o = T["PQ%d" % n][:, 40 * upper(n):40 * upper(n) + 40], "PO%da PO%db" % (n, n)
+                    ts("PN0 PN1", o, new, pn, float(SELF), A.add)
+                    send(n, "ap%d" % n, o, o.replace("O", "P"), new, new)
+                return
+            if t < 2:
+                n = t + 1
+                at = 40 * upper(n) + 20 * e
+                new, o = T["PQ%d" % n][:, at:at + 20], "PO%d%s" % (n, "ab"[e])
+                ts("PN%d" % e, o, new, T.PN[:, e, 5:120:6], float(SELF), A.add)
+                send(n, "a%s%d" % ("pq"[e], n), o, o.replace("O", "P"), new, new)
+                return
+            turn("PN%d PNpad" % e, "OT%d" % e, T.OT[:, 32 * e:32 * e + 32], T.PN[:, e, 5:192:6])
+            for a in range(4):
+                dma("ys"[a % 2], "out2", "OT%d" % e, "", T.ov[2 * a + e, :], T.OT[32 * a:32 * a + 20, 32 * e:32 * e + 16])
+
+        steps = {"G": own_pick, "P": partner_pick, "B": second_pick, "v": y_vector, "s": y_scalar, "q": y_quant, "z": pointers,
+                 "m": products, "o": other_side, "c": compare, "p": places, "M": least, "R": reached, "l": asked, "D": steps_down, "a": along, "r": relu, "w": v_out,
+                 "k": key_out, "x": state, "d": match, "f": first, "n": lowest, "L": leave, "S": table_scalar, "V": table_vector,
+                 "O": own_marks, "K": couples, "t": terms, "u": swap, "h": handed,
+                 "A": pairs, "F": fills, "e": some_lists, "g": as_offsets, "j": some_tables}
+        for step in ROUND[t].split():
+            if t and step[0] in "AFegj":
+                continue
+            steps[step[0]](int(step[1]))
 
     for s, n in count.items():
         if seen.get(s, 0) < n:

from concourse.mybir import dt, AluOpType as A, ActivationFunctionType as F

C = 320
STEP = [2, 1, 3]
CODE = "float8_e4m3fn_x4"
CUT = (0, 192, 320)
SEG = 81
BIG = 16384.0
PLACE = 1048576.0
LAST = 7 * PLACE
SELF = 786432
SHIFT = 4194304
STILL, MID = 2.875, 5.375 * PLACE
ON_V = 8
SCANS = ((0, 4), (8, 13), (4, 8), (13, 16), (16, 18), (18, 20))
PIECES = (0, 224, 448, 672, 960, 1280)
FIRST = 128
WHOLE = False
AHEAD = 22
SGAPS = (2, 2, 1, 2)
PICKS = ["e9 z0 A2 z1 G0 A3 z2 G1 z3 z4 V7 F0 S7 P0 P1 B0 B1 B2 B3 A7 A5 j0 e9 A6 ",
         "z0 G0 z1 G1 z2 z3 z4 V7 S7 P0 P1 B0 B1 B2 B3 "]
REST = ("v0 s1 s3 v2 g0 z6 q0 m0 m1 s4 s5 v6 s7 D0 z7 j1 j2 z5 q1 m5 m2 m3 "
        "M0 M1 D2 L4 o0 o1 R0 V0 R1 M2 m6 m7 o2 l0 c0 c1 R2 l1 r0 a0 c2 m4 p0 l2 a3 p1 r1 p2 w2 a1 a2 k2 L0 x0 F1 j3 "
        "d0 f0 g1 d1 f1 f2 f3 f4 f5 r2 x1 n0 x2 n1 L1 S0 r3 x3 n2 S2 S1 S4 x4 V3 V8 V4 S8 L2 F2 V6 V2 V1 "
        "K1 S6 S9 K0 O0 K2 K3 K4 O1 O2 F3 K5 O3 L3 K6 t0 t1 u0 u1 h0 h1")
ROUND = [PICKS[0] + REST, PICKS[1] + REST, PICKS[1] + REST]

SCRATCH = {}


def _buf(name, n, dtype, where="sbuf"):
    SCRATCH[name] = (where, [128] + (n if isinstance(n, list) else [n]), dtype)


for _k in range(8):
    _buf("ps%d" % _k, 512, "float32", "psum")
for _n, _w in (("xin", 1280), ("uin", 512), ("vin", 512), ("Xt", 1280), ("Yt", 1280), ("Z", 1040), ("D0", 20 * SEG), ("SO", 20 * SEG),
               ("ST", 5 * SEG), ("D", 216)):
    _buf(_n, _w, "bfloat16")
for _n, _w in (("QF0", 640), ("QF1", 640), ("QF2", 640), ("G0", 1280), ("G1", 1280), ("G2", 1280), ("B0", 640), ("B1", 640), ("B2", 640),
               ("QX3", C), ("QY", 384), ("QE", 1024), ("QW", 512), ("QU", 128), ("QAB", 160), ("QV", 128)):
    _buf(_n, _w, CODE)
    _buf("S" + _n, _w, "uint8")
for _n, _w in (("TB", 1280), ("SL", 216), ("Mm", 288), ("SC", [3, 72]), ("VR", 80), ("SW", [4, 48]), ("AR", 96), ("KK", 32),
               ("FL", [48, 4]), ("DL", [48, 4]), ("RM", [3, 8]), ("PD", 32), ("OD", 30), ("OF", 30), ("OM", 30),
               ("M1", 20), ("MO", 60), ("MQ", [2, 16]), ("MP0", 20), ("MP1", 20), ("MP2", 20),
               ("VV0", 224), ("VV1", 224), ("VV2", 224), ("Tin", [52, 16]), ("Tout", 640), ("GG", C), ("ZZ", [20, 16]),
               ("va", 80), ("vh", 80), ("dd", 80), ("T1", 32), ("Z3", [4, 16]), ("ZT", 64),
               ("ZO", [20, 2]), ("Q3", 240), ("S3", 240), ("PN", [2, 192]),
               ("ne", 40), ("PS", 40), ("PZ", 256), ("PA", 80), ("OT", 64), ("ys", C),
               ("idm", 128), ("CF", 48), ("NI", 8), ("NJ", 8), ("t8", 8), ("CL", 32), ("xc", 20), ("xcb", 20),
               ("YJ", 80), ("YR", 640), ("C1", 80), ("CZ", 80), ("CK", 8)):
    _buf(_n, _w, "float32")
for _n, _w in (("Vi", 20), ("Vp", 20), ("PI", 1), ("CI", 16), ("I1", 16), ("I2", 16), ("II", 30)):
    _buf(_n, _w, "int32")
for _n, _w in (("CU", 30), ("OFF", 20), ("PQ0", 80), ("PQ1", 80), ("PQ2", 80)):
    _buf(_n, _w, "uint16")

SEMAPHORES = ["cv", "cs", "ct", "cg", "sent", "lx", "lx1", "lg", "lu", "lw", "lv", "lp", "out", "out2"]
for _t in range(3):
    SEMAPHORES += ["ax%d" % _t, "as%d" % _t, "ap%d" % _t, "aq%d" % _t, "av%d" % _t, "am%d" % _t]


def rank_program(g, core, T, topo):
    r = T.rank_of(core)
    if r is None:
        return
    V, S, PE = g.vector, g.scalar, g.tensor
    queue = {"v": V, "s": S, "t": PE, "y": g.sync, "g": g}
    own = {"v": "cv", "s": "cs", "t": "ct", "g": "cg"}
    count, know, wrote, read, clock, seen = {}, {q: {} for q in queue}, {}, {}, {}, {}

    def order(q, R, W):
        need = {}
        deps = []
        for k in R:
            deps += wrote.get(k, [])
            if k.startswith("ps"):
                deps += [d for d in read.get(k, []) if d[0] != own.get(q)]
        for k in W:
            deps += wrote.get(k, []) + read.get(k, [])
        for s, n in deps:
            if n is None:
                n = count[s]
            if q == "t" and s == "ct":
                continue
            if know[q].get(s, 0) < n:
                need[s] = max(need.get(s, 0), n)
        for s in list(need):
            if any(o != s and clock.get((o, need[o]), {}).get(s, 0) >= need[s] for o in need):
                need.pop(s)
        for s, n in need.items():
            queue[q].wait_ge(T.sem[s], n)
            seen[s] = max(seen.get(s, 0), n)
            know[q][s] = n
            for o, m in clock.get((s, n), {}).items():
                know[q][o] = max(know[q].get(o, 0), m)

    def note(tok, R, W):
        for k in R:
            read.setdefault(k, []).append(tok)
        for k in W:
            wrote[k] = [tok]
            read[k] = []

    def op(q, R, W, call, *a, **kw):
        R, W = R.split(), W.split()
        order(q, R, W)
        s = own[q]
        call(*a, **kw).then_inc(T.sem[s], 1)
        count[s] = count.get(s, 0) + 1
        clock[(s, count[s])] = dict(know[q])
        note((s, count[s]), R, W)

    def dma(q, s, R, W, out, in_):
        R, W = R.split(), W.split()
        order(q, R, W)
        queue[q].dma_start(out, in_).then_inc(T.sem[s], 16)
        count[s] = count.get(s, 0) + 16
        note((s, None), R, W)

    def send(t, s, R, W, out, in_):
        dst = T.cores[r ^ STEP[t]]
        order("g", R.split(), [])
        rid, pid = topo.addr(dst)[:2]
        g.remote_dma(out, in_, T.sem[s], T.sem.sent, pid, rid, topo.mask(core, dst))
        k = len(topo.engines(core, dst))
        count["sent"] = count.get("sent", 0) + k
        count[s] = count.get(s, 0) + k
        note((s, None), [], W.split())

    def ts(R, W, out, in0, s1, o0, s2=None, o1=None):
        if o1 is None:
            op("v", R, W, V.tensor_scalar, out, in0, s1, None, o0)
        else:
            op("v", R, W, V.tensor_scalar, out, in0, s1, s2, o0, o1)

    def tt(R, W, out, a, b, o):
        op("v", R, W, V.tensor_tensor, out, a, b, o)

    def cp(R, W, out, a):
        op("v", R, W, V.tensor_copy, out, a)

    def scan(R, W, out, a, b, first, o0, o1):
        op("v", R, W, V.tensor_tensor_scan, out, a, b, first, o0, o1)

    def turn(R, W, out, a):
        op("v", R, W, V.transpose, out, a)

    def fill(W, ap, c):
        op("v", "", W, V.memset, ap, c)

    def act(R, W, out, a, f=F.Copy, **kw):
        op("s", R, W, S.activation, out, a, f, **kw)

    def aff(R, W, out, a, scale, bias):
        act(R, W, out, a, F.Identity, scale=scale, bias=bias)

    def quant(R, W, name, lo, hi, tile):
        op("v", R, W, V.quantize_mx, T[name][:, lo:hi], T["S" + name][:, lo:hi], tile)

    def mm(bank, w, at, x, lo, n, R, start=True, stop=True):
        op("t", R, "ps%d" % bank, PE.matmul_mx, T["ps%d" % bank][:, 0:n], T[w][:, at:at + 128], T["S" + w][:, at:at + 128],
           T[x][:, lo:lo + n], T["S" + x][:, lo:lo + n], start, stop)

    def iota(W, out, pat, cm, first=0, R=""):
        order("g", [], ["crossing"])
        op("g", R + " staying", W, g.iota, out, pat, first, cm, allow_small_or_imprecise_dtypes=True)

    def gfill(R, W, ap, n, c):
        iota(W, ap, [[0, n]], 0, int(c), R)

    def ps(k, n=C):
        return T["ps%d" % k][:, 0:n]

    def keys(form, *ranges):
        out = [()]
        for n in ranges:
            out = [o + (i,) for o in out for i in (range(n) if isinstance(n, int) else n)]
        return " ".join(form % o for o in out)

    def upper(t):
        return int(r > (r ^ STEP[t]))

    def words(ap):
        return ap.bitcast(dt.uint32)

    def pick(R, W, dst, at, src, lo, off):
        n = 16 * off.shape[1]
        cp(R.replace("#", "c"), W + "c", words(T[dst][:, at:at + n]), words(T[src][:, lo:lo + 640]).indirect(off))
        act(R.replace("#", "s"), W + "s", T["S" + dst][:, at:at + n], T["S" + src][:, lo:lo + 640].indirect(off))

    def move(q, R, W, out, a):
        if q == "s":
            act(R, W, out, a)
        else:
            order("g", [], ["staying"])
            op("g", R + " crossing", W, g.affine_select, out, a, [[0, a.shape[1]]], A.is_equal, 0.0, 0, 0)

    def spread1(R, key, buf, at, n, q):
        move(q, R, key + "a", buf[0:64, at + n:at + 2 * n], buf[64:128, at:at + n])
        move(q, R, key + "b", buf[64:128, at + n:at + 2 * n], buf[0:64, at:at + n])

    def spread2(key, buf, at, n, q):
        for a in range(4):
            move(q, "%sa %sb" % (key, key), "%s_%d" % (key, a), buf[32 * (a ^ 1):32 * (a ^ 1) + 32, at + 2 * n:at + 4 * n],
                 buf[32 * a:32 * a + 32, at:at + 2 * n])

    shr, band = A.logical_shift_right, A.bitwise_and
    DIGITS = (("h16", 0, 16), ("i", 0, 15), ("r32", 0, 96), ("e", 0, 1), ("k0", 1, 1), ("r0", 5, 1), ("k1", 2, 1), ("r1", 6, 1),
              ("i3", 3, 1))
    MORE = ("i8", "m", "q4", "h", "even", "x0", "sg", "x1", "sh", "x2", "x3", "dR", "dT", "dV", "dS", "a0", "a1", "a2", "a3", "end",
            "g0", "g1", "m8", "hm", "s0", "jump", "kb", "dR2", "dR3", "n0", "n1", "dU", "i7", "u0", "u1", "q1")
    col = {n: T.CF[:, k:k + 1] for k, n in enumerate([d[0] for d in DIGITS] + list(MORE))}
    CAB, CR, CT, CV, CS, CD = (0, 10), (10, 15), (16, 18), (18, 23), (24, 26), (28, 30)

    def cu(c):
        return T.CU[:, c[0]:c[1]]
    H = C // 2

    def send_codes(t, R, lo, hi):
        q, at = "QF%d" % t, C * upper(t)
        send(t, "ax%d" % t, R, q + "c", T[q][:, at + lo:at + hi].bitcast(dt.uint8), T[q][:, at + lo:at + hi].bitcast(dt.uint8))

    def send_scales(t):
        q, at = "QF%d" % t, C * upper(t)
        send(t, "as%d" % t, q, q + "s", T["S" + q][:, at:at + C], T["S" + q][:, at:at + C])

    def tile_e(par, b):
        at = 512 * par + 128 * b
        quant("Z%d" % par, "QE%d%d" % (par, b), "QE", at, at + 128, T.Z[:, 520 * par + 3 - b:520 * par + 515 - b])

    dma("s", "lg", "", "Vi", T.Vi[:], T.vg[:])
    dma("y", "lx", "", "xin0", T.xin[:, 0:4 * FIRST], T.x[:, 0:4 * FIRST])
    dma("y", "lx1", "", "xin", T.xin[:, 4 * FIRST:1280], T.x[:, 4 * FIRST:1280])
    dma("y", "lu", "", "uin", T.uin[:], T.u[:])
    iota("PI", T.PI[:], [[0, 1]], 1)
    iota("NI", T.NI[:], [[16, 8]], 0)
    iota("idm", T.idm[:], [[-1, 128]], 1)
    iota("YJ", T.YJ[:], [[C, 2], [0, 2], [16, 20]], 0, -SELF)
    gfill("", "PZ", T.PZ[:, 0:64], 64, -8)
    send(0, "ap0", "Vi", "Vp", T.Vp[:], T.Vi[:])

    def both_halves(src, dst, at):
        yield cp(src + " OT", "OTa", T.OT[:, 0:20], T[src][:])
        yield turn("OTa", "T1", T.T1[:], T.OT[:, 0:32])
        for h in range(2):
            act("T1", "Z3%d" % h, T.Z3[:, h:4:2, :], T.T1[:])
        yield
        yield turn("Z30 Z31", "ZT", T.ZT[:], T.Z3[:])
        for e in range(2):
            cp("ZT", dst + "ab"[e], T.PQ0[:, at + 20 * e:at + 20 * e + 20], T.ZT[:, 32 * e:32 * e + 20])
        yield
    mine, theirs = both_halves("Vi", "PO0", 40 * upper(0)), both_halves("Vp", "PP0", 40 - 40 * upper(0))

    fill("Z", T.Z[:], 0.0)
    fill("OT", T.OT[:, 20:32], 0.0)
    for W, ap, n, c in (("Mm", T.Mm[:, 0:216], 216, 1.0), ("ST", T.ST[:], 5 * SEG, 1.0), ("Tin", T.Tin[:, 0:40, 11:16], 200, -1.0)):
        aff("Z Z0 Z1", W, ap, T.Z[:, 0:n], 1.0, c)
    for k, (n, sh, m) in enumerate(DIGITS):
        ts("PI", "CI%d" % k, T.CI[:, k:k + 1], T.PI[:], sh, shr, m, band)
    cp(keys("CI%d", len(DIGITS)), "CF", T.CF[:, 0:len(DIGITS)], T.CI[:, 0:len(DIGITS)])
    next(mine)
    at0 = C * upper(0)
    quant("xin0", "QF0h", "QF0", at0, at0 + FIRST, T.xin[:, 0:4 * FIRST])
    send_codes(0, "QF0h", 0, FIRST)
    aff("NI CF", "NJ", T.NJ[:], T.NI[:], 1.0, col["i"])
    aff("CF", "h", col["h"], col["h16"], 0.0625, 0.0)
    aff("CF", "even", col["even"], col["h16"], -0.0625, 1.0)
    aff("NI CF", "t8", T.t8[:], T.NI[:], 0.125, col["i3"])
    aff("NJ", "If", T.CL[:, 16:21], T.NJ[:, 0:5], 1.0 / 9, -4.0 / 9)
    ts("CF", "x0", col["x0"], col["k0"], col["r0"], A.not_equal, 2.0, A.mult)
    next(mine)
    quant("xin QF0h", "QF0", "QF0", at0 + FIRST, at0 + C, T.xin[:, 4 * FIRST:1280])
    send_scales(0)
    send_codes(0, "QF0", FIRST, C)
    next(mine)
    Ii, Is, I7, Ia, Ib = [T.II[:, 6 * k:6 * k + 5] for k in range(5)]
    for par in range(2):
        ts("idm Z h even", "Z%d" % par, T.Z[:, 520 * par + 3:520 * par + 515:4], T.idm[:], 0.0, A.is_equal,
           col["h" if par else "even"], A.mult)
    next(mine)
    ts("CF x0", "sg", col["sg"], col["k1"], col["r1"], A.not_equal, col["x0"], A.add)
    tile_e(0, 0)
    next(mine)
    cp("If", "Ii", Ii, T.CL[:, 16:21])
    tile_e(0, 1)
    pn = T.PN[:, :, 5:120:6]
    ts("PO0a PO0b", "PN0 PN1", pn, T.PQ0[:, 40 * upper(0):40 * upper(0) + 40], -float(SELF), A.add)
    ts("Ii", "Im", T.CL[:, 24:29], Ii, -9.0, A.mult)
    tile_e(0, 2)
    tile_e(0, 3)
    next(theirs)
    tt("Im NJ", "Is", Is, T.CL[:, 24:29], T.NJ[:, 0:5], A.add)
    tile_e(1, 0)
    next(theirs)
    ts("YJ CF", "YJ", T.YJ[:], T.YJ[:], col["i"], A.add)
    tile_e(1, 1)
    tile_e(1, 2)

    def pairs(k):
        if k == 0:
            ts("Is", "I7", I7, Is, 7.0, A.add)
            ts("Is", "Ib", Ib, Is, 7, band)
        if k == 1:
            ts("I7", "Ia", Ia, I7, 7, band)
            tt("Ii Ib", "Ib", Ib, Ii, Ib, A.max)
        if k == 2:
            tt("Ii Ia", "Ia", Ia, Ii, Ia, A.min)
            ts("Ib", "CAb", T.CU[:, 5:10], Ib, 7.0, A.min, 16.0, A.mult)
        if k == 3:
            ts("Ia", "CAa", T.CU[:, 0:4], T.II[:, 18:22], 16.0, A.mult)
            ts("i7", "CAc", T.CU[:, 4:5], col["i7"], -16.0, A.mult, 120.0, A.add)
        if k == 4:
            quant("uin", "QU", "QU", 0, 128, T.uin[:])
        if k == 5:
            act("QU CAa CAb CAc", "QABs", T.SQAB[:], T.SQU[:].indirect(cu(CAB)))
        if k == 6:
            cp("QU CAa CAb CAc", "QABc", words(T.QAB[:]), words(T.QU[:]).indirect(cu(CAB)))
        if k == 7:
            ts("t8 dT", "CUt", cu(CT), T.t8[:, 0:2], 8.0, A.mult, col["dT"], A.add)
            ts("CF dU", "CUd0", T.CU[:, CD[0]:CD[0] + 1], col["r1"], -64.0, A.mult, col["dU"], A.add)
            ts("q1 dU", "CUd1", T.CU[:, CD[0] + 1:CD[1]], col["q1"], 64.0, A.mult, col["dU"], A.add)
    dma("y", "lp", "QF0c QF0", "QYpad", T.QY[:, 0:64].bitcast(dt.uint8), T.QF0[:, at0:at0 + 64].bitcast(dt.uint8))
    dma("y", "lp", "", "QYpad2", T.SQY[:, 0:64], T.SQF0[:, at0:at0 + 64])
    dma("y", "lw", "", "QW", T.QW[:].bitcast(dt.uint8), T.wc[:])
    dma("y", "lw", "", "QW2", T.SQW[:], T.ws[:])
    dma("y", "lv", "", "vin", T.vin[:], T.v[:])

    aff("CF h", "dT", col["dT"], col["r32"], 0.0625, col["h"])
    for e in range(2):
        aff("CF", "g%d" % e, col["g%d" % e], col["r32"], -0.0625, 7.0 - e + SELF / PLACE)
    act("CF", "s0", col["s0"], col["r32"], F.Sign, bias=-1.0)
    aff("h CF", "dR", col["dR"], col["e"], 20.0, col["h"])
    aff("CF", "dV", col["dV"], col["r32"], 0.0625, col["e"])
    aff("CF", "end", col["end"], col["r32"], -1.0, -63.0)
    aff("CF", "jump", col["jump"], col["r1"], 80.0, 33.0)
    aff("CF", "q4", col["q4"], col["i3"], 2.0, col["k1"])
    aff("CF", "m", col["m"], col["h16"], 1.0, col["i"])
    aff("CF", "i8", col["i8"], col["i3"], 8.0, 56.0)
    aff("dT CF", "dT", col["dT"], col["e"], 32.0, col["dT"])
    aff("g0 s0", "g0", col["g0"], col["g0"], col["s0"], 0.0)
    aff("dR q4", "dR", col["dR"], col["q4"], 2.0, col["dR"])
    aff("s0", "s0", col["s0"], col["s0"], 1.0 / PLACE, 0.0)
    aff("sg dT", "dT", col["dT"], col["sg"], 64.0, col["dT"])
    act("CF", "i7", col["i7"], col["i"], F.Abs, bias=-7.5)
    aff("CF", "q1", col["q1"], col["r1"], 1.0, -1.0)
    gfill("Mm", "Mmb", T.Mm[:, 8:216:9], 24, -PLACE)
    gfill("Mm", "Mma", T.Mm[:, 0:216:9], 24, 0)
    for k in range(3):
        gfill("Mm", "Mm%d" % k, T.Mm[:, 72 * k + 11:72 * k + 62:10], 6, -1)
    gfill("", "Mmb", T.Mm[:, 71:216:72], 3, PLACE)
    iota("xc", T.xc[:], [[32, 20]], 0)
    iota("C1", T.C1[:], [[32, 20], [0, 4]], 0, -SELF)
    gfill("", "DL", T.DL[:, 16:48, :], 128, 0)
    gfill("", "DL1", T.DL[:, 1:16:2, :], 32, PLACE)
    gfill("", "FL", T.FL[:, 17:48, :], 124, 1)
    gfill("", "FL0", T.FL[:, 0, :], 4, 0)
    gfill("", "FLa", T.FL[:, 1:16:2, :], 32, 1)
    gfill("", "CLpad", T.CL[:, 11:16:2], 3, 0)

    def fills(k):
        if k == 0:
            iota("CK", T.CK[:], [[C, 2], [128, 4]], 1, -64)
            gfill("", "SW0", T.SW[:, 3, 47:48], 1, 0)
            for j, c in ((47, 97), (80, -4096)):
                gfill("ST", "ST%d" % j, T.ST[:, j:5 * SEG:SEG], 5, c)
            gfill("", "D0r", T.D0[:, SEG - 1:20 * SEG:SEG], 20, BIG)
        if k == 1:
            gfill("", "KKpad", T.KK[:, 20:32], 12, 0)
            iota("OF", T.OF[:], [[0, 10], [1, 3]], 0)
            gfill("", "Tin2", T.Tin[:, 40:52, 3:8:4], 24, -1)
            gfill("", "Tin3", T.Tin[:, 0:40, 2:8:4], 80, -1)
        if k == 2:
            gfill("", "Q30", T.Q3[:, 0:240:6], 40, 0)
            gfill("", "Q31", T.Q3[:, 1:240:3], 80, 1)
        if k == 3:
            gfill("", "PNpad", T.PN[:, :, 120:192], 144, 0)

    def lists_of_the_table():
        def line(W, a, scale, bias, f=F.Identity):
            R = " ".join(n for n in (a, scale, bias) if isinstance(n, str))
            act("CF " + R, W, col[W], col[a], f, scale=col.get(scale, scale), bias=col.get(bias, bias))

        def entries(W, out, lo, hi, step, first):
            aff("NI " + first, W, out, T.NI[:, lo:hi], step, col[first])
        yield line("dR2", "i3", 20.0, "dR")
        yield line("dR3", "dR", 1.0, 20.0)
        yield line("n0", "r0", -1.0, 0.0)
        yield line("n1", "r1", -1.0, 0.0)
        yield line("dU", "r32", 0.0625, "h")
        yield line("u1", "k0", 16.0, 224.0)
        yield line("u0", "i3", 1.0, "n0", F.Square)
        yield line("dU", "e", 8.0, "dU")
        yield line("u1", "k1", -32.0, "u1")
        for lo, hi, a in ((0, 2, "dR"), (2, 3, "dR2"), (3, 5, "dR3")):
            yield entries("CLr%d" % lo, T.CL[:, lo:hi], lo, hi, 0.5, a)
        yield line("dU", "u0", -128.0, "dU")
        for W, a, n in (("x1", "e", "n0"), ("x2", "k1", "n0"), ("x3", "i3", "n1"), ("sh", "k0", "n1")):
            yield line(W, a, 1.0, n, F.Square)
        yield line("dU", "u1", 1.0, "dU")
        yield line("kb", "q4", -1.0, 3.0)
        yield line("m8", "i", 1.0, -8.0, F.Abs)
        yield line("x2", "x2", 112.0, "dV")
        yield line("a3", "x3", -112.0, "i8")
        yield line("x1", "x1", 112.0, 83.0)
        yield line("kb", "k0", -1.0, "kb", F.Relu)
        yield line("m8", "m8", -1.0, 1.0, F.Relu)
        yield line("a0", "x3", 56.0, "x2")
        yield line("a2", "a3", -1.0, 12.0)
        yield line("sh", "sh", -56.0, "x1")
        yield line("hm", "h16", "m8", 0.0)
        yield line("a1", "a3", 1.0, "a0")
        yield line("a0", "a0", 1.0, 12.0)
        yield line("dS", "kb", -1.0, "sh")
        yield line("a2", "a2", "i3", "a1")
        yield entries("CLv0", T.CL[:, 6:8], 0, 2, 0.5, "a1")
        yield entries("CLv3", T.CL[:, 9:11], 3, 5, 0.5, "a0")
        yield entries("CLs", T.CL[:, 12:15:2], 0, 2, 1.75, "dS")
        yield entries("CLv2", T.CL[:, 8:9], 2, 3, 0.5, "a2")

    def tables():
        yield aff("xc m", "xc", T.xc[:], T.xc[:], 1.0, col["m"])
        yield aff("C1 m", "C1", T.C1[:], T.C1[:], 1.0, col["m"])
        yield act("xc", "xcb", T.xcb[:], T.xc[:], scale=-BIG)
        yield aff("C1", "CZ", T.CZ[:], T.C1[:], 1024.0, SHIFT + 1024.0 * SELF)
        yield aff("CK", "CK", T.CK[:], T.CK[:], 1024.0, 0.0)
        for k, c in ((15, "jump"), (79, "end")):
            yield aff("ST " + c, "ST%d" % k, T.ST[:, k:5 * SEG:SEG], T.ST[:, k:5 * SEG:SEG], col[c], 0.0)
    late, later = lists_of_the_table(), tables()

    def some_lists(k):
        for _ in range(k):
            next(late, None)

    def some_tables(k):
        for _ in range(SGAPS[k]):
            next(later, None)

    def as_offsets(k):
        if k == 0:
            cp("CLr0 CLr2 CLr3", "CUr", cu(CR), T.CL[:, 0:5])
        else:
            cp("CLv0 CLv2 CLv3 CLs CLpad", "CUv", T.CU[:, CV[0]:CV[0] + 10], T.CL[:, 6:16])
    some_lists(AHEAD)
    next(theirs)
    pairs(0)
    tile_e(1, 3)
    next(theirs)
    pairs(1)
    pairs(4)
    next(theirs)

    for t in range(3):
        u = upper(t)
        B0, Bp, b0 = C * u, C - C * u, 10 * u
        QF, G, B, PQ, VV, MP = ["%s%d" % (n, t) for n in ("QF", "G", "B", "PQ", "VV", "MP")]
        PO, PP = "PO%d" % t, "PP%d" % t
        win = "%s %s# " % (QF, QF)
        kv = keys(VV + "_%d", 4) + " CUv"

        def lists(who, e, lo=0, hi=20):
            return T[PQ][:, 40 * who + 20 * e + lo:40 * who + 20 * e + hi]

        def unpack(h, e, x, at, R, start, stop):
            for b in range(4):
                mm(4 * h + b, "QE", 512 * e + 128 * b, x, at + CUT[h], CUT[h + 1] - CUT[h], "QE%d%d %s" % (e, b, R), start, stop)

        def own_pick(e):
            pick(win + PO + "ab"[e], "Go%d" % e, G, 640 * e + B0, QF, 0, lists(u, e))
            for h in range(2):
                unpack(h, e, G, 640 * e + B0, "Go%dc Go%ds" % (e, e), e == 0, False)

        def partner_pick(e):
            pick(win + PP + "ab"[e], "Gp%d" % e, G, 640 * e + Bp, QF, 0, lists(1 - u, e))

        def second_pick(k):
            h, e = divmod(k, 2)
            pick("Go%d# Gp%d# %s" % (e, e, PO + "ab"[e]), "B%d%d" % (e, h), B, C * e + CUT[h], G, 640 * e,
                 lists(u, e, CUT[h] // 16, CUT[h + 1] // 16))
            unpack(h, e, B, C * e, "B%d%dc B%d%ds" % (e, h, e, h), False, e == 1)

        def y_part(k):
            h, b = divmod(k, 4)
            return T.Yt[:, 4 * CUT[h] + b:4 * CUT[h + 1]:4], ps(k, CUT[h + 1] - CUT[h])

        def y_vector(k):
            ts("ps%d" % k, "Y%d" % k, *y_part(k), 0.5, A.mult)

        def y_scalar(k):
            act("ps%d" % k, "Y%d" % k, *y_part(k), scale=0.5)

        def y_quant(k):
            quant(keys("Y%d", range(4 * k, 4 * k + 4)), "QY%d" % k, "QY", 64 + CUT[k], 64 + CUT[k + 1], T.Yt[:, 4 * CUT[k]:4 * CUT[k + 1]])

        def pointers(k):
            if k == 0:
                tt("PN0 PN1 YJ", "ne", T.ne[:], pn, T.YJ[:, 40 * u:40 * u + 40], A.not_equal)
            if k == 1:
                tt("ne PN0 PN1", "PS", T.PS[:], T.ne[:], pn, A.mult)
            if k == 2:
                for e in range(2):
                    ts("PS PZ s0 g%d" % e, "PZ%d" % e, T.PZ[:, 32 * e + 4:32 * e + 24], T.PS[:, 20 * e:20 * e + 20],
                       1.0 / PLACE if e else col["s0"], A.mult, col["g%d" % e], A.add)
            if k == 3:
                spread1("PZ0 PZ1", "PZ", T.PZ, 0, 64, "g")
            if k == 4:
                spread2("PZ", T.PZ, 0, 64, "g")
            if k == 5:
                act(keys("PZ_%d", 4) + " CUt Mm", "PT", T.Mm[:, 1:288:9], T.PZ[:].indirect(cu(CT)))
            if k == 6:
                ts("%sa %sb %sa %sb" % (PO, PO, PP, PP), "PA", T.PA[:], T[PQ][:], -float(SELF), A.add)
            if k == 7:
                act("PA CUr", "VR", T.VR[:], T.PA[:].indirect(cu(CR)))

        def products(k):
            if k < 3:
                mm(k, "QY", 128 * k, "QAB", 0, 160, "QY%d QYpad QYpad2 QABc QABs" % (k // 2))
            if k == 5:
                mm(3, "QY", 256, "QAB", 32, 128, "QY1 QABc QABs")
            for b in {3: (0, 1), 7: (2, 3)}.get(k, ()):
                mm(4 + b, "QW", 128 * b, "QY", 64, C, "QW QW2 QY0 QY1")
            for b in {6: (0,), 4: (1, 2, 3)}.get(k, ()):
                for e in range(2):
                    mm((3 + b) % 4, "QE", 512 * e + 128 * b, QF, B0, C, "QE%d%d %s" % (e, b, QF), e == 0, e == 1)

        def other_side(k):
            act("ps%d" % k, "SL%d" % k, T.SL[:, 72 * k:72 * k + 72], T["ps%d" % k][:, 80:152])

        def compare(k):
            tt("ps%d SL%d" % (k, k), "D%d" % k, T.D[:, 72 * k:72 * k + 72], ps(k, 72), T.SL[:, 72 * k:72 * k + 72], A.is_ge)

        def places(k):
            scan("D%d PT Mma Mmb Mm%d" % (k, k), "SC%d" % k, T.SC[:, k, 0:72], T.Mm[:, 72 * k:72 * k + 72],
                 T.D[:, 72 * k:72 * k + 72], 0.0, A.mult, A.add)

        def least(k):
            bank, at = ((0, 72), (1, 72), (3, 40))[k]
            scan("ps%d DL" % bank, "RM%d" % k, T.RM[:, k, :], T["ps%d" % bank][:, at:at + 8], T.DL[:, 16:24, 0], 1e29, A.min, A.add)

        def reached(k):
            ts("RM%d" % k, "FL%d" % (k + 1), T.FL[:, 2:18:2, k], T.RM[:, k, :], T.RM[:, k, 7:8], A.is_le)

        def asked(k):
            scan("FL FL0 FLa FL%d DL DL1 DLa DLb DLc" % (k + 1), "SW%d" % k, T.SW[:, k, :], T.FL[:, :, k], T.DL[:, :, k],
                 0.0, A.mult, A.add)

        def steps_down(k):
            if k == 0:
                act(keys("PZ_%d", 4) + " CUd0 CUd1", "PD", T.PD[:], T.PZ[:].indirect(cu(CD)), scale=PLACE)
            if k == 2:
                tt("PD", "DLa", T.DL[:, 0:12:2, :], T.PD[:, 0:24], T.PD[:, 4:28], A.subtract)
                tt("PD", "DLb", T.DL[:, 12, :], T.PD[:, 24:28], T.PD[:, 28:32], A.add)
                ts("PD", "DLc", T.DL[:, 14, :], T.PD[:, 28:32], -1.0, A.mult, -8 * PLACE, A.add)

        def along(k):
            if k == 0:
                turn("SW0", "AR0 AR1", T.AR[64:128, 16:48], T.SW[64:128, 0, 16:48])
            elif k == 3:
                turn("SW0", "AR3", T.AR[0:64, 0:32], T.SW[64:128, 0, 16:48])
            else:
                turn("SW%d" % k, "AR%d" % k, T.AR[:, 32 * k:32 * k + 32], T.SW[:, k, 16:48])

        def relu(b):
            act("ps%d" % (4 + b), "TB%d" % b, T.TB[:, C * b:C * b + C], ps(4 + b), F.Relu, scale=0.03125)

        def v_out(k):
            act("SC0 SC1 SC2", VV + "v", T[VV][:, 28 * u:28 * u + 24], T.SC[:, :, 8:72:9])

        def key_out(k):
            tt("SW0 SW1 SW2 CK", VV + "k", T[VV][:, 28 * u + 24:28 * u + 28], T.SW[:, :, 47], T.CK[:, 4 * u:4 * u + 4], A.add)

        def state(n):
            for b in range(4):
                lo, hi = max(PIECES[n] - C * b, 0), min(PIECES[n + 1] - C * b, C)
                if lo < hi:
                    k = (3 + b) % 4
                    tt("TB%d ps%d" % (b, k), "X%d%d" % (n, b), T.Xt[:, 4 * lo + b:4 * hi:4], T.TB[:, C * b + lo:C * b + hi],
                       T["ps%d" % k][:, lo:hi], A.add)

        def match(k):
            for j in range(ON_V, 20) if k else range(ON_V):
                out = T.D0[:, SEG * j:SEG * j + 80]
                if k:
                    act(keys("AR%d", 4) + " xcb", "D0_%d" % j, out, T.AR[:, 16:96], F.Abs, scale=BIG, bias=T.xcb[:, j:j + 1])
                else:
                    ts(keys("AR%d", 4) + " xc", "D0_%d" % j, out, T.AR[:, 16:96], T.xc[:, j:j + 1], A.not_equal, BIG, A.mult)

        def first(k):
            lo, hi = SCANS[k]
            scan(keys("D0_%d", range(lo, hi)) + " D0r ST15 ST47 ST79 ST80", "SO%d" % lo, T.SO[:, SEG * lo:SEG * hi],
                 T.D0[:, SEG * lo:SEG * hi], T.ST[:, 0:SEG * (hi - lo)], 4096.0, A.min, A.subtract)

        def lowest(k):
            if k == 0:
                tt(keys("SO%d", [lo for lo, hi in SCANS]), "M1", T.M1[0:64, :], T.SO[0:64, 79:20 * SEG:SEG],
                   T.SO[64:128, 79:20 * SEG:SEG], A.min)
            for a in range(4 * (k == 1)):
                tt("M1", "MO%d" % a, T.MO[32 * a:32 * a + 32, 20 * t:20 * t + 20], T.M1[0:32, :], T.M1[32:64, :], A.min)
            if k == 2:
                ts(keys("MO%d", 4), "KK", T.KK[:, 0:20], T.MO[:, 20 * t:20 * t + 20], 160.0 + B0, A.add, 1025.0, A.mult)

        def leave(k):
            if k == 0:
                send(t, "av%d" % t, keys(VV + "%s", "vk"), VV + "p", T[VV][:, 28 * u:28 * u + 28], T[VV][:, 28 * u:28 * u + 28])
            if k == 1:
                send(t, "am%d" % t, keys("MO%d", 4), MP, T[MP][:], T.MO[:, 20 * t:20 * t + 20])
            if k == 2 and t < 2:
                q, at = "QF%d" % (t + 1), C * upper(t + 1)
                quant(keys("X%d%d", 5, 4), q, q, at, at + C, T.Xt[:])
                send_codes(t + 1, q, 0, C)
                send_scales(t + 1)
            if k == 2 and t == 2:
                quant(keys("X%d%d", 5, 4), "QX3", "QX3", 0, C, T.Xt[:])
                mm(4, "QV", 0, "QX3", 0, C, "QV QX3")
                dma("y", "out", "QX3", "", T.oc[:], T.QX3[:].bitcast(dt.uint8))
                for a in range(4):
                    dma("y", "out", "QX3", "", T.osc[4 * a:4 * a + 4, :], T.SQX3[32 * a:32 * a + 4, :])
            if k == 3 and t == 2:
                act("ps4", "ys", T.ys[:], ps(4))
                dma("y", "out", "ys", "", T.y[:], T.ys[:])
            if k == 4 and t == 1:
                quant("vin", "QV", "QV", 0, 128, T.vin[:])

        def table_scalar(k):
            if k == 0:
                spread1("%s %sp" % (keys(VV + "%s", "vk"), VV), VV, T[VV], 0, 56, "s")
            if k == 1:
                act("VR", "Tr", T.Tin[:, 0:40, 1:8:4], T.VR[:])
            if k == 2:
                spread2(VV, T[VV], 0, 56, "s")
            if k == 4:
                act(kv, "va", T.va[:], T[VV][:].indirect(cu(CV)), F.Abs, scale=STILL, bias=-MID * STILL)
            for h in range(2 * (k == 8)):
                act("MQ0 MQ1", "Tq%d" % h, T.Tin[:, h:40:2, 8], T.MQ[:, :, 0:10])
                aff("MQ0 MQ1", "Tt%d" % h, T.Tin[:, h:40:2, 10], T.MQ[:, :, 0:10], 1.0 / 1025, -160.0 - Bp)
            for e in range(2 * (k == 9)):
                p = T.PN[:, e, 5:120:6]
                act("PN%d" % e, "S34%d" % e, T.S3[:, 120 * e + 4:120 * e + 120:6], p, scale=-1.0)
                aff("PN%d" % e, "S35%d" % e, T.S3[:, 120 * e + 5:120 * e + 120:6], p, 1.0, float(SELF) if t == 2 else 0.0)
            new = u not in [upper(n) for n in range(t)]
            if k == 6 and new:
                aff("YR%d m8 hm" % u, "YR%d" % u, T.YR[:, B0:B0 + C], T.YR[:, B0:B0 + C], col["m8"], col["hm"])
            if k == 7 and new:
                iota("YR%d" % u, T.YR[:, B0:B0 + C], [[32, 10], [0, 2], [1, 16]], 0, B0 - SHIFT)

        def table_vector(k):
            if k == 0:
                tt("C1 VR", "dd", T.dd[:], T.C1[:], T.VR[:], A.subtract)
            if k == 1:
                tt("vh dd", "Th", T.Tin[:, 0:40, 0:8:4], T.vh[:], T.dd[:], A.mult)
            if k == 2:
                tt("va CZ", "Tz", T.Tin[:, 0:40, 3:8:4], T.va[:], T.CZ[:], A.min)
            if k == 3:
                ts(kv, "vh", T.vh[:], T[VV][:].indirect(cu(CV)), LAST, A.is_ge)
            for w in {4: (0, 1), 8: (u,)}.get(k, ()):
                W, out = ("MQ%d" % w, T.MQ[:, w, :]) if k == 4 else ("I1", T.I1[:])
                tt("KK KKpad " + kv, W, out, T[VV][:].indirect(T.CU[:, CS[0] + 2 * w:CS[0] + 2 * w + 1]), T.KK[:, 10 * w:10 * w + 16], A.min)
            if k == 6:
                ts("I1", "I2", T.I2[:], T.I1[:], 1023, band)
            if k == 7:
                gfill("", "OD1", T.OD[:, 1:30:3], 10, -160 - Bp)

        def own_marks(k):
            if k == 0:
                turn("Tz Tin2", "T1", T.T1[:], T.Tin[:, 2 * b0:2 * b0 + 32:2, 3:8:4])
            if k == 2:
                turn("Z30 Z31", "ZT", T.ZT[:], T.Z3[:])
            for h in range(2):
                if k == 1:
                    act("T1", "Z3%d" % h, T.Z3[:, h:4:2, :], T.T1[:])
                if k == 3:
                    act("ZT", "ZO%d" % h, T.ZO[:, h:20:2, :], T.ZT[:, 32 * h:32 * h + 20])

        def couples(k):
            w = T[MP][:, b0:b0 + 10]
            if k == 0:
                tt("I2 " + MP, "OD0", T.OD[:, 0:30:3], T.I2[:, 0:10], w, A.subtract)
                ts(MP, "OD2", T.OD[:, 2:30:3], w, 160.0 + Bp, A.add)
                tt("Tt0 OF " + MP, "OF2", T.OF[:, 2:30:3], w, T.Tin[:, 2 * b0:2 * b0 + 20:2, 10], A.is_gt)
            if k == 2:
                scan("OD0 OD1 OD2 OF2", "OM", T.OM[:], T.OF[:], T.OD[:], 0.0, A.mult, A.add)
            if k == 3:
                turn("Tk0 Tk1 Tq0 Tq1 Tt0 Tt1 Tr Tz Th Tin Tin3", "Tout", T.Tout[:], T.Tin[:, 0:40, :])
            for h in range(2):
                if k == 1:
                    act(MP, "Tk%d" % h, T.Tin[:, h:40:2, 9], T[MP][:])
                if k == 4:
                    ts("OM", "OFF%d" % h, T.OFF[:, h:20:2], T.OM[:, 2:30:3], 639.0, A.min)
                if k == 5:
                    tt("Tout OFF0 OFF1 YR%d" % u, "GG%d" % h, T.GG[:, H * h:H * h + H], T.Tout[:].indirect(T.OFF[:, 10 * h:10 * h + 10]),
                       T.YR[:, B0 + H * h:B0 + H * h + H], A.subtract)
                if k == 6:
                    turn("GG%d" % h, "ZZ%d" % h, T.ZZ[:, 10 * h:10 * h + 10, :], T.GG[:, H * h:H * h + H])

        def terms(e):
            lo, hi = 120 * e, 120 * e + 120
            p, theirs = T.PN[:, e, 5:120:6], T.ZZ[:, :, 4 * e + 1]
            act("ZZ0 ZZ1", "S31%d" % e, T.S3[:, lo + 1:hi:6], T.ZZ[:, :, 4 * e], scale=-1.0)
            act("ZZ0 ZZ1", "S32%d" % e, T.S3[:, lo + 2:hi:6], T.ZZ[:, :, 4 * e])
            act("ZZ0 ZZ1", "S33%d" % e, T.S3[:, lo + 3:hi:6], theirs)
            tt("ZZ0 ZZ1 PN%d" % e, "S30%d" % e, T.S3[:, lo:hi:6], p, theirs, A.subtract)
            tt("ZZ0 ZZ1", "Q32%d" % e, T.Q3[:, lo + 2:hi:6], T.ZZ[:, :, 8], T.ZZ[:, :, 4 * e + 3], A.not_equal)
            tt("ZZ0 ZZ1 ZO0 ZO1", "Q33%d" % e, T.Q3[:, lo + 3:hi:6], T.ZZ[:, :, 8], T.ZO[:, :, e], A.not_equal)
            tt("ZZ0 ZZ1", "Q35%d" % e, T.Q3[:, lo + 5:hi:6], T.ZZ[:, :, 9], T.ZZ[:, :, 10], A.is_gt)

        def swap(e):
            lo, hi = 120 * e, 120 * e + 120
            scan(keys("S3%d%d", 6, (e,)) + " Q30 Q31 " + keys("Q3%d%d", (2, 3, 5), (e,)), "PN%d" % e, T.PN[:, e, 0:120], T.Q3[:, lo:hi],
                 T.S3[:, lo:hi], 0.0, A.mult, A.add)

        def handed(e):
            if t < 2 and WHOLE:
                if e:
                    n = t + 1
                    new, o = T["PQ%d" % n][:, 40 * upper(n):40 * upper(n) + 40], "PO%da PO%db" % (n, n)
                    ts("PN0 PN1", o, new, pn, float(SELF), A.add)
                    send(n, "ap%d" % n, o, o.replace("O", "P"), new, new)
                return
            if t < 2:
                n = t + 1
                at = 40 * upper(n) + 20 * e
                new, o = T["PQ%d" % n][:, at:at + 20], "PO%d%s" % (n, "ab"[e])
                ts("PN%d" % e, o, new, T.PN[:, e, 5:120:6], float(SELF), A.add)
                send(n, "a%s%d" % ("pq"[e], n), o, o.replace("O", "P"), new, new)
                return
            turn("PN%d PNpad" % e, "OT%d" % e, T.OT[:, 32 * e:32 * e + 32], T.PN[:, e, 5:192:6])
            for a in range(4):
                dma("ys"[a % 2], "out2", "OT%d" % e, "", T.ov[2 * a + e, :], T.OT[32 * a:32 * a + 20, 32 * e:32 * e + 16])

        steps = {"G": own_pick, "P": partner_pick, "B": second_pick, "v": y_vector, "s": y_scalar, "q": y_quant, "z": pointers,
                 "m": products, "o": other_side, "c": compare, "p": places, "M": least, "R": reached, "l": asked, "D": steps_down, "a": along, "r": relu, "w": v_out,
                 "k": key_out, "x": state, "d": match, "f": first, "n": lowest, "L": leave, "S": table_scalar, "V": table_vector,
                 "O": own_marks, "K": couples, "t": terms, "u": swap, "h": handed,
                 "A": pairs, "F": fills, "e": some_lists, "g": as_offsets, "j": some_tables}
        for step in ROUND[t].split():
            if t and step[0] in "AFegj":
                continue
            steps[step[0]](int(step[1]))

    for s, n in count.items():
        if seen.get(s, 0) < n:
            g.wait_ge(T.sem[s], n)
